import numpy as np
import ml_dtypes


def mxq(x, axis, fmt="e4m3"):
    dtype, down = {"e4m3": (ml_dtypes.float8_e4m3fn, 7), "e5m2": (ml_dtypes.float8_e5m2, 14)}[fmt]
    v = np.moveaxis(np.asarray(x, np.float32).astype(ml_dtypes.bfloat16).astype(np.float64), axis, -1)
    blocks = v.reshape(v.shape[:-1] + (-1, 32))
    amax = np.abs(blocks).max(-1, keepdims=True)
    byte = np.maximum(np.where(amax > 0, np.frexp(amax)[1] - 1 + 127, 0) - down, 1)
    scale = np.exp2(byte - 127.0)
    codes = (blocks / scale).astype(np.float32).astype(dtype).astype(np.float64)
    return np.moveaxis((codes * scale).reshape(v.shape), -1, axis)


WIDE = False


def mx_kscale(k):
    if not WIDE:
        return np.ones(k)
    levels = np.array([10, -10, 5, -5, 0])
    if k % 512:
        return np.exp2(np.random.permutation(np.resize(levels, k // 32))).repeat(32)
    a = np.empty((k // 512, 16))
    for p in range(k // 512):
        a[p, :8] = np.random.permutation(np.resize(levels, 8))
        for g in range(8):
            far = levels[np.abs(levels - a[p, g]) >= 10]
            a[p, g + 8] = far[np.random.randint(len(far))]
    return np.exp2(a.ravel()).repeat(32)


def f64(x):
    return np.asarray(x).astype(np.float64)


def striped(idx):
    return np.tile(idx.reshape(-1, 16).T, (8, 1)).astype(np.uint16)


def unstriped(offs):
    return offs[:16].T.reshape(-1).astype(np.int64)


E2M1 = np.array([0.0, 0.5, 1.0, 1.5, 2.0, 3.0, 4.0, 6.0, -0.0, -0.5, -1.0, -1.5, -2.0, -3.0, -4.0, -6.0])


def pack_weight(w, fmt):
    k, n = w.shape
    w = f64(np.asarray(w, np.float32).astype(ml_dtypes.bfloat16)).reshape(k // 32, 32, n)
    amax = np.abs(w).max(1)
    if fmt == "e4m3":
        byte = np.frexp(amax)[1] - 1 + 127 - 7
    else:
        mant, ex = np.frexp(amax / 6.0)
        byte = np.where(mant > 0.5, ex, ex - 1) + 127
    byte = np.clip(np.where(amax > 0, byte, 1), 1, 254)
    scaled = (w * np.exp2(127.0 - byte)[:, None, :]).reshape(k, n).astype(np.float32)
    by_word = np.ascontiguousarray(scaled.reshape(k // 512, 128, 4, n).transpose(0, 1, 3, 2))
    if fmt == "e4m3":
        words = by_word.astype(ml_dtypes.float8_e4m3fn).view(np.uint8)
    else:
        c = by_word.astype(ml_dtypes.float4_e2m1fn).view(np.uint8) & 0xF
        words = (c[..., 0::2] | (c[..., 1::2] << 4)).reshape(k // 512, 128, 2 * n)
    return np.ascontiguousarray(words), np.ascontiguousarray(byte.astype(np.uint8).reshape(k // 512, 16, n))


def unpack_weight(words, scales, fmt):
    g, _, n = scales.shape
    words = np.ascontiguousarray(words).reshape(g, 128, n, -1)
    if fmt == "e4m3":
        vals = words.view(ml_dtypes.float8_e4m3fn).astype(np.float64)
    else:
        nib = np.empty((g, 128, n, 4), np.uint8)
        nib[..., 0::2] = words & 0xF
        nib[..., 1::2] = words >> 4
        vals = E2M1[nib]
    vals = vals * np.repeat(np.exp2(scales.astype(np.float64) - 127.0), 8, axis=1)[..., None]
    return vals.transpose(0, 1, 3, 2).reshape(g * 512, n)


def silu(v):
    return v / (1.0 + np.exp(-np.maximum(v, -700.0)))


def d_silu(v):
    s = 1.0 / (1.0 + np.exp(-np.maximum(v, -700.0)))
    return s * (1.0 + v * (1.0 - s))


K, T, E, C, H, N = 256, 1280, 4, 256, 512, 512


def by_expert(wq, xq):
    return np.concatenate([wq[e].T @ xq[:, e * C:(e + 1) * C] for e in range(E)], axis=1)


def setup_inputs():
    n = np.random.standard_normal
    s = mx_kscale(N)[:, None]
    u = mx_kscale(H)
    w2 = [pack_weight(m, "e2m1") for m in n((E, N, H)) / np.sqrt(N) / s[None] * u[None, None, :]]
    w1 = [pack_weight(m, "e2m1") for m in n((E, H, K)) / np.sqrt(H) / u[None, :, None]]
    w3 = [pack_weight(m, "e2m1") for m in n((E, H, K)) / np.sqrt(H) / u[None, :, None]]
    return {
        "dyT": (n((N, T)) * s).astype(np.float32),
        "a1": n((H, E * C)).astype(np.float32),
        "a3": n((H, E * C)).astype(np.float32),
        "w2_words": np.stack([m[0] for m in w2]),
        "w2_scales": np.stack([m[1] for m in w2]),
        "w1_words": np.stack([m[0] for m in w1]),
        "w1_scales": np.stack([m[1] for m in w1]),
        "w3_words": np.stack([m[0] for m in w3]),
        "w3_scales": np.stack([m[1] for m in w3]),
        "gate": np.tile(np.random.uniform(0.2, 1.0, E * C), (N, 1)).astype(np.float32),
        "offs": striped(np.random.permutation(T)[:E * C]),
    }


def reference(dyT, a1, a3, w2_words, w2_scales, w1_words, w1_scales, w3_words, w3_scales, gate, offs):
    idx = unstriped(offs)
    w2 = np.stack([unpack_weight(w2_words[e], w2_scales[e], "e2m1") for e in range(E)])
    w1 = np.stack([unpack_weight(w1_words[e], w1_scales[e], "e2m1") for e in range(E)])
    w3 = np.stack([unpack_weight(w3_words[e], w3_scales[e], "e2m1") for e in range(E)])
    gq = mxq(f64(gate) * f64(dyT)[:, idx], 0, "e4m3")
    dh = by_expert(w2, gq)
    da1 = dh * f64(a3) * d_silu(f64(a1))
    da3 = dh * silu(f64(a1))
    dx = by_expert(w1, mxq(da1, 0, "e4m3")) + by_expert(w3, mxq(da3, 0, "e4m3"))
    out = np.zeros((K, T))
    out[:, idx] = dx
    return out

@@ -1,0 +1,297 @@
+from contextlib import ExitStack
+
+import concourse.mybir as mybir
+
+F32 = mybir.dt.float32
+BF16 = mybir.dt.bfloat16
+U32 = mybir.dt.uint32
+I32 = mybir.dt.int32
+U16 = mybir.dt.uint16
+U8 = mybir.dt.uint8
+FP8X4 = mybir.dt.float8_e4m3fn_x4
+FP4X4 = mybir.dt.float4_e2m1fn_x4
+ACT = mybir.ActivationFunctionType
+ALU = mybir.AluOpType
+
+P = 128
+PACK = 4
+N = 512
+H = 512
+K = 256
+T = 1280
+E = 4
+C = 256
+S = E * C
+HALF = 512
+CHUNK = 128
+ON_VECTOR = (0,)
+DA3_ON_GPSIMD = (3,)
+
+FLOPS = 2 * S * (N * H + 2 * H * K)
+BYTES = 4 * (N * T + 2 * H * S + K * T + S) + E * P * (2 * H + 4 * K) + E * 16 * (H + 2 * K) + 2 * 16 * S // 16
+
+
+def tile_moe_bdx_glu_silu_kernel(
+    tc, dyT, a1, a3, w2_words, w2_scales, w1_words, w1_scales, w3_words, w3_scales, gate, offs, out
+):
+    nc = tc.nc
+    with ExitStack() as ctx:
+        listp = ctx.enter_context(tc.tile_pool(name="listp", bufs=1))
+        keep = ctx.enter_context(tc.tile_pool(name="keep", bufs=1))
+        ring = ctx.enter_context(tc.tile_pool(name="ring", bufs=3))
+        psum = ctx.enter_context(tc.psum_pool(name="psum", bufs=1))
+
+        offsets = listp.tile([P, S // 16], U16, name="offsets")
+
+        planes = [keep.tile([P, T], F32, name=f"plane{t}") for t in range(PACK)]
+        gate_sb = keep.tile([P, S], F32, name="gate_sb")
+        a1_sb = keep.tile([P, PACK, S], F32, name="a1_sb")
+        a3_sb = keep.tile([P, PACK, S], F32, name="a3_sb")
+        h_sb = keep.tile([P, PACK, S], F32, name="h_sb")
+        s_sb = keep.tile([P, PACK, S], F32, name="s_sb")
+        p_sb = keep.tile([P, PACK, S], F32, name="p_sb")
+        w2_raw = keep.tile([P, E, 2 * H], U8, name="w2_raw", align_bytes=64)
+        w2_perm = keep.tile([P, E, 2 * H], U8, name="w2_perm", align_bytes=64)
+        w2s_raw = keep.tile([P, E, H], U8, name="w2s_raw", align_bytes=64)
+        w2s_perm = keep.tile([P, E, H], U8, name="w2s_perm", align_bytes=64)
+        w1_sb = keep.tile([P, E, 2 * K], U8, name="w1_sb", align_bytes=64)
+        w3_sb = keep.tile([P, E, 2 * K], U8, name="w3_sb", align_bytes=64)
+        w1s = keep.tile([P, E, K], U8, name="w1s", align_bytes=64)
+        w3s = keep.tile([P, E, K], U8, name="w3s", align_bytes=64)
+        win = [keep.tile([P, T], F32, name=f"win{b}") for b in range(K // P)]
+        warm = keep.tile([P, 1], F32, name="warm")
+
+        nc.vector.memset(w2s_raw[:].bitcast(I32), 0)
+        nc.vector.memset(warm[:], 0.0)
+        nc.scalar.activation(warm[:], warm[:], ACT.Silu)
+        nc.gpsimd.memset(w1s[:].bitcast(I32), 0)
+        nc.gpsimd.memset(w3s[:].bitcast(I32), 0)
+        for b in range(K // P):
+            nc.vector.memset(win[b][:], 0.0)
+
+        w2_i = w2_words.bitcast(I32)
+        w1_i = w1_words.bitcast(I32)
+        w3_i = w3_words.bitcast(I32)
+
+        def load_words(tile, dram_i, e0, e1):
+            nc.sync.dma_start(
+                tile[:, e0:e1, :].bitcast(I32), dram_i[e0:e1, 0].rearrange("e p b -> p e b")
+            )
+
+        def load_scales(queue, tile, dram):
+            for q in range(4):
+                queue.dma_start(
+                    tile[32 * q : 32 * q + 4].bitcast(I32),
+                    dram.bitcast(I32)[:, 0, 4 * q : 4 * q + 4, :].rearrange("e f i -> f e i"),
+                )
+
+        dy4 = dyT.rearrange("(p j) t -> p j t", j=PACK)
+        a1_4 = a1.rearrange("(p j) s -> p j s", j=PACK)
+        a3_4 = a3.rearrange("(p j) s -> p j s", j=PACK)
+
+        halves = [slice(0, HALF), slice(HALF, 2 * HALF)]
+
+        def load_plane(t):
+            nc.sync.dma_start(planes[t][:], dy4[:, t, :])
+
+        def load_saved(tile, dram, e):
+            cols = slice(e * C, (e + 1) * C)
+            nc.sync.dma_start(tile[:, :, cols], dram[:, :, cols])
+
+        nc.sync.dma_start(offsets[:], offs)
+        load_scales(nc.sync, w2s_raw, w2_scales)
+        nc.sync.dma_start(gate_sb[:, halves[0]], gate[0:P, halves[0]])
+        load_plane(0)
+        load_saved(a1_sb, a1_4, 0)
+        nc.sync.dma_start(gate_sb[:, halves[1]], gate[0:P, halves[1]])
+        load_plane(1)
+        load_words(w2_raw, w2_i, 0, E)
+        load_saved(a1_sb, a1_4, 1)
+        load_plane(2)
+        load_plane(3)
+        load_saved(a3_sb, a3_4, 0)
+        load_saved(a3_sb, a3_4, 1)
+        nc.sync.dma_start(a1_sb[:, :, halves[1]], a1_4[:, :, halves[1]])
+        load_words(w1_sb, w1_i, 0, E)
+        load_words(w3_sb, w3_i, 0, E)
+        nc.sync.dma_start(a3_sb[:, :, halves[1]], a3_4[:, :, halves[1]])
+        load_scales(nc.sync, w1s, w1_scales)
+        load_scales(nc.sync, w3s, w3_scales)
+
+        def permute(e0, e1):
+            nc.vector.tensor_copy(
+                w2_perm[:, e0:e1, :].bitcast(U16).rearrange("p e (t m) -> p e t m", t=PACK),
+                w2_raw[:, e0:e1, :].bitcast(U16).rearrange("p e (m t) -> p e t m", t=PACK),
+            )
+
+        def permute_scales(e0, e1):
+            nc.vector.tensor_copy(
+                w2s_perm[:, e0:e1, :].rearrange("p e (t m) -> p e t m", t=PACK),
+                w2s_raw[:, e0:e1, :].rearrange("p e (m t) -> p e t m", t=PACK),
+            )
+
+        g_planes = [ring.tile([P, PACK, HALF], F32, name=f"g_planes{h}", bufs=1) for h in range(2)]
+
+        def gather(h, t):
+            nc.vector.tensor_tensor(
+                g_planes[h][:, t, :],
+                planes[t][:].indirect(offsets[:, h * 32 : (h + 1) * 32]),
+                gate_sb[:, halves[h]],
+                ALU.mult,
+            )
+
+        g_bf = [keep.tile([P, C, PACK], BF16, name=f"g_bf{e}", align_bytes=64) for e in range(E)]
+        g_codes = [keep.tile([P, C], U32, name=f"g_codes{e}", align_bytes=64) for e in range(E)]
+        g_scales = [keep.tile([P, C], U8, name=f"g_scales{e}", align_bytes=64) for e in range(E)]
+
+        def interleave(e):
+            src = g_planes[e // 2][:, :, (e % 2) * C : (e % 2 + 1) * C]
+            nc.scalar.activation(
+                g_bf[e][:].rearrange("p (c i) j -> p c j i", i=4),
+                src.rearrange("p j (c i) -> p c j i", i=4),
+                ACT.Copy,
+            )
+
+        def quantize_g(e):
+            nc.vector.quantize_mx(
+                out=g_codes[e][:].bitcast(FP8X4),
+                scales=g_scales[e][:],
+                in_=g_bf[e][:].rearrange("p n j -> p (n j)"),
+            )
+
+        def activations(e):
+            cols = slice(e * C, (e + 1) * C)
+            nc.scalar.activation(s_sb[:, :, cols], a1_sb[:, :, cols], ACT.Tanh, scale=0.5)
+            sign = -0.5 if e in ON_VECTOR else 0.5
+            nc.scalar.activation(s_sb[:, :, cols], s_sb[:, :, cols], ACT.Copy, scale=sign, bias=sign)
+            nc.scalar.activation(p_sb[:, :, cols], a1_sb[:, :, cols], ACT.Silu, scale=-1.0)
+            if e not in ON_VECTOR:
+                nc.scalar.activation(p_sb[:, :, cols], p_sb[:, :, cols], ACT.Copy, scale=-1.0, bias=1.0)
+            nc.scalar.activation(h_sb[:, :, cols], a1_sb[:, :, cols], ACT.Silu)
+
+        def factors(e):
+            chunks = [slice(e * C + c * CHUNK, e * C + (c + 1) * CHUNK) for c in range(2)]
+            if e in ON_VECTOR:
+                for cols in chunks:
+                    a3_cols = a3_sb[:, :, cols]
+                    nc.vector.tensor_tensor(a3_cols, s_sb[:, :, cols], a3_cols, ALU.mult)
+                for cols in chunks:
+                    a3_cols = a3_sb[:, :, cols]
+                    nc.vector.scalar_tensor_tensor(a3_cols, p_sb[:, :, cols], 1.0, a3_cols, ALU.subtract, ALU.mult)
+                return
+            for cols in chunks:
+                nc.gpsimd.tensor_tensor(a3_sb[:, :, cols], a3_sb[:, :, cols], s_sb[:, :, cols], ALU.mult)
+                nc.gpsimd.tensor_tensor(a3_sb[:, :, cols], a3_sb[:, :, cols], p_sb[:, :, cols], ALU.mult)
+
+        da_bf = [ring.tile([P, 2, C, PACK], BF16, name=f"da_bf{e}", tag="da_bf", align_bytes=64) for e in range(E)]
+        da_codes = [ring.tile([P, 2, C], U32, name=f"da_codes{e}", tag="da_codes", align_bytes=64) for e in range(E)]
+        da_scales = [ring.tile([P, 2, C], U8, name=f"da_scales{e}", tag="da_scales", align_bytes=64) for e in range(E)]
+        dx_sb = [keep.tile([P, 2, C], F32, name=f"dx_sb{e}") for e in range(E)]
+
+        def hidden(e, c):
+            dh = psum.tile([P, PACK, CHUNK], F32, name="dh", bufs=5)
+            slots = slice(c * CHUNK, (c + 1) * CHUNK)
+            for t in range(PACK):
+                nc.tensor.matmul_mx(
+                    out=dh[:, t, :],
+                    lhsT=w2_perm[:, e, 2 * P * t : 2 * P * (t + 1)].bitcast(FP4X4),
+                    lhsT_scale=w2s_perm[:, e, P * t : P * (t + 1)],
+                    rhs=g_codes[e][:, slots].bitcast(FP8X4),
+                    rhs_scale=g_scales[e][:, slots],
+                    start=True,
+                    stop=True,
+                )
+            cols = slice(e * C + c * CHUNK, e * C + (c + 1) * CHUNK)
+            for i, factor in ((1, h_sb), (0, a3_sb)):
+                factor_nj = factor[:, :, cols].rearrange("p j (c i) -> p c j i", i=4)
+                da_nj = da_bf[e][:, i, slots, :].rearrange("p (c i) j -> p c j i", i=4)
+                if i == 1 and e in DA3_ON_GPSIMD:
+                    dh_sb = ring.tile([P, PACK, CHUNK], F32, name="dh_sb", bufs=2)
+                    nc.scalar.copy(dh_sb[:], dh[:])
+                    nc.gpsimd.tensor_tensor(
+                        da_nj, dh_sb[:].rearrange("p j (c i) -> p c j i", i=4), factor_nj, ALU.mult
+                    )
+                    continue
+                nc.vector.tensor_tensor(
+                    da_nj, dh[:].rearrange("p j (c i) -> p c j i", i=4), factor_nj, ALU.mult
+                )
+
+        def quantize_da(e):
+            nc.vector.quantize_mx(
+                out=da_codes[e][:].rearrange("p i n -> p (i n)").bitcast(FP8X4),
+                scales=da_scales[e][:].rearrange("p i n -> p (i n)"),
+                in_=da_bf[e][:].rearrange("p i n j -> p (i n j)"),
+            )
+
+        def project(e):
+            dx = psum.tile([P, 2, C], F32, name="dx", bufs=3)
+            for b in range(2):
+                for c in range(2):
+                    slots = slice(c * CHUNK, (c + 1) * CHUNK)
+                    for i, (w, ws) in enumerate(((w1_sb, w1s), (w3_sb, w3s))):
+                        nc.tensor.matmul_mx(
+                            out=dx[:, b, slots],
+                            lhsT=w[:, e, 2 * P * b : 2 * P * (b + 1)].bitcast(FP4X4),
+                            lhsT_scale=ws[:, e, P * b : P * (b + 1)],
+                            rhs=da_codes[e][:, i, slots].bitcast(FP8X4),
+                            rhs_scale=da_scales[e][:, i, slots],
+                            start=(i == 0),
+                            stop=(i == 1),
+                        )
+            nc.scalar.copy(dx_sb[e][:], dx[:])
+
+        def scatter(e, b):
+            nc.vector.tensor_copy(win[b][:].indirect(offsets[:, e * 16 : (e + 1) * 16]), dx_sb[e][:, b, :])
+
+        permute_scales(0, E)
+        gather(0, 0)
+        gather(0, 1)
+        gather(0, 2)
+        gather(0, 3)
+        permute(0, E)
+        interleave(0)
+        activations(0)
+        interleave(1)
+        quantize_g(0)
+        quantize_g(1)
+        activations(1)
+        gather(1, 0)
+        gather(1, 1)
+        gather(1, 2)
+        gather(1, 3)
+        interleave(2)
+        interleave(3)
+        quantize_g(2)
+        quantize_g(3)
+        factors(0)
+        hidden(0, 0)
+        hidden(0, 1)
+        quantize_da(0)
+        project(0)
+        activations(2)
+        factors(1)
+        hidden(1, 0)
+        hidden(1, 1)
+        scatter(0, 0)
+        quantize_da(1)
+        project(1)
+        activations(3)
+        scatter(0, 1)
+        factors(2)
+        hidden(2, 0)
+        hidden(2, 1)
+        scatter(1, 0)
+        quantize_da(2)
+        project(2)
+        scatter(1, 1)
+        factors(3)
+        hidden(3, 0)
+        hidden(3, 1)
+        scatter(2, 0)
+        quantize_da(3)
+        project(3)
+        scatter(2, 1)
+        scatter(3, 0)
+        nc.sync.dma_start(out[0 * P : (0 + 1) * P, :], win[0][:])
+        scatter(3, 1)
+        nc.sync.dma_start(out[1 * P : (1 + 1) * P, :], win[1][:])

@@ -24,8 +24,6 @@ C = 256
 S = E * C
 HALF = 512
 CHUNK = 128
-ON_VECTOR = (0,)
-DA3_ON_GPSIMD = (3,)
 
 FLOPS = 2 * S * (N * H + 2 * H * K)
 BYTES = 4 * (N * T + 2 * H * S + K * T + S) + E * P * (2 * H + 4 * K) + E * 16 * (H + 2 * K) + 2 * 16 * S // 16
@@ -44,12 +42,14 @@ def tile_moe_bdx_glu_silu_kernel(
         offsets = listp.tile([P, S // 16], U16, name="offsets")
 
         planes = [keep.tile([P, T], F32, name=f"plane{t}") for t in range(PACK)]
-        gate_sb = keep.tile([P, S], F32, name="gate_sb")
-        a1_sb = keep.tile([P, PACK, S], F32, name="a1_sb")
-        a3_sb = keep.tile([P, PACK, S], F32, name="a3_sb")
-        h_sb = keep.tile([P, PACK, S], F32, name="h_sb")
-        s_sb = keep.tile([P, PACK, S], F32, name="s_sb")
-        p_sb = keep.tile([P, PACK, S], F32, name="p_sb")
+        g_planes = [keep.tile([P, PACK, HALF], F32, name=f"g_planes{h}") for h in range(2)]
+        gate_last = keep.tile([P, HALF], F32, name="gate_last")
+        gate_sb = [g_planes[1][:, 2, :], gate_last[:]]
+        a1_sb = [keep.tile([P, PACK, C], F32, name=f"a1_{e}") for e in range(E)]
+        a3_sb = [keep.tile([P, PACK, C], F32, name=f"a3_{e}") for e in range(E)]
+        h_sb = [keep.tile([P, PACK, C], F32, name=f"h_{e}") for e in range(E)]
+        s_sb = [keep.tile([P, PACK, C], F32, name=f"s_{e}") for e in range(E)]
+        m_sb = [keep.tile([P, PACK, C], F32, name=f"m_{e}") for e in range(E)]
         w2_raw = keep.tile([P, E, 2 * H], U8, name="w2_raw", align_bytes=64)
         w2_perm = keep.tile([P, E, 2 * H], U8, name="w2_perm", align_bytes=64)
         w2s_raw = keep.tile([P, E, H], U8, name="w2s_raw", align_bytes=64)
@@ -61,7 +61,7 @@ def tile_moe_bdx_glu_silu_kernel(
         win = [keep.tile([P, T], F32, name=f"win{b}") for b in range(K // P)]
         warm = keep.tile([P, 1], F32, name="warm")
 
-        nc.vector.memset(w2s_raw[:].bitcast(I32), 0)
+        nc.gpsimd.memset(w2s_raw[:].bitcast(I32), 0)
         nc.vector.memset(warm[:], 0.0)
         nc.scalar.activation(warm[:], warm[:], ACT.Silu)
         nc.gpsimd.memset(w1s[:].bitcast(I32), 0)
@@ -69,18 +69,12 @@ def tile_moe_bdx_glu_silu_kernel(
         for b in range(K // P):
             nc.vector.memset(win[b][:], 0.0)
 
-        w2_i = w2_words.bitcast(I32)
-        w1_i = w1_words.bitcast(I32)
-        w3_i = w3_words.bitcast(I32)
+        def load_words(tile, dram):
+            nc.sync.dma_start(tile[:].bitcast(I32), dram.bitcast(I32)[:, 0].rearrange("e p b -> p e b"))
 
-        def load_words(tile, dram_i, e0, e1):
-            nc.sync.dma_start(
-                tile[:, e0:e1, :].bitcast(I32), dram_i[e0:e1, 0].rearrange("e p b -> p e b")
-            )
-
-        def load_scales(queue, tile, dram):
-            for q in range(4):
-                queue.dma_start(
+        def load_scales(tile, dram, quadrants=range(4)):
+            for q in quadrants:
+                nc.sync.dma_start(
                     tile[32 * q : 32 * q + 4].bitcast(I32),
                     dram.bitcast(I32)[:, 0, 4 * q : 4 * q + 4, :].rearrange("e f i -> f e i"),
                 )
@@ -89,65 +83,68 @@ def tile_moe_bdx_glu_silu_kernel(
         a1_4 = a1.rearrange("(p j) s -> p j s", j=PACK)
         a3_4 = a3.rearrange("(p j) s -> p j s", j=PACK)
 
-        halves = [slice(0, HALF), slice(HALF, 2 * HALF)]
-
         def load_plane(t):
             nc.sync.dma_start(planes[t][:], dy4[:, t, :])
 
-        def load_saved(tile, dram, e):
-            cols = slice(e * C, (e + 1) * C)
-            nc.sync.dma_start(tile[:, :, cols], dram[:, :, cols])
+        def load_gate(h):
+            nc.sync.dma_start(gate_sb[h], gate[0:P, h * HALF : (h + 1) * HALF])
+
+        def load_a1(e):
+            nc.sync.dma_start(a1_sb[e][:], a1_4[:, :, e * C : (e + 1) * C])
+
+        def load_a3(e):
+            nc.sync.dma_start(a3_sb[e][:], a3_4[:, :, e * C : (e + 1) * C])
 
         nc.sync.dma_start(offsets[:], offs)
-        load_scales(nc.sync, w2s_raw, w2_scales)
-        nc.sync.dma_start(gate_sb[:, halves[0]], gate[0:P, halves[0]])
+        load_gate(0)
         load_plane(0)
-        load_saved(a1_sb, a1_4, 0)
-        nc.sync.dma_start(gate_sb[:, halves[1]], gate[0:P, halves[1]])
+        load_gate(1)
+        load_scales(w2s_raw, w2_scales)
+        load_a1(0)
         load_plane(1)
-        load_words(w2_raw, w2_i, 0, E)
-        load_saved(a1_sb, a1_4, 1)
+        load_words(w2_raw, w2_words)
+        load_a1(1)
         load_plane(2)
         load_plane(3)
-        load_saved(a3_sb, a3_4, 0)
-        load_saved(a3_sb, a3_4, 1)
-        nc.sync.dma_start(a1_sb[:, :, halves[1]], a1_4[:, :, halves[1]])
-        load_words(w1_sb, w1_i, 0, E)
-        load_words(w3_sb, w3_i, 0, E)
-        nc.sync.dma_start(a3_sb[:, :, halves[1]], a3_4[:, :, halves[1]])
-        load_scales(nc.sync, w1s, w1_scales)
-        load_scales(nc.sync, w3s, w3_scales)
+        load_a1(2)
+        load_a1(3)
+        load_words(w1_sb, w1_words)
+        load_words(w3_sb, w3_words)
+        load_a3(0)
+        load_a3(1)
+        load_scales(w1s, w1_scales)
+        load_a3(2)
+        load_scales(w3s, w3_scales)
+        load_a3(3)
 
-        def permute(e0, e1):
+        def permute_words():
             nc.vector.tensor_copy(
-                w2_perm[:, e0:e1, :].bitcast(U16).rearrange("p e (t m) -> p e t m", t=PACK),
-                w2_raw[:, e0:e1, :].bitcast(U16).rearrange("p e (m t) -> p e t m", t=PACK),
+                w2_perm[:].bitcast(U16).rearrange("p e (t m) -> p e t m", t=PACK),
+                w2_raw[:].bitcast(U16).rearrange("p e (m t) -> p e t m", t=PACK),
             )
 
-        def permute_scales(e0, e1):
+        def permute_scales():
             nc.vector.tensor_copy(
-                w2s_perm[:, e0:e1, :].rearrange("p e (t m) -> p e t m", t=PACK),
-                w2s_raw[:, e0:e1, :].rearrange("p e (m t) -> p e t m", t=PACK),
+                w2s_perm[:].rearrange("p e (t m) -> p e t m", t=PACK),
+                w2s_raw[:].rearrange("p e (m t) -> p e t m", t=PACK),
             )
-
-        g_planes = [ring.tile([P, PACK, HALF], F32, name=f"g_planes{h}", bufs=1) for h in range(2)]
 
         def gather(h, t):
             nc.vector.tensor_tensor(
                 g_planes[h][:, t, :],
                 planes[t][:].indirect(offsets[:, h * 32 : (h + 1) * 32]),
-                gate_sb[:, halves[h]],
+                gate_sb[h],
                 ALU.mult,
             )
 
-        g_bf = [keep.tile([P, C, PACK], BF16, name=f"g_bf{e}", align_bytes=64) for e in range(E)]
-        g_codes = [keep.tile([P, C], U32, name=f"g_codes{e}", align_bytes=64) for e in range(E)]
-        g_scales = [keep.tile([P, C], U8, name=f"g_scales{e}", align_bytes=64) for e in range(E)]
+        g_bf = [keep.tile([P, HALF, PACK], BF16, name=f"g_bf{h}", align_bytes=64) for h in range(2)]
+        g_codes = [keep.tile([P, HALF], U32, name=f"g_codes{h}", align_bytes=64) for h in range(2)]
+        g_scales = [keep.tile([P, HALF], U8, name=f"g_scales{h}", align_bytes=64) for h in range(2)]
 
         def interleave(e):
             src = g_planes[e // 2][:, :, (e % 2) * C : (e % 2 + 1) * C]
             nc.scalar.activation(
-                g_bf[e][:].rearrange("p (c i) j -> p c j i", i=4),
+                g_bf[e // 2][:, (e % 2) * C : (e % 2 + 1) * C, :].rearrange("p (c i) j -> p c j i", i=4),
                 src.rearrange("p j (c i) -> p c j i", i=4),
                 ACT.Copy,
             )
@@ -159,62 +156,78 @@ def tile_moe_bdx_glu_silu_kernel(
                 in_=g_bf[e][:].rearrange("p n j -> p (n j)"),
             )
 
-        def activations(e):
-            cols = slice(e * C, (e + 1) * C)
-            nc.scalar.activation(s_sb[:, :, cols], a1_sb[:, :, cols], ACT.Tanh, scale=0.5)
-            sign = -0.5 if e in ON_VECTOR else 0.5
-            nc.scalar.activation(s_sb[:, :, cols], s_sb[:, :, cols], ACT.Copy, scale=sign, bias=sign)
-            nc.scalar.activation(p_sb[:, :, cols], a1_sb[:, :, cols], ACT.Silu, scale=-1.0)
-            if e not in ON_VECTOR:
-                nc.scalar.activation(p_sb[:, :, cols], p_sb[:, :, cols], ACT.Copy, scale=-1.0, bias=1.0)
-            nc.scalar.activation(h_sb[:, :, cols], a1_sb[:, :, cols], ACT.Silu)
+        def act_m(e):
+            nc.scalar.activation(m_sb[e][:], a1_sb[e][:], ACT.Silu, scale=-1.0)
 
-        def factors(e):
-            chunks = [slice(e * C + c * CHUNK, e * C + (c + 1) * CHUNK) for c in range(2)]
-            if e in ON_VECTOR:
-                for cols in chunks:
-                    a3_cols = a3_sb[:, :, cols]
-                    nc.vector.tensor_tensor(a3_cols, s_sb[:, :, cols], a3_cols, ALU.mult)
-                for cols in chunks:
-                    a3_cols = a3_sb[:, :, cols]
-                    nc.vector.scalar_tensor_tensor(a3_cols, p_sb[:, :, cols], 1.0, a3_cols, ALU.subtract, ALU.mult)
-                return
-            for cols in chunks:
-                nc.gpsimd.tensor_tensor(a3_sb[:, :, cols], a3_sb[:, :, cols], s_sb[:, :, cols], ALU.mult)
-                nc.gpsimd.tensor_tensor(a3_sb[:, :, cols], a3_sb[:, :, cols], p_sb[:, :, cols], ALU.mult)
+        def act_h(e):
+            nc.scalar.activation(h_sb[e][:], a1_sb[e][:], ACT.Silu)
 
-        da_bf = [ring.tile([P, 2, C, PACK], BF16, name=f"da_bf{e}", tag="da_bf", align_bytes=64) for e in range(E)]
+        def act_s(e):
+            nc.scalar.activation(s_sb[e][:], a1_sb[e][:], ACT.Tanh, scale=0.5)
+            nc.scalar.activation(s_sb[e][:], s_sb[e][:], ACT.Copy, scale=-0.5, bias=-0.5)
+
+        def chunk_cols(c):
+            return slice(c * CHUNK, (c + 1) * CHUNK)
+
+        def factor(e, c):
+            cols = chunk_cols(c)
+            nc.gpsimd.tensor_tensor(a3_sb[e][:, :, cols], a3_sb[e][:, :, cols], s_sb[e][:, :, cols], ALU.mult)
+
+        da_bf = [ring.tile([P, 2, C, PACK], BF16, name=f"da_bf{e}", tag="da_bf", bufs=4, align_bytes=64) for e in range(E)]
         da_codes = [ring.tile([P, 2, C], U32, name=f"da_codes{e}", tag="da_codes", align_bytes=64) for e in range(E)]
         da_scales = [ring.tile([P, 2, C], U8, name=f"da_scales{e}", tag="da_scales", align_bytes=64) for e in range(E)]
-        dx_sb = [keep.tile([P, 2, C], F32, name=f"dx_sb{e}") for e in range(E)]
+        dx_last = keep.tile([P, 2, C], F32, name="dx_last")
+        dx_own = keep.tile([P, E, C], F32, name="dx_own")
+        dx_sb = [[dx_own[:, e, :], a3_sb[e + 1][:, 0, :] if e + 1 < E else dx_last[:, 1, :]] for e in range(E)]
+
+        def walk_planes(ap):
+            return ap.rearrange("p j (c i) -> p c j i", i=4)
+
+        def walk_packed(ap):
+            return ap.rearrange("p (c i) j -> p c j i", i=4)
+
+        dh_ps = {}
+        parts = {}
 
         def hidden(e, c):
             dh = psum.tile([P, PACK, CHUNK], F32, name="dh", bufs=5)
-            slots = slice(c * CHUNK, (c + 1) * CHUNK)
+            dh_ps[e, c] = dh
+            slots = slice((e % 2) * C + c * CHUNK, (e % 2) * C + (c + 1) * CHUNK)
             for t in range(PACK):
                 nc.tensor.matmul_mx(
                     out=dh[:, t, :],
                     lhsT=w2_perm[:, e, 2 * P * t : 2 * P * (t + 1)].bitcast(FP4X4),
                     lhsT_scale=w2s_perm[:, e, P * t : P * (t + 1)],
-                    rhs=g_codes[e][:, slots].bitcast(FP8X4),
-                    rhs_scale=g_scales[e][:, slots],
+                    rhs=g_codes[e // 2][:, slots].bitcast(FP8X4),
+                    rhs_scale=g_scales[e // 2][:, slots],
                     start=True,
                     stop=True,
                 )
-            cols = slice(e * C + c * CHUNK, e * C + (c + 1) * CHUNK)
-            for i, factor in ((1, h_sb), (0, a3_sb)):
-                factor_nj = factor[:, :, cols].rearrange("p j (c i) -> p c j i", i=4)
-                da_nj = da_bf[e][:, i, slots, :].rearrange("p (c i) j -> p c j i", i=4)
-                if i == 1 and e in DA3_ON_GPSIMD:
-                    dh_sb = ring.tile([P, PACK, CHUNK], F32, name="dh_sb", bufs=2)
-                    nc.scalar.copy(dh_sb[:], dh[:])
-                    nc.gpsimd.tensor_tensor(
-                        da_nj, dh_sb[:].rearrange("p j (c i) -> p c j i", i=4), factor_nj, ALU.mult
-                    )
-                    continue
-                nc.vector.tensor_tensor(
-                    da_nj, dh[:].rearrange("p j (c i) -> p c j i", i=4), factor_nj, ALU.mult
-                )
+
+        def partial(e, c):
+            part = ring.tile([P, PACK, CHUNK], F32, name="part", bufs=8)
+            parts[e, c] = part
+            nc.vector.scalar_tensor_tensor(
+                part[:], m_sb[e][:, :, chunk_cols(c)], 1.0, dh_ps[e, c][:], ALU.subtract, ALU.mult
+            )
+
+        def da3(e, c):
+            cols = chunk_cols(c)
+            nc.vector.tensor_tensor(
+                walk_packed(da_bf[e][:, 1, cols, :]),
+                walk_planes(dh_ps[e, c][:]),
+                walk_planes(h_sb[e][:, :, cols]),
+                ALU.mult,
+            )
+
+        def da1(e, c, engine):
+            cols = chunk_cols(c)
+            engine.tensor_tensor(
+                walk_packed(da_bf[e][:, 0, cols, :]),
+                walk_planes(parts[e, c][:]),
+                walk_planes(a3_sb[e][:, :, cols]),
+                ALU.mult,
+            )
 
         def quantize_da(e):
             nc.vector.quantize_mx(
@@ -223,75 +236,125 @@ def tile_moe_bdx_glu_silu_kernel(
                 in_=da_bf[e][:].rearrange("p i n j -> p (i n j)"),
             )
 
+        dx_ps = {}
+
         def project(e):
             dx = psum.tile([P, 2, C], F32, name="dx", bufs=3)
             for b in range(2):
                 for c in range(2):
-                    slots = slice(c * CHUNK, (c + 1) * CHUNK)
+                    cols = chunk_cols(c)
                     for i, (w, ws) in enumerate(((w1_sb, w1s), (w3_sb, w3s))):
                         nc.tensor.matmul_mx(
-                            out=dx[:, b, slots],
+                            out=dx[:, b, cols],
                             lhsT=w[:, e, 2 * P * b : 2 * P * (b + 1)].bitcast(FP4X4),
                             lhsT_scale=ws[:, e, P * b : P * (b + 1)],
-                            rhs=da_codes[e][:, i, slots].bitcast(FP8X4),
-                            rhs_scale=da_scales[e][:, i, slots],
+                            rhs=da_codes[e][:, i, cols].bitcast(FP8X4),
+                            rhs_scale=da_scales[e][:, i, cols],
                             start=(i == 0),
                             stop=(i == 1),
                         )
-            nc.scalar.copy(dx_sb[e][:], dx[:])
+            dx_ps[e] = dx
+
+        def copy_out(e, b):
+            nc.scalar.copy(dx_sb[e][b], dx_ps[e][:, b, :])
 
         def scatter(e, b):
-            nc.vector.tensor_copy(win[b][:].indirect(offsets[:, e * 16 : (e + 1) * 16]), dx_sb[e][:, b, :])
+            nc.vector.tensor_copy(win[b][:].indirect(offsets[:, e * 16 : (e + 1) * 16]), dx_sb[e][b])
 
-        permute_scales(0, E)
+        def store(b):
+            nc.sync.dma_start(out[b * P : (b + 1) * P, :], win[b][:])
+
         gather(0, 0)
+        gather(1, 0)
+        permute_scales()
+        act_m(0)
+        act_h(0)
+        act_s(0)
         gather(0, 1)
+        gather(1, 1)
+        permute_words()
+        act_m(1)
+        act_h(1)
         gather(0, 2)
         gather(0, 3)
-        permute(0, E)
         interleave(0)
-        activations(0)
         interleave(1)
-        quantize_g(0)
-        quantize_g(1)
-        activations(1)
-        gather(1, 0)
-        gather(1, 1)
         gather(1, 2)
         gather(1, 3)
+        quantize_g(0)
         interleave(2)
         interleave(3)
-        quantize_g(2)
-        quantize_g(3)
-        factors(0)
+        factor(0, 0)
+        factor(0, 1)
         hidden(0, 0)
+        partial(0, 0)
+        da3(0, 0)
+        da1(0, 0, nc.gpsimd)
         hidden(0, 1)
+        partial(0, 1)
+        da3(0, 1)
+        da1(0, 1, nc.gpsimd)
+        quantize_g(1)
+        act_s(1)
+        factor(1, 0)
+        factor(1, 1)
+        hidden(1, 0)
+        partial(1, 0)
+        da3(1, 0)
+        da1(1, 0, nc.gpsimd)
+        hidden(1, 1)
+        partial(1, 1)
+        da3(1, 1)
+        da1(1, 1, nc.gpsimd)
         quantize_da(0)
         project(0)
-        activations(2)
-        factors(1)
-        hidden(1, 0)
-        hidden(1, 1)
+        act_m(2)
+        act_h(2)
+        copy_out(0, 0)
         scatter(0, 0)
+        act_s(2)
+        factor(2, 0)
+        factor(2, 1)
+        hidden(2, 0)
+        partial(2, 0)
+        da3(2, 0)
+        da1(2, 0, nc.gpsimd)
+        hidden(2, 1)
+        partial(2, 1)
+        da3(2, 1)
+        da1(2, 1, nc.gpsimd)
         quantize_da(1)
         project(1)
-        activations(3)
+        copy_out(0, 1)
         scatter(0, 1)
-        factors(2)
-        hidden(2, 0)
-        hidden(2, 1)
+        act_m(3)
+        act_h(3)
+        copy_out(1, 0)
         scatter(1, 0)
+        act_s(3)
+        factor(3, 0)
+        factor(3, 1)
+        hidden(3, 0)
+        partial(3, 0)
+        da3(3, 0)
+        da1(3, 0, nc.vector)
+        hidden(3, 1)
+        partial(3, 1)
+        da3(3, 1)
+        da1(3, 1, nc.vector)
         quantize_da(2)
         project(2)
+        copy_out(1, 1)
         scatter(1, 1)
-        factors(3)
-        hidden(3, 0)
-        hidden(3, 1)
+        copy_out(2, 0)
         scatter(2, 0)
         quantize_da(3)
         project(3)
+        copy_out(2, 1)
         scatter(2, 1)
+        copy_out(3, 0)
+        copy_out(3, 1)
         scatter(3, 0)
-        nc.sync.dma_start(out[0 * P : (0 + 1) * P, :], win[0][:])
+        store(0)
         scatter(3, 1)
-        nc.sync.dma_start(out[1 * P : (1 + 1) * P, :], win[1][:])
+        store(1)

@@ -1,6 +1,7 @@
 from contextlib import ExitStack
 
 import concourse.mybir as mybir
+from concourse.masks import make_identity
 
 F32 = mybir.dt.float32
 BF16 = mybir.dt.bfloat16
@@ -24,6 +25,10 @@ C = 256
 S = E * C
 HALF = 512
 CHUNK = 128
+TURN_BANK = (0, 1, 2, 3, 7, 6, 0, 1)
+HIDDEN_BANK = (0, 1, 4, 5, 2, 4, 3, 5)
+HOMES = {("s", 1): "gated3", ("m", 2): "gated4", ("h", 2): "gated5", ("t", 2): "tanh_1", ("m", 3): "gated7", ("h", 3): "gated6", ("t", 3): "tanh_1", ("dx", 0, 1): "da_bf1", ("dx", 1, 1): "da_bf2", ("dx", 2, 1): "da_bf3", ("codes", 0): "h_1", ("codes", 1): "gated5", ("codes", 2): "gated6", ("codes", 3): "dx_sb20"}
+LATE_HOME = {2: "gathered3"}
 
 FLOPS = 2 * S * (N * H + 2 * H * K)
 BYTES = 4 * (N * T + 2 * H * S + K * T + S) + E * P * (2 * H + 4 * K) + E * 16 * (H + 2 * K) + 2 * 16 * S // 16
@@ -42,16 +47,23 @@ def tile_moe_bdx_glu_silu_kernel(
         offsets = listp.tile([P, S // 16], U16, name="offsets")
 
         planes = [keep.tile([P, T], F32, name=f"plane{t}") for t in range(PACK)]
-        g_planes = [keep.tile([P, PACK, HALF], F32, name=f"g_planes{h}") for h in range(2)]
-        gate_last = keep.tile([P, HALF], F32, name="gate_last")
-        gate_sb = [g_planes[1][:, 2, :], gate_last[:]]
-        a1_sb = [keep.tile([P, PACK, C], F32, name=f"a1_{e}") for e in range(E)]
-        a3_sb = [keep.tile([P, PACK, C], F32, name=f"a3_{e}") for e in range(E)]
-        h_sb = [keep.tile([P, PACK, C], F32, name=f"h_{e}") for e in range(E)]
-        s_sb = [keep.tile([P, PACK, C], F32, name=f"s_{e}") for e in range(E)]
-        m_sb = [keep.tile([P, PACK, C], F32, name=f"m_{e}") for e in range(E)]
-        w2_raw = keep.tile([P, E, 2 * H], U8, name="w2_raw", align_bytes=64)
-        w2_perm = keep.tile([P, E, 2 * H], U8, name="w2_perm", align_bytes=64)
+        early = [keep.tile([P, HALF], F32, name=f"early{t}", tag=f"gathered{t}")[:] for t in range(PACK)]
+        late = [keep.tile([P, HALF], F32, name=f"late{t}", tag=LATE_HOME.get(t, f"late{t}"))[:] for t in range(PACK)]
+        g_planes = [early, late]
+        gate_rows = keep.tile([P, P], F32, name="gate_rows")
+        gate_col = keep.tile([P, S // P], F32, name="gate_col")
+        ident = keep.tile([P, P], F32, name="ident")
+        a1_late = keep.tile([P, PACK, HALF], F32, name="a1_late")
+        a3_late = keep.tile([P, PACK, HALF], F32, name="a3_late")
+        a1_sb = [keep.tile([P, PACK, C], F32, name=f"a1_{e}")[:] for e in range(2)]
+        a3_sb = [keep.tile([P, PACK, C], F32, name=f"a3_{e}")[:] for e in range(2)]
+        a1_sb = a1_sb + [a1_late[:, :, 0:C], a1_late[:, :, C:HALF]]
+        a3_sb = a3_sb + [a3_late[:, :, 0:C], a3_late[:, :, C:HALF]]
+        h_sb, m_sb, s_sb, tanh_sb = {}, {}, {}, {}
+        w2_raw = [
+            keep.tile([P, 2, 2 * H], U8, name="w2_raw_early", align_bytes=64),
+            keep.tile([P, 2, 2 * H], U8, name="w2_raw_late", align_bytes=64),
+        ]
         w2s_raw = keep.tile([P, E, H], U8, name="w2s_raw", align_bytes=64)
         w2s_perm = keep.tile([P, E, H], U8, name="w2s_perm", align_bytes=64)
         w1_sb = keep.tile([P, E, 2 * K], U8, name="w1_sb", align_bytes=64)
@@ -62,15 +74,21 @@ def tile_moe_bdx_glu_silu_kernel(
         warm = keep.tile([P, 1], F32, name="warm")
 
         nc.gpsimd.memset(w2s_raw[:].bitcast(I32), 0)
+        nc.gpsimd.memset(gate_rows[:], 0.0)
+        make_identity(nc, ident[:])
         nc.vector.memset(warm[:], 0.0)
         nc.scalar.activation(warm[:], warm[:], ACT.Silu)
         nc.gpsimd.memset(w1s[:].bitcast(I32), 0)
         nc.gpsimd.memset(w3s[:].bitcast(I32), 0)
         for b in range(K // P):
-            nc.vector.memset(win[b][:], 0.0)
+            nc.gpsimd.memset(win[b][:], 0.0)
 
         def load_words(tile, dram):
             nc.sync.dma_start(tile[:].bitcast(I32), dram.bitcast(I32)[:, 0].rearrange("e p b -> p e b"))
+
+        def load_w2(h):
+            words = w2_words.bitcast(I32)[2 * h : 2 * h + 2, 0]
+            nc.sync.dma_start(w2_raw[h][:].bitcast(I32), words.rearrange("e p b -> p e b"))
 
         def load_scales(tile, dram, quadrants=range(4)):
             for q in quadrants:
@@ -86,41 +104,44 @@ def tile_moe_bdx_glu_silu_kernel(
         def load_plane(t):
             nc.sync.dma_start(planes[t][:], dy4[:, t, :])
 
-        def load_gate(h):
-            nc.sync.dma_start(gate_sb[h], gate[0:P, h * HALF : (h + 1) * HALF])
+        def load_gate():
+            nc.sync.dma_start(gate_rows[0 : S // P, :], gate[0, :].rearrange("(b n) -> b n", n=P))
+
+        def turn_gate():
+            turned = psum.tile([P, P], F32, name="turned", tag="bank6")
+            nc.tensor.transpose(turned[:], gate_rows[:], ident[:])
+            nc.scalar.copy(gate_col[:], turned[:, 0 : S // P])
 
         def load_a1(e):
-            nc.sync.dma_start(a1_sb[e][:], a1_4[:, :, e * C : (e + 1) * C])
+            nc.sync.dma_start(a1_sb[e], a1_4[:, :, e * C : (e + 1) * C])
 
         def load_a3(e):
-            nc.sync.dma_start(a3_sb[e][:], a3_4[:, :, e * C : (e + 1) * C])
+            nc.sync.dma_start(a3_sb[e], a3_4[:, :, e * C : (e + 1) * C])
 
         nc.sync.dma_start(offsets[:], offs)
-        load_gate(0)
-        load_plane(0)
-        load_gate(1)
         load_scales(w2s_raw, w2_scales)
+        load_plane(0)
+        load_gate()
         load_a1(0)
         load_plane(1)
-        load_words(w2_raw, w2_words)
         load_a1(1)
+        load_w2(0)
         load_plane(2)
         load_plane(3)
-        load_a1(2)
-        load_a1(3)
+        load_a3(0)
+        load_w2(1)
+        nc.sync.dma_start(a1_late[:], a1_4[:, :, HALF:])
+        load_a3(1)
         load_words(w1_sb, w1_words)
         load_words(w3_sb, w3_words)
-        load_a3(0)
-        load_a3(1)
         load_scales(w1s, w1_scales)
-        load_a3(2)
         load_scales(w3s, w3_scales)
-        load_a3(3)
+        nc.sync.dma_start(a3_late[:], a3_4[:, :, HALF:])
 
-        def permute_words():
+        def permute_words(h):
             nc.vector.tensor_copy(
-                w2_perm[:].bitcast(U16).rearrange("p e (t m) -> p e t m", t=PACK),
-                w2_raw[:].bitcast(U16).rearrange("p e (m t) -> p e t m", t=PACK),
+                w2_perm[h][:].bitcast(U16).rearrange("p e (t m) -> p e t m", t=PACK),
+                w2_raw[h][:].bitcast(U16).rearrange("p e (m t) -> p e t m", t=PACK),
             )
 
         def permute_scales():
@@ -130,55 +151,87 @@ def tile_moe_bdx_glu_silu_kernel(
             )
 
         def gather(h, t):
-            nc.vector.tensor_tensor(
-                g_planes[h][:, t, :],
+            nc.vector.tensor_copy(
+                g_planes[h][t],
                 planes[t][:].indirect(offsets[:, h * 32 : (h + 1) * 32]),
-                gate_sb[h],
-                ALU.mult,
             )
 
-        g_bf = [keep.tile([P, HALF, PACK], BF16, name=f"g_bf{h}", align_bytes=64) for h in range(2)]
-        g_codes = [keep.tile([P, HALF], U32, name=f"g_codes{h}", align_bytes=64) for h in range(2)]
-        g_scales = [keep.tile([P, HALF], U8, name=f"g_scales{h}", align_bytes=64) for h in range(2)]
+        g_bf = {}
+        w2_perm = [
+            keep.tile([P, 2, 2 * H], U8, name="w2_perm_early", align_bytes=64),
+            keep.tile([P, 2, 2 * H], U8, name="w2_perm_late", align_bytes=64),
+        ]
+        g_codes = keep.tile([P, S], U32, name="g_codes", align_bytes=64)
+        g_scales = keep.tile([P, S], U8, name="g_scales", align_bytes=64)
 
-        def interleave(e):
-            src = g_planes[e // 2][:, :, (e % 2) * C : (e % 2 + 1) * C]
+        def turn_block(block):
+            e, c = divmod(block, 2)
+            cols = slice((block % 4) * P, (block % 4 + 1) * P)
+            by_slot = psum.tile([P, PACK, P], F32, name=f"by_slot{block}", tag=f"bank{TURN_BANK[block]}")
+            for t in range(PACK):
+                nc.tensor.transpose(by_slot[:, t, :], g_planes[e // 2][t][:, cols], ident[:])
+            gated = keep.tile([P, 2, P, 2], BF16, name=f"gated{block}", tag=f"gated{block}", align_bytes=64)
             nc.scalar.activation(
-                g_bf[e // 2][:, (e % 2) * C : (e % 2 + 1) * C, :].rearrange("p (c i) j -> p c j i", i=4),
-                src.rearrange("p j (c i) -> p c j i", i=4),
+                gated[:],
+                by_slot[:].rearrange("s (u v) p -> s u p v", u=2),
                 ACT.Copy,
+                scale=gate_col[:, block : block + 1],
+            )
+            return gated[:].rearrange("s u p v -> s (u p v)").bitcast(F32)
+
+        def pack_blocks(blocks, bank):
+            words = psum.tile([P, len(blocks), 2, P], F32, name=f"words{blocks[0]}", tag=f"bank{bank}")
+            for n, block in enumerate(blocks):
+                pairs = turn_block(block)
+                for u in range(2):
+                    nc.tensor.transpose(words[:, n, u, :], pairs[:, u * P : (u + 1) * P], ident[:])
+            packed = keep.tile([P, len(blocks), P, 2], F32, name=f"packed{blocks[0]}", tag=f"packed{blocks[0]}", align_bytes=64)
+            g_bf[blocks[0]] = packed
+            nc.scalar.copy(
+                packed[:],
+                words[:].rearrange("p c u s -> p c s u"),
             )
 
-        def quantize_g(e):
+        def quantize_g(first, count):
+            slots = slice(first * P, (first + count) * P)
             nc.vector.quantize_mx(
-                out=g_codes[e][:].bitcast(FP8X4),
-                scales=g_scales[e][:],
-                in_=g_bf[e][:].rearrange("p n j -> p (n j)"),
+                out=g_codes[:, slots].bitcast(FP8X4),
+                scales=g_scales[:, slots],
+                in_=g_bf[first][:].rearrange("p c s u -> p (c s u)").bitcast(BF16),
             )
 
         def act_m(e):
-            nc.scalar.activation(m_sb[e][:], a1_sb[e][:], ACT.Silu, scale=-1.0)
+            m_sb[e] = keep.tile([P, PACK, C], F32, name=f"m_{e}", tag=HOMES.get(("m", e), f"m_{e}"), align_bytes=64)[:]
+            nc.scalar.activation(m_sb[e], a1_sb[e], ACT.Silu, scale=-1.0)
 
         def act_h(e):
-            nc.scalar.activation(h_sb[e][:], a1_sb[e][:], ACT.Silu)
+            h_sb[e] = keep.tile([P, PACK, C], F32, name=f"h_{e}", tag=HOMES.get(("h", e), f"h_{e}"), align_bytes=64)[:]
+            nc.scalar.activation(h_sb[e], a1_sb[e], ACT.Silu)
 
         def act_s(e):
-            nc.scalar.activation(s_sb[e][:], a1_sb[e][:], ACT.Tanh, scale=0.5)
-            nc.scalar.activation(s_sb[e][:], s_sb[e][:], ACT.Copy, scale=-0.5, bias=-0.5)
+            tanh_sb[e] = keep.tile([P, PACK, C], F32, name=f"tanh_{e}", tag=HOMES.get(("t", e), f"tanh_{e}"), align_bytes=64)[:]
+            nc.scalar.activation(tanh_sb[e], a1_sb[e], ACT.Tanh, scale=0.5)
+
+        def act_affine(e):
+            s_sb[e] = keep.tile([P, PACK, C], F32, name=f"s_{e}", tag=HOMES.get(("s", e), f"s_{e}"), align_bytes=64)[:]
+            nc.scalar.activation(s_sb[e], tanh_sb[e], ACT.Copy, scale=-0.5, bias=-0.5)
 
         def chunk_cols(c):
             return slice(c * CHUNK, (c + 1) * CHUNK)
 
+        y_sb = a3_sb
+
+        def factor_whole(e, engine=nc.gpsimd):
+            engine.tensor_tensor(y_sb[e], a3_sb[e], s_sb[e], ALU.mult)
+
         def factor(e, c):
             cols = chunk_cols(c)
-            nc.gpsimd.tensor_tensor(a3_sb[e][:, :, cols], a3_sb[e][:, :, cols], s_sb[e][:, :, cols], ALU.mult)
+            nc.gpsimd.tensor_tensor(y_sb[e][:, :, cols], a3_sb[e][:, :, cols], s_sb[e][:, :, cols], ALU.mult)
 
-        da_bf = [ring.tile([P, 2, C, PACK], BF16, name=f"da_bf{e}", tag="da_bf", bufs=4, align_bytes=64) for e in range(E)]
-        da_codes = [ring.tile([P, 2, C], U32, name=f"da_codes{e}", tag="da_codes", align_bytes=64) for e in range(E)]
-        da_scales = [ring.tile([P, 2, C], U8, name=f"da_scales{e}", tag="da_scales", align_bytes=64) for e in range(E)]
-        dx_last = keep.tile([P, 2, C], F32, name="dx_last")
-        dx_own = keep.tile([P, E, C], F32, name="dx_own")
-        dx_sb = [[dx_own[:, e, :], a3_sb[e + 1][:, 0, :] if e + 1 < E else dx_last[:, 1, :]] for e in range(E)]
+        da_bf = [keep.tile([P, 2, C, PACK], BF16, name=f"da_bf{e}", tag=f"da_bf{e}", align_bytes=64) for e in range(E)]
+        da_codes = {}
+        da_scales = [ring.tile([P, 2, C], U8, name=f"da_scales{e}", tag="da_scales", bufs=4, align_bytes=64) for e in range(E)]
+        dx_sb = {}
 
         def walk_planes(ap):
             return ap.rearrange("p j (c i) -> p c j i", i=4)
@@ -190,22 +243,22 @@ def tile_moe_bdx_glu_silu_kernel(
         parts = {}
 
         def hidden(e, c):
-            dh = psum.tile([P, PACK, CHUNK], F32, name="dh", bufs=5)
+            dh = psum.tile([P, PACK, CHUNK], F32, name=f"dh{e}{c}", tag=f"bank{HIDDEN_BANK[2 * e + c]}")
             dh_ps[e, c] = dh
-            slots = slice((e % 2) * C + c * CHUNK, (e % 2) * C + (c + 1) * CHUNK)
+            slots = slice(e * C + c * CHUNK, e * C + (c + 1) * CHUNK)
             for t in range(PACK):
                 nc.tensor.matmul_mx(
                     out=dh[:, t, :],
-                    lhsT=w2_perm[:, e, 2 * P * t : 2 * P * (t + 1)].bitcast(FP4X4),
+                    lhsT=w2_perm[e // 2][:, e % 2, 2 * P * t : 2 * P * (t + 1)].bitcast(FP4X4),
                     lhsT_scale=w2s_perm[:, e, P * t : P * (t + 1)],
-                    rhs=g_codes[e // 2][:, slots].bitcast(FP8X4),
-                    rhs_scale=g_scales[e // 2][:, slots],
+                    rhs=g_codes[:, slots].bitcast(FP8X4),
+                    rhs_scale=g_scales[:, slots],
                     start=True,
                     stop=True,
                 )
 
         def partial(e, c):
-            part = ring.tile([P, PACK, CHUNK], F32, name="part", bufs=8)
+            part = keep.tile([P, PACK, CHUNK], F32, name=f"part{e}{c}", tag=f"part{e}{c}", align_bytes=64)
             parts[e, c] = part
             nc.vector.scalar_tensor_tensor(
                 part[:], m_sb[e][:, :, chunk_cols(c)], 1.0, dh_ps[e, c][:], ALU.subtract, ALU.mult
@@ -225,11 +278,13 @@ def tile_moe_bdx_glu_silu_kernel(
             engine.tensor_tensor(
                 walk_packed(da_bf[e][:, 0, cols, :]),
                 walk_planes(parts[e, c][:]),
-                walk_planes(a3_sb[e][:, :, cols]),
+                walk_planes(y_sb[e][:, :, cols]),
                 ALU.mult,
             )
 
         def quantize_da(e):
+            home = HOMES.get(("codes", e), f"da_codes{e}")
+            da_codes[e] = keep.tile([P, 2, C], U32, name=f"da_codes{e}", tag=home, align_bytes=64)
             nc.vector.quantize_mx(
                 out=da_codes[e][:].rearrange("p i n -> p (i n)").bitcast(FP8X4),
                 scales=da_scales[e][:].rearrange("p i n -> p (i n)"),
@@ -239,7 +294,7 @@ def tile_moe_bdx_glu_silu_kernel(
         dx_ps = {}
 
         def project(e):
-            dx = psum.tile([P, 2, C], F32, name="dx", bufs=3)
+            dx = psum.tile([P, 2, C], F32, name=f"dx{e}", tag=f"bank{6 + e % 2}")
             for b in range(2):
                 for c in range(2):
                     cols = chunk_cols(c)
@@ -256,34 +311,41 @@ def tile_moe_bdx_glu_silu_kernel(
             dx_ps[e] = dx
 
         def copy_out(e, b):
-            nc.scalar.copy(dx_sb[e][b], dx_ps[e][:, b, :])
+            home = HOMES.get(("dx", e, b), f"dx_sb{e}{b}")
+            dx_sb[e, b] = keep.tile([P, C], F32, name=f"dx_sb{e}{b}", tag=home, align_bytes=64)
+            nc.scalar.copy(dx_sb[e, b][:], dx_ps[e][:, b, :])
 
         def scatter(e, b):
-            nc.vector.tensor_copy(win[b][:].indirect(offsets[:, e * 16 : (e + 1) * 16]), dx_sb[e][b])
+            nc.vector.tensor_copy(win[b][:].indirect(offsets[:, e * 16 : (e + 1) * 16]), dx_sb[e, b][:])
 
         def store(b):
             nc.sync.dma_start(out[b * P : (b + 1) * P, :], win[b][:])
 
+        permute_scales()
+        turn_gate()
         gather(0, 0)
         gather(1, 0)
-        permute_scales()
-        act_m(0)
-        act_h(0)
         act_s(0)
-        gather(0, 1)
-        gather(1, 1)
-        permute_words()
+        act_m(0)
+        act_affine(0)
+        act_h(0)
         act_m(1)
         act_h(1)
+        act_s(1)
+        gather(0, 1)
+        gather(1, 1)
+        permute_words(0)
         gather(0, 2)
         gather(0, 3)
-        interleave(0)
-        interleave(1)
-        gather(1, 2)
+        pack_blocks([0], 6)
+        pack_blocks([1], 7)
+        pack_blocks([2, 3], 6)
         gather(1, 3)
-        quantize_g(0)
-        interleave(2)
-        interleave(3)
+        gather(1, 2)
+        permute_words(1)
+        quantize_g(0, 1)
+        quantize_g(1, 1)
+        quantize_g(2, 2)
         factor(0, 0)
         factor(0, 1)
         hidden(0, 0)
@@ -294,8 +356,10 @@ def tile_moe_bdx_glu_silu_kernel(
         partial(0, 1)
         da3(0, 1)
         da1(0, 1, nc.gpsimd)
-        quantize_g(1)
-        act_s(1)
+        act_affine(1)
+        pack_blocks([4, 5], 2)
+        act_m(2)
+        act_h(2)
         factor(1, 0)
         factor(1, 1)
         hidden(1, 0)
@@ -306,13 +370,15 @@ def tile_moe_bdx_glu_silu_kernel(
         partial(1, 1)
         da3(1, 1)
         da1(1, 1, nc.gpsimd)
+        quantize_g(4, 2)
         quantize_da(0)
         project(0)
-        act_m(2)
-        act_h(2)
         copy_out(0, 0)
         scatter(0, 0)
         act_s(2)
+        act_affine(2)
+        pack_blocks([6, 7], 3)
+        quantize_g(6, 2)
         factor(2, 0)
         factor(2, 1)
         hidden(2, 0)
@@ -327,21 +393,22 @@ def tile_moe_bdx_glu_silu_kernel(
         project(1)
         copy_out(0, 1)
         scatter(0, 1)
-        act_m(3)
-        act_h(3)
         copy_out(1, 0)
         scatter(1, 0)
+        act_m(3)
+        act_h(3)
         act_s(3)
+        act_affine(3)
         factor(3, 0)
         factor(3, 1)
         hidden(3, 0)
         partial(3, 0)
         da3(3, 0)
-        da1(3, 0, nc.vector)
+        da1(3, 0, nc.gpsimd)
         hidden(3, 1)
         partial(3, 1)
         da3(3, 1)
-        da1(3, 1, nc.vector)
+        da1(3, 1, nc.gpsimd)
         quantize_da(2)
         project(2)
         copy_out(1, 1)

@@ -25,10 +25,11 @@ C = 256
 S = E * C
 HALF = 512
 CHUNK = 128
-TURN_BANK = (0, 1, 2, 3, 7, 6, 0, 1)
-HIDDEN_BANK = (0, 1, 4, 5, 2, 4, 3, 5)
-HOMES = {("s", 1): "gated3", ("m", 2): "gated4", ("h", 2): "gated5", ("t", 2): "tanh_1", ("m", 3): "gated7", ("h", 3): "gated6", ("t", 3): "tanh_1", ("dx", 0, 1): "da_bf1", ("dx", 1, 1): "da_bf2", ("dx", 2, 1): "da_bf3", ("codes", 0): "h_1", ("codes", 1): "gated5", ("codes", 2): "gated6", ("codes", 3): "dx_sb20"}
-LATE_HOME = {2: "gathered3"}
+PLACES = {"tanh_1": 0, "part00": 3, "packed2": 4, "y_2": 8, "h_1": 10, "y_3": 12, "m_1": 16, "g_codes2": 16, "g_codes3": 17, "h_3": 20, "da_codes0": 20, "da_codes1": 22, "y_1": 24, "packed0": 27, "w2_perm1": 28}
+TURN_BANK = (0, 1, 2, 3, 2, 3, 6, 7)
+HIDDEN_BANK = (0, 1, 2, 3, 0, 1, 2, 3)
+DX_BANK = (4, 5, 6, 7)
+HOMES = {"gathered12": "gathered03", "tanh_2": "gated3", "tanh_3": "gated4", "m_2": "gated5", "h_2": "gated6", "m_3": "gated7", "da_codes2": "m_3"}
 
 FLOPS = 2 * S * (N * H + 2 * H * K)
 BYTES = 4 * (N * T + 2 * H * S + K * T + S) + E * P * (2 * H + 4 * K) + E * 16 * (H + 2 * K) + 2 * 16 * S // 16
@@ -41,37 +42,41 @@ def tile_moe_bdx_glu_silu_kernel(
     with ExitStack() as ctx:
         listp = ctx.enter_context(tc.tile_pool(name="listp", bufs=1))
         keep = ctx.enter_context(tc.tile_pool(name="keep", bufs=1))
-        ring = ctx.enter_context(tc.tile_pool(name="ring", bufs=3))
         psum = ctx.enter_context(tc.psum_pool(name="psum", bufs=1))
+
+        shared = ctx.enter_context(tc.tile_pool(name="shared", bufs=1))
+        homes = {}
+
+        def new_tile(name, shape, dtype):
+            if name in PLACES:
+                return shared.tile(shape, dtype, name=name, offset=PLACES[name] * 1024, align_bytes=64)
+            homes[name] = homes[HOMES[name]] if name in HOMES else name
+            return keep.tile(shape, dtype, name=name, tag=homes[name], align_bytes=64)
+
+        def bank(name, shape, number):
+            return psum.tile(shape, F32, name=name, tag=f"bank{number}")
 
         offsets = listp.tile([P, S // 16], U16, name="offsets")
 
-        planes = [keep.tile([P, T], F32, name=f"plane{t}") for t in range(PACK)]
-        early = [keep.tile([P, HALF], F32, name=f"early{t}", tag=f"gathered{t}")[:] for t in range(PACK)]
-        late = [keep.tile([P, HALF], F32, name=f"late{t}", tag=LATE_HOME.get(t, f"late{t}"))[:] for t in range(PACK)]
-        g_planes = [early, late]
-        gate_rows = keep.tile([P, P], F32, name="gate_rows")
-        gate_col = keep.tile([P, S // P], F32, name="gate_col")
-        ident = keep.tile([P, P], F32, name="ident")
-        a1_late = keep.tile([P, PACK, HALF], F32, name="a1_late")
-        a3_late = keep.tile([P, PACK, HALF], F32, name="a3_late")
-        a1_sb = [keep.tile([P, PACK, C], F32, name=f"a1_{e}")[:] for e in range(2)]
-        a3_sb = [keep.tile([P, PACK, C], F32, name=f"a3_{e}")[:] for e in range(2)]
+        planes = [new_tile(f"plane{t}", [P, T], F32) for t in range(PACK)]
+        ident = new_tile("ident", [P, P], F32)
+        a1_late = new_tile("a1_late", [P, PACK, HALF], F32)
+        a3_late = new_tile("a3_late", [P, PACK, HALF], F32)
+        a1_sb = [new_tile(f"a1_{e}", [P, PACK, C], F32)[:] for e in range(2)]
+        a3_sb = [new_tile(f"a3_{e}", [P, PACK, C], F32)[:] for e in range(2)]
         a1_sb = a1_sb + [a1_late[:, :, 0:C], a1_late[:, :, C:HALF]]
         a3_sb = a3_sb + [a3_late[:, :, 0:C], a3_late[:, :, C:HALF]]
-        h_sb, m_sb, s_sb, tanh_sb = {}, {}, {}, {}
-        w2_raw = [
-            keep.tile([P, 2, 2 * H], U8, name="w2_raw_early", align_bytes=64),
-            keep.tile([P, 2, 2 * H], U8, name="w2_raw_late", align_bytes=64),
-        ]
-        w2s_raw = keep.tile([P, E, H], U8, name="w2s_raw", align_bytes=64)
-        w2s_perm = keep.tile([P, E, H], U8, name="w2s_perm", align_bytes=64)
-        w1_sb = keep.tile([P, E, 2 * K], U8, name="w1_sb", align_bytes=64)
-        w3_sb = keep.tile([P, E, 2 * K], U8, name="w3_sb", align_bytes=64)
-        w1s = keep.tile([P, E, K], U8, name="w1s", align_bytes=64)
-        w3s = keep.tile([P, E, K], U8, name="w3s", align_bytes=64)
-        win = [keep.tile([P, T], F32, name=f"win{b}") for b in range(K // P)]
-        warm = keep.tile([P, 1], F32, name="warm")
+        w2_raw = [new_tile(f"w2_raw{h}", [P, 2, 2 * H], U8) for h in range(2)]
+        w2s_raw = new_tile("w2s_raw", [P, E, H], U8)
+        w2s_perm = new_tile("w2s_perm", [P, E, H], U8)
+        w1_sb = new_tile("w1_sb", [P, E, 2 * K], U8)
+        w3_sb = new_tile("w3_sb", [P, E, 2 * K], U8)
+        w1s = new_tile("w1s", [P, E, K], U8)
+        w3s = new_tile("w3s", [P, E, K], U8)
+        win = [new_tile(f"win{b}", [P, T], F32) for b in range(K // P)]
+        warm = new_tile("warm", [P, 1], F32)
+        gate_rows = new_tile("gate_rows", [P, P], F32)
+        gate_col = new_tile("gate_col", [P, S // P], F32)
 
         nc.gpsimd.memset(w2s_raw[:].bitcast(I32), 0)
         nc.gpsimd.memset(gate_rows[:], 0.0)
@@ -81,7 +86,7 @@ def tile_moe_bdx_glu_silu_kernel(
         nc.gpsimd.memset(w1s[:].bitcast(I32), 0)
         nc.gpsimd.memset(w3s[:].bitcast(I32), 0)
         for b in range(K // P):
-            nc.gpsimd.memset(win[b][:], 0.0)
+            nc.vector.memset(win[b][:], 0.0)
 
         def load_words(tile, dram):
             nc.sync.dma_start(tile[:].bitcast(I32), dram.bitcast(I32)[:, 0].rearrange("e p b -> p e b"))
@@ -90,8 +95,8 @@ def tile_moe_bdx_glu_silu_kernel(
             words = w2_words.bitcast(I32)[2 * h : 2 * h + 2, 0]
             nc.sync.dma_start(w2_raw[h][:].bitcast(I32), words.rearrange("e p b -> p e b"))
 
-        def load_scales(tile, dram, quadrants=range(4)):
-            for q in quadrants:
+        def load_scales(tile, dram):
+            for q in range(4):
                 nc.sync.dma_start(
                     tile[32 * q : 32 * q + 4].bitcast(I32),
                     dram.bitcast(I32)[:, 0, 4 * q : 4 * q + 4, :].rearrange("e f i -> f e i"),
@@ -104,19 +109,19 @@ def tile_moe_bdx_glu_silu_kernel(
         def load_plane(t):
             nc.sync.dma_start(planes[t][:], dy4[:, t, :])
 
-        def load_gate():
-            nc.sync.dma_start(gate_rows[0 : S // P, :], gate[0, :].rearrange("(b n) -> b n", n=P))
-
-        def turn_gate():
-            turned = psum.tile([P, P], F32, name="turned", tag="bank6")
-            nc.tensor.transpose(turned[:], gate_rows[:], ident[:])
-            nc.scalar.copy(gate_col[:], turned[:, 0 : S // P])
-
         def load_a1(e):
             nc.sync.dma_start(a1_sb[e], a1_4[:, :, e * C : (e + 1) * C])
 
         def load_a3(e):
             nc.sync.dma_start(a3_sb[e], a3_4[:, :, e * C : (e + 1) * C])
+
+        def load_gate():
+            nc.sync.dma_start(gate_rows[0 : S // P, :], gate[0, :].rearrange("(b n) -> b n", n=P))
+
+        def turn_gate():
+            turned = bank("turned", [P, P], 6)
+            nc.tensor.transpose(turned[:], gate_rows[:], ident[:])
+            nc.scalar.copy(gate_col[:], turned[:, 0 : S // P])
 
         nc.sync.dma_start(offsets[:], offs)
         load_scales(w2s_raw, w2_scales)
@@ -129,16 +134,19 @@ def tile_moe_bdx_glu_silu_kernel(
         load_plane(2)
         load_plane(3)
         load_a3(0)
+        load_a3(1)
         load_w2(1)
         nc.sync.dma_start(a1_late[:], a1_4[:, :, HALF:])
-        load_a3(1)
+        nc.sync.dma_start(a3_late[:], a3_4[:, :, HALF:])
         load_words(w1_sb, w1_words)
         load_words(w3_sb, w3_words)
         load_scales(w1s, w1_scales)
         load_scales(w3s, w3_scales)
-        nc.sync.dma_start(a3_late[:], a3_4[:, :, HALF:])
+
+        w2_perm = {}
 
         def permute_words(h):
+            w2_perm[h] = new_tile(f"w2_perm{h}", [P, 2, 2 * H], U8)
             nc.vector.tensor_copy(
                 w2_perm[h][:].bitcast(U16).rearrange("p e (t m) -> p e t m", t=PACK),
                 w2_raw[h][:].bitcast(U16).rearrange("p e (m t) -> p e t m", t=PACK),
@@ -150,27 +158,28 @@ def tile_moe_bdx_glu_silu_kernel(
                 w2s_raw[:].rearrange("p e (m t) -> p e t m", t=PACK),
             )
 
-        def gather(h, t):
-            nc.vector.tensor_copy(
-                g_planes[h][t],
-                planes[t][:].indirect(offsets[:, h * 32 : (h + 1) * 32]),
-            )
+        def walk_planes(ap):
+            return ap.rearrange("p j (c i) -> p c j i", i=4)
+
+        def walk_packed(ap):
+            return ap.rearrange("p (c i) j -> p c j i", i=4)
 
         g_bf = {}
-        w2_perm = [
-            keep.tile([P, 2, 2 * H], U8, name="w2_perm_early", align_bytes=64),
-            keep.tile([P, 2, 2 * H], U8, name="w2_perm_late", align_bytes=64),
-        ]
-        g_codes = keep.tile([P, S], U32, name="g_codes", align_bytes=64)
-        g_scales = keep.tile([P, S], U8, name="g_scales", align_bytes=64)
+        g_codes = {}
+        g_scales = new_tile("g_scales", [P, S], U8)
+
+        gathered = {}
+
+        def gather(h, t):
+            gathered[h, t] = new_tile(f"gathered{h}{t}", [P, HALF], F32)
+            nc.vector.tensor_copy(gathered[h, t][:], planes[t][:].indirect(offsets[:, h * 32 : (h + 1) * 32]))
 
         def turn_block(block):
-            e, c = divmod(block, 2)
             cols = slice((block % 4) * P, (block % 4 + 1) * P)
-            by_slot = psum.tile([P, PACK, P], F32, name=f"by_slot{block}", tag=f"bank{TURN_BANK[block]}")
+            by_slot = bank(f"by_slot{block}", [P, PACK, P], TURN_BANK[block])
             for t in range(PACK):
-                nc.tensor.transpose(by_slot[:, t, :], g_planes[e // 2][t][:, cols], ident[:])
-            gated = keep.tile([P, 2, P, 2], BF16, name=f"gated{block}", tag=f"gated{block}", align_bytes=64)
+                nc.tensor.transpose(by_slot[:, t, :], gathered[block // 4, t][:, cols], ident[:])
+            gated = new_tile(f"gated{block}", [P, 2, P, 2], BF16)
             nc.scalar.activation(
                 gated[:],
                 by_slot[:].rearrange("s (u v) p -> s u p v", u=2),
@@ -179,71 +188,48 @@ def tile_moe_bdx_glu_silu_kernel(
             )
             return gated[:].rearrange("s u p v -> s (u p v)").bitcast(F32)
 
-        def pack_blocks(blocks, bank):
-            words = psum.tile([P, len(blocks), 2, P], F32, name=f"words{blocks[0]}", tag=f"bank{bank}")
+        def pack_blocks(blocks, number):
+            words = bank(f"words{blocks[0]}", [P, len(blocks), 2, P], number)
             for n, block in enumerate(blocks):
                 pairs = turn_block(block)
                 for u in range(2):
                     nc.tensor.transpose(words[:, n, u, :], pairs[:, u * P : (u + 1) * P], ident[:])
-            packed = keep.tile([P, len(blocks), P, 2], F32, name=f"packed{blocks[0]}", tag=f"packed{blocks[0]}", align_bytes=64)
-            g_bf[blocks[0]] = packed
-            nc.scalar.copy(
-                packed[:],
-                words[:].rearrange("p c u s -> p c s u"),
-            )
+            packed = new_tile(f"packed{blocks[0]}", [P, len(blocks), P, 2], F32)
+            g_bf[blocks[0]] = packed[:].rearrange("p c s u -> p (c s u)").bitcast(BF16)
+            nc.scalar.copy(packed[:], words[:].rearrange("p c u s -> p c s u"))
 
         def quantize_g(first, count):
             slots = slice(first * P, (first + count) * P)
-            nc.vector.quantize_mx(
-                out=g_codes[:, slots].bitcast(FP8X4),
-                scales=g_scales[:, slots],
-                in_=g_bf[first][:].rearrange("p c s u -> p (c s u)").bitcast(BF16),
-            )
+            g_codes[first // 2] = new_tile(f"g_codes{first // 2}", [P, C], U32)
+            nc.vector.quantize_mx(out=g_codes[first // 2][:].bitcast(FP8X4), scales=g_scales[:, slots], in_=g_bf[first])
+
+        h_sb, m_sb, tanh_sb, y_sb = {}, {}, {}, {}
 
         def act_m(e):
-            m_sb[e] = keep.tile([P, PACK, C], F32, name=f"m_{e}", tag=HOMES.get(("m", e), f"m_{e}"), align_bytes=64)[:]
-            nc.scalar.activation(m_sb[e], a1_sb[e], ACT.Silu, scale=-1.0)
+            m_sb[e] = new_tile(f"m_{e}", [P, PACK, C], F32)
+            nc.scalar.activation(m_sb[e][:], a1_sb[e], ACT.Silu, scale=-1.0)
 
         def act_h(e):
-            h_sb[e] = keep.tile([P, PACK, C], F32, name=f"h_{e}", tag=HOMES.get(("h", e), f"h_{e}"), align_bytes=64)[:]
-            nc.scalar.activation(h_sb[e], a1_sb[e], ACT.Silu)
+            h_sb[e] = new_tile(f"h_{e}", [P, C, PACK], F32)
+            nc.scalar.activation(walk_packed(h_sb[e][:]), walk_planes(a1_sb[e]), ACT.Silu)
 
-        def act_s(e):
-            tanh_sb[e] = keep.tile([P, PACK, C], F32, name=f"tanh_{e}", tag=HOMES.get(("t", e), f"tanh_{e}"), align_bytes=64)[:]
-            nc.scalar.activation(tanh_sb[e], a1_sb[e], ACT.Tanh, scale=0.5)
-
-        def act_affine(e):
-            s_sb[e] = keep.tile([P, PACK, C], F32, name=f"s_{e}", tag=HOMES.get(("s", e), f"s_{e}"), align_bytes=64)[:]
-            nc.scalar.activation(s_sb[e], tanh_sb[e], ACT.Copy, scale=-0.5, bias=-0.5)
+        def act_tanh(e):
+            tanh_sb[e] = new_tile(f"tanh_{e}", [P, PACK, C], F32)
+            nc.scalar.activation(tanh_sb[e][:], a1_sb[e], ACT.Tanh, scale=-0.5)
 
         def chunk_cols(c):
             return slice(c * CHUNK, (c + 1) * CHUNK)
 
-        y_sb = a3_sb
+        def factor(e):
+            y_sb[e] = new_tile(f"y_{e}", [P, PACK, C], F32)
+            nc.vector.scalar_tensor_tensor(y_sb[e][:], tanh_sb[e][:], 1.0, a3_sb[e], ALU.subtract, ALU.mult)
 
-        def factor_whole(e, engine=nc.gpsimd):
-            engine.tensor_tensor(y_sb[e], a3_sb[e], s_sb[e], ALU.mult)
-
-        def factor(e, c):
-            cols = chunk_cols(c)
-            nc.gpsimd.tensor_tensor(y_sb[e][:, :, cols], a3_sb[e][:, :, cols], s_sb[e][:, :, cols], ALU.mult)
-
-        da_bf = [keep.tile([P, 2, C, PACK], BF16, name=f"da_bf{e}", tag=f"da_bf{e}", align_bytes=64) for e in range(E)]
-        da_codes = {}
-        da_scales = [ring.tile([P, 2, C], U8, name=f"da_scales{e}", tag="da_scales", bufs=4, align_bytes=64) for e in range(E)]
-        dx_sb = {}
-
-        def walk_planes(ap):
-            return ap.rearrange("p j (c i) -> p c j i", i=4)
-
-        def walk_packed(ap):
-            return ap.rearrange("p (c i) j -> p c j i", i=4)
-
-        dh_ps = {}
-        parts = {}
+        da_bf = [new_tile(f"da_bf{e}", [P, 2, C, PACK], BF16) for e in range(E)]
+        da_scales = [new_tile(f"da_scales{e}", [P, 2, C], U8) for e in range(E)]
+        da_codes, dh_ps, parts, dx_ps, dx_sb = {}, {}, {}, {}, {}
 
         def hidden(e, c):
-            dh = psum.tile([P, PACK, CHUNK], F32, name=f"dh{e}{c}", tag=f"bank{HIDDEN_BANK[2 * e + c]}")
+            dh = bank(f"dh{e}{c}", [P, PACK, CHUNK], HIDDEN_BANK[2 * e + c])
             dh_ps[e, c] = dh
             slots = slice(e * C + c * CHUNK, e * C + (c + 1) * CHUNK)
             for t in range(PACK):
@@ -251,50 +237,51 @@ def tile_moe_bdx_glu_silu_kernel(
                     out=dh[:, t, :],
                     lhsT=w2_perm[e // 2][:, e % 2, 2 * P * t : 2 * P * (t + 1)].bitcast(FP4X4),
                     lhsT_scale=w2s_perm[:, e, P * t : P * (t + 1)],
-                    rhs=g_codes[:, slots].bitcast(FP8X4),
+                    rhs=g_codes[e][:, chunk_cols(c)].bitcast(FP8X4),
                     rhs_scale=g_scales[:, slots],
                     start=True,
                     stop=True,
                 )
 
         def partial(e, c):
-            part = keep.tile([P, PACK, CHUNK], F32, name=f"part{e}{c}", tag=f"part{e}{c}", align_bytes=64)
-            parts[e, c] = part
+            parts[e, c] = new_tile(f"part{e}{c}", [P, PACK, CHUNK], F32)
             nc.vector.scalar_tensor_tensor(
-                part[:], m_sb[e][:, :, chunk_cols(c)], 1.0, dh_ps[e, c][:], ALU.subtract, ALU.mult
+                parts[e, c][:], m_sb[e][:, :, chunk_cols(c)], 1.0, dh_ps[e, c][:], ALU.subtract, ALU.mult
             )
 
         def da3(e, c):
             cols = chunk_cols(c)
-            nc.vector.tensor_tensor(
-                walk_packed(da_bf[e][:, 1, cols, :]),
-                walk_planes(dh_ps[e, c][:]),
-                walk_planes(h_sb[e][:, :, cols]),
+            nc.vector.scalar_tensor_tensor(
+                da_bf[e][:, 1, cols, :],
+                dh_ps[e, c][:].rearrange("p j n -> p n j"),
+                2.0,
+                h_sb[e][:, cols, :],
+                ALU.mult,
                 ALU.mult,
             )
 
         def da1(e, c, engine):
-            cols = chunk_cols(c)
-            engine.tensor_tensor(
-                walk_packed(da_bf[e][:, 0, cols, :]),
-                walk_planes(parts[e, c][:]),
-                walk_planes(y_sb[e][:, :, cols]),
-                ALU.mult,
-            )
+            pieces = 1 if engine is nc.gpsimd else 1
+            for n in range(pieces):
+                inner = slice(n * CHUNK // pieces, (n + 1) * CHUNK // pieces)
+                cols = slice(c * CHUNK + inner.start, c * CHUNK + inner.stop)
+                engine.tensor_tensor(
+                    walk_packed(da_bf[e][:, 0, cols, :]),
+                    walk_planes(parts[e, c][:, :, inner]),
+                    walk_planes(y_sb[e][:, :, cols]),
+                    ALU.mult,
+                )
 
         def quantize_da(e):
-            home = HOMES.get(("codes", e), f"da_codes{e}")
-            da_codes[e] = keep.tile([P, 2, C], U32, name=f"da_codes{e}", tag=home, align_bytes=64)
+            da_codes[e] = new_tile(f"da_codes{e}", [P, 2, C], U32)
             nc.vector.quantize_mx(
                 out=da_codes[e][:].rearrange("p i n -> p (i n)").bitcast(FP8X4),
                 scales=da_scales[e][:].rearrange("p i n -> p (i n)"),
                 in_=da_bf[e][:].rearrange("p i n j -> p (i n j)"),
             )
 
-        dx_ps = {}
-
         def project(e):
-            dx = psum.tile([P, 2, C], F32, name=f"dx{e}", tag=f"bank{6 + e % 2}")
+            dx = bank(f"dx{e}", [P, 2, C], DX_BANK[e])
             for b in range(2):
                 for c in range(2):
                     cols = chunk_cols(c)
@@ -310,13 +297,12 @@ def tile_moe_bdx_glu_silu_kernel(
                         )
             dx_ps[e] = dx
 
-        def copy_out(e, b):
-            home = HOMES.get(("dx", e, b), f"dx_sb{e}{b}")
-            dx_sb[e, b] = keep.tile([P, C], F32, name=f"dx_sb{e}{b}", tag=home, align_bytes=64)
-            nc.scalar.copy(dx_sb[e, b][:], dx_ps[e][:, b, :])
+        def copy_out(e):
+            dx_sb[e] = new_tile(f"dx_sb{e}", [P, 2, C], F32)
+            nc.scalar.activation(dx_sb[e][:], dx_ps[e][:], ACT.Copy, scale=0.5)
 
         def scatter(e, b):
-            nc.vector.tensor_copy(win[b][:].indirect(offsets[:, e * 16 : (e + 1) * 16]), dx_sb[e, b][:])
+            nc.vector.tensor_copy(win[b][:].indirect(offsets[:, e * 16 : (e + 1) * 16]), dx_sb[e][:, b, :])
 
         def store(b):
             nc.sync.dma_start(out[b * P : (b + 1) * P, :], win[b][:])
@@ -325,29 +311,28 @@ def tile_moe_bdx_glu_silu_kernel(
         turn_gate()
         gather(0, 0)
         gather(1, 0)
-        act_s(0)
+        act_tanh(0)
         act_m(0)
-        act_affine(0)
         act_h(0)
+        act_tanh(1)
         act_m(1)
         act_h(1)
-        act_s(1)
         gather(0, 1)
         gather(1, 1)
         permute_words(0)
         gather(0, 2)
         gather(0, 3)
-        pack_blocks([0], 6)
-        pack_blocks([1], 7)
-        pack_blocks([2, 3], 6)
+        pack_blocks([0, 1], 6)
+        pack_blocks([2, 3], 7)
         gather(1, 3)
         gather(1, 2)
+        factor(0)
+        quantize_g(0, 2)
+        factor(1)
         permute_words(1)
-        quantize_g(0, 1)
-        quantize_g(1, 1)
         quantize_g(2, 2)
-        factor(0, 0)
-        factor(0, 1)
+        pack_blocks([4, 5], 4)
+        pack_blocks([6, 7], 5)
         hidden(0, 0)
         partial(0, 0)
         da3(0, 0)
@@ -356,12 +341,6 @@ def tile_moe_bdx_glu_silu_kernel(
         partial(0, 1)
         da3(0, 1)
         da1(0, 1, nc.gpsimd)
-        act_affine(1)
-        pack_blocks([4, 5], 2)
-        act_m(2)
-        act_h(2)
-        factor(1, 0)
-        factor(1, 1)
         hidden(1, 0)
         partial(1, 0)
         da3(1, 0)
@@ -371,16 +350,13 @@ def tile_moe_bdx_glu_silu_kernel(
         da3(1, 1)
         da1(1, 1, nc.gpsimd)
         quantize_g(4, 2)
-        quantize_da(0)
-        project(0)
-        copy_out(0, 0)
-        scatter(0, 0)
-        act_s(2)
-        act_affine(2)
-        pack_blocks([6, 7], 3)
         quantize_g(6, 2)
-        factor(2, 0)
-        factor(2, 1)
+        act_tanh(2)
+        act_tanh(3)
+        factor(2)
+        factor(3)
+        act_m(2)
+        act_h(2)
         hidden(2, 0)
         partial(2, 0)
         da3(2, 0)
@@ -389,39 +365,35 @@ def tile_moe_bdx_glu_silu_kernel(
         partial(2, 1)
         da3(2, 1)
         da1(2, 1, nc.gpsimd)
-        quantize_da(1)
-        project(1)
-        copy_out(0, 1)
-        scatter(0, 1)
-        copy_out(1, 0)
-        scatter(1, 0)
         act_m(3)
         act_h(3)
-        act_s(3)
-        act_affine(3)
-        factor(3, 0)
-        factor(3, 1)
         hidden(3, 0)
         partial(3, 0)
         da3(3, 0)
-        da1(3, 0, nc.gpsimd)
         hidden(3, 1)
         partial(3, 1)
         da3(3, 1)
-        da1(3, 1, nc.gpsimd)
+        da1(3, 0, nc.vector)
+        da1(3, 1, nc.vector)
+        quantize_da(0)
+        project(0)
+        copy_out(0)
+        quantize_da(1)
+        project(1)
+        copy_out(1)
         quantize_da(2)
         project(2)
-        copy_out(1, 1)
-        scatter(1, 1)
-        copy_out(2, 0)
-        scatter(2, 0)
+        copy_out(2)
         quantize_da(3)
         project(3)
-        copy_out(2, 1)
-        scatter(2, 1)
-        copy_out(3, 0)
-        copy_out(3, 1)
+        copy_out(3)
+        scatter(0, 0)
+        scatter(1, 0)
+        scatter(2, 0)
         scatter(3, 0)
         store(0)
+        scatter(0, 1)
+        scatter(1, 1)
+        scatter(2, 1)
         scatter(3, 1)
         store(1)

@@ -23,16 +23,42 @@ T = 1280
 E = 4
 C = 256
 S = E * C
-HALF = 512
-CHUNK = 128
-PLACES = {"tanh_1": 0, "part00": 3, "packed2": 4, "y_2": 8, "h_1": 10, "y_3": 12, "m_1": 16, "g_codes2": 16, "g_codes3": 17, "h_3": 20, "da_codes0": 20, "da_codes1": 22, "y_1": 24, "packed0": 27, "w2_perm1": 28}
-TURN_BANK = (0, 1, 2, 3, 2, 3, 6, 7)
-HIDDEN_BANK = (0, 1, 2, 3, 0, 1, 2, 3)
-DX_BANK = (4, 5, 6, 7)
-HOMES = {"gathered12": "gathered03", "tanh_2": "gated3", "tanh_3": "gated4", "m_2": "gated5", "h_2": "gated6", "m_3": "gated7", "da_codes2": "m_3"}
+HALF = S // 2
+BLOCKS = S // P
+LIST_ROWS = 16
+KIB = 1024
 
 FLOPS = 2 * S * (N * H + 2 * H * K)
 BYTES = 4 * (N * T + 2 * H * S + K * T + S) + E * P * (2 * H + 4 * K) + E * 16 * (H + 2 * K) + 2 * 16 * S // 16
+
+SUCCEEDS = {
+    "gathered12": "gathered03",
+    "tanh_3": "gated3",
+    "tanh_2": "gated4",
+    "neg_3": "gated5",
+    "neg_2": "gated6",
+    "silu_2": "gated7",
+    "da_codes2": "da_bf0",
+}
+PLACES = {
+    "tanh_1": 0,
+    "part00": 3,
+    "factor_2": 8,
+    "silu_1": 10,
+    "factor_3": 12,
+    "neg_1": 16,
+    "g_codes2": 16,
+    "g_codes3": 17,
+    "silu_3": 20,
+    "da_codes0": 20,
+    "da_codes1": 22,
+    "factor_1": 24,
+    "packed0": 27,
+}
+TURN_BANK = (0, 1, 2, 3, 2, 3, 6, 7)
+WORDS_BANK = (6, 7, 4, 5)
+GATE_BANK = 6
+DH_BANKS = 4
 
 
 def tile_moe_bdx_glu_silu_kernel(
@@ -43,20 +69,20 @@ def tile_moe_bdx_glu_silu_kernel(
         listp = ctx.enter_context(tc.tile_pool(name="listp", bufs=1))
         keep = ctx.enter_context(tc.tile_pool(name="keep", bufs=1))
         psum = ctx.enter_context(tc.psum_pool(name="psum", bufs=1))
-
         shared = ctx.enter_context(tc.tile_pool(name="shared", bufs=1))
-        homes = {}
 
         def new_tile(name, shape, dtype):
             if name in PLACES:
-                return shared.tile(shape, dtype, name=name, offset=PLACES[name] * 1024, align_bytes=64)
-            homes[name] = homes[HOMES[name]] if name in HOMES else name
-            return keep.tile(shape, dtype, name=name, tag=homes[name], align_bytes=64)
+                return shared.tile(shape, dtype, name=name, offset=PLACES[name] * KIB, align_bytes=64)
+            return keep.tile(shape, dtype, name=name, tag=SUCCEEDS.get(name, name), align_bytes=64)
 
         def bank(name, shape, number):
             return psum.tile(shape, F32, name=name, tag=f"bank{number}")
 
-        offsets = listp.tile([P, S // 16], U16, name="offsets")
+        offsets = listp.tile([P, S // LIST_ROWS], U16, name="offsets")
+
+        def entries(first, count):
+            return offsets[:, first // LIST_ROWS : (first + count) // LIST_ROWS]
 
         planes = [new_tile(f"plane{t}", [P, T], F32) for t in range(PACK)]
         ident = new_tile("ident", [P, P], F32)
@@ -66,7 +92,7 @@ def tile_moe_bdx_glu_silu_kernel(
         a3_sb = [new_tile(f"a3_{e}", [P, PACK, C], F32)[:] for e in range(2)]
         a1_sb = a1_sb + [a1_late[:, :, 0:C], a1_late[:, :, C:HALF]]
         a3_sb = a3_sb + [a3_late[:, :, 0:C], a3_late[:, :, C:HALF]]
-        w2_raw = [new_tile(f"w2_raw{h}", [P, 2, 2 * H], U8) for h in range(2)]
+        w2_raw = new_tile("w2_raw", [P, E, 2 * H], U8)
         w2s_raw = new_tile("w2s_raw", [P, E, H], U8)
         w2s_perm = new_tile("w2s_perm", [P, E, H], U8)
         w1_sb = new_tile("w1_sb", [P, E, 2 * K], U8)
@@ -74,15 +100,12 @@ def tile_moe_bdx_glu_silu_kernel(
         w1s = new_tile("w1s", [P, E, K], U8)
         w3s = new_tile("w3s", [P, E, K], U8)
         win = [new_tile(f"win{b}", [P, T], F32) for b in range(K // P)]
-        warm = new_tile("warm", [P, 1], F32)
         gate_rows = new_tile("gate_rows", [P, P], F32)
-        gate_col = new_tile("gate_col", [P, S // P], F32)
+        gate_col = new_tile("gate_col", [P, BLOCKS], F32)
 
         nc.gpsimd.memset(w2s_raw[:].bitcast(I32), 0)
         nc.gpsimd.memset(gate_rows[:], 0.0)
         make_identity(nc, ident[:])
-        nc.vector.memset(warm[:], 0.0)
-        nc.scalar.activation(warm[:], warm[:], ACT.Silu)
         nc.gpsimd.memset(w1s[:].bitcast(I32), 0)
         nc.gpsimd.memset(w3s[:].bitcast(I32), 0)
         for b in range(K // P):
@@ -90,10 +113,6 @@ def tile_moe_bdx_glu_silu_kernel(
 
         def load_words(tile, dram):
             nc.sync.dma_start(tile[:].bitcast(I32), dram.bitcast(I32)[:, 0].rearrange("e p b -> p e b"))
-
-        def load_w2(h):
-            words = w2_words.bitcast(I32)[2 * h : 2 * h + 2, 0]
-            nc.sync.dma_start(w2_raw[h][:].bitcast(I32), words.rearrange("e p b -> p e b"))
 
         def load_scales(tile, dram):
             for q in range(4):
@@ -109,33 +128,21 @@ def tile_moe_bdx_glu_silu_kernel(
         def load_plane(t):
             nc.sync.dma_start(planes[t][:], dy4[:, t, :])
 
-        def load_a1(e):
-            nc.sync.dma_start(a1_sb[e], a1_4[:, :, e * C : (e + 1) * C])
-
-        def load_a3(e):
-            nc.sync.dma_start(a3_sb[e], a3_4[:, :, e * C : (e + 1) * C])
-
-        def load_gate():
-            nc.sync.dma_start(gate_rows[0 : S // P, :], gate[0, :].rearrange("(b n) -> b n", n=P))
-
-        def turn_gate():
-            turned = bank("turned", [P, P], 6)
-            nc.tensor.transpose(turned[:], gate_rows[:], ident[:])
-            nc.scalar.copy(gate_col[:], turned[:, 0 : S // P])
+        def load_expert(tiles, dram, e):
+            nc.sync.dma_start(tiles[e], dram[:, :, e * C : (e + 1) * C])
 
         nc.sync.dma_start(offsets[:], offs)
         load_scales(w2s_raw, w2_scales)
         load_plane(0)
-        load_gate()
-        load_a1(0)
+        nc.sync.dma_start(gate_rows[0:BLOCKS, :], gate[0, :].rearrange("(b n) -> b n", n=P))
+        load_expert(a1_sb, a1_4, 0)
         load_plane(1)
-        load_a1(1)
-        load_w2(0)
+        load_expert(a1_sb, a1_4, 1)
         load_plane(2)
         load_plane(3)
-        load_a3(0)
-        load_a3(1)
-        load_w2(1)
+        load_words(w2_raw, w2_words)
+        load_expert(a3_sb, a3_4, 0)
+        load_expert(a3_sb, a3_4, 1)
         nc.sync.dma_start(a1_late[:], a1_4[:, :, HALF:])
         nc.sync.dma_start(a3_late[:], a3_4[:, :, HALF:])
         load_words(w1_sb, w1_words)
@@ -143,13 +150,12 @@ def tile_moe_bdx_glu_silu_kernel(
         load_scales(w1s, w1_scales)
         load_scales(w3s, w3_scales)
 
-        w2_perm = {}
+        w2_perm = new_tile("w2_perm", [P, E, 2 * H], U8)
 
-        def permute_words(h):
-            w2_perm[h] = new_tile(f"w2_perm{h}", [P, 2, 2 * H], U8)
+        def permute_words():
             nc.vector.tensor_copy(
-                w2_perm[h][:].bitcast(U16).rearrange("p e (t m) -> p e t m", t=PACK),
-                w2_raw[h][:].bitcast(U16).rearrange("p e (m t) -> p e t m", t=PACK),
+                w2_perm[:].bitcast(U16).rearrange("p e (t m) -> p e t m", t=PACK),
+                w2_raw[:].bitcast(U16).rearrange("p e (m t) -> p e t m", t=PACK),
             )
 
         def permute_scales():
@@ -158,27 +164,28 @@ def tile_moe_bdx_glu_silu_kernel(
                 w2s_raw[:].rearrange("p e (m t) -> p e t m", t=PACK),
             )
 
-        def walk_planes(ap):
+        def walk_planar(ap):
             return ap.rearrange("p j (c i) -> p c j i", i=4)
 
         def walk_packed(ap):
             return ap.rearrange("p (c i) j -> p c j i", i=4)
 
-        g_bf = {}
-        g_codes = {}
-        g_scales = new_tile("g_scales", [P, S], U8)
+        def turn_gate():
+            turned = bank("turned", [P, P], GATE_BANK)
+            nc.tensor.transpose(turned[:], gate_rows[:], ident[:])
+            nc.scalar.copy(gate_col[:], turned[:, 0:BLOCKS])
 
         gathered = {}
 
         def gather(h, t):
             gathered[h, t] = new_tile(f"gathered{h}{t}", [P, HALF], F32)
-            nc.vector.tensor_copy(gathered[h, t][:], planes[t][:].indirect(offsets[:, h * 32 : (h + 1) * 32]))
+            nc.vector.tensor_copy(gathered[h, t][:], planes[t][:].indirect(entries(h * HALF, HALF)))
 
-        def turn_block(block):
-            cols = slice((block % 4) * P, (block % 4 + 1) * P)
+        def gate_block(block):
+            h, first = divmod(block * P, HALF)
             by_slot = bank(f"by_slot{block}", [P, PACK, P], TURN_BANK[block])
             for t in range(PACK):
-                nc.tensor.transpose(by_slot[:, t, :], gathered[block // 4, t][:, cols], ident[:])
+                nc.tensor.transpose(by_slot[:, t, :], gathered[h, t][:, first : first + P], ident[:])
             gated = new_tile(f"gated{block}", [P, 2, P, 2], BF16)
             nc.scalar.activation(
                 gated[:],
@@ -188,212 +195,173 @@ def tile_moe_bdx_glu_silu_kernel(
             )
             return gated[:].rearrange("s u p v -> s (u p v)").bitcast(F32)
 
-        def pack_blocks(blocks, number):
-            words = bank(f"words{blocks[0]}", [P, len(blocks), 2, P], number)
-            for n, block in enumerate(blocks):
-                pairs = turn_block(block)
+        g_bf, g_codes = {}, {}
+        g_scales = new_tile("g_scales", [P, S], U8)
+
+        def pack_g(e):
+            words = bank(f"words{e}", [P, 2, 2, P], WORDS_BANK[e])
+            for c in range(2):
+                pairs = gate_block(2 * e + c)
                 for u in range(2):
-                    nc.tensor.transpose(words[:, n, u, :], pairs[:, u * P : (u + 1) * P], ident[:])
-            packed = new_tile(f"packed{blocks[0]}", [P, len(blocks), P, 2], F32)
-            g_bf[blocks[0]] = packed[:].rearrange("p c s u -> p (c s u)").bitcast(BF16)
+                    nc.tensor.transpose(words[:, c, u, :], pairs[:, u * P : (u + 1) * P], ident[:])
+            packed = new_tile(f"packed{e}", [P, 2, P, 2], F32)
+            g_bf[e] = packed[:].rearrange("p c s u -> p (c s u)").bitcast(BF16)
             nc.scalar.copy(packed[:], words[:].rearrange("p c u s -> p c s u"))
 
-        def quantize_g(first, count):
-            slots = slice(first * P, (first + count) * P)
-            g_codes[first // 2] = new_tile(f"g_codes{first // 2}", [P, C], U32)
-            nc.vector.quantize_mx(out=g_codes[first // 2][:].bitcast(FP8X4), scales=g_scales[:, slots], in_=g_bf[first])
+        def quantize_g(e):
+            g_codes[e] = new_tile(f"g_codes{e}", [P, C], U32)
+            nc.vector.quantize_mx(
+                out=g_codes[e][:].bitcast(FP8X4), scales=g_scales[:, e * C : (e + 1) * C], in_=g_bf[e]
+            )
 
-        h_sb, m_sb, tanh_sb, y_sb = {}, {}, {}, {}
+        neg_sb, silu_sb, tanh_sb, factor_sb = {}, {}, {}, {}
 
-        def act_m(e):
-            m_sb[e] = new_tile(f"m_{e}", [P, PACK, C], F32)
-            nc.scalar.activation(m_sb[e][:], a1_sb[e], ACT.Silu, scale=-1.0)
+        def act_neg(e):
+            neg_sb[e] = new_tile(f"neg_{e}", [P, PACK, C], F32)
+            nc.scalar.activation(neg_sb[e][:], a1_sb[e], ACT.Silu, scale=-1.0)
 
-        def act_h(e):
-            h_sb[e] = new_tile(f"h_{e}", [P, C, PACK], F32)
-            nc.scalar.activation(walk_packed(h_sb[e][:]), walk_planes(a1_sb[e]), ACT.Silu)
+        def act_silu(e):
+            silu_sb[e] = new_tile(f"silu_{e}", [P, C, PACK], F32)
+            nc.scalar.activation(walk_packed(silu_sb[e][:]), walk_planar(a1_sb[e]), ACT.Silu)
 
         def act_tanh(e):
             tanh_sb[e] = new_tile(f"tanh_{e}", [P, PACK, C], F32)
             nc.scalar.activation(tanh_sb[e][:], a1_sb[e], ACT.Tanh, scale=-0.5)
 
-        def chunk_cols(c):
-            return slice(c * CHUNK, (c + 1) * CHUNK)
+        def block_cols(c):
+            return slice(c * P, (c + 1) * P)
 
-        def factor(e):
-            y_sb[e] = new_tile(f"y_{e}", [P, PACK, C], F32)
-            nc.vector.scalar_tensor_tensor(y_sb[e][:], tanh_sb[e][:], 1.0, a3_sb[e], ALU.subtract, ALU.mult)
+        def make_factor(e):
+            factor_sb[e] = new_tile(f"factor_{e}", [P, PACK, C], F32)
+            nc.vector.scalar_tensor_tensor(factor_sb[e][:], tanh_sb[e][:], 1.0, a3_sb[e], ALU.subtract, ALU.mult)
 
         da_bf = [new_tile(f"da_bf{e}", [P, 2, C, PACK], BF16) for e in range(E)]
         da_scales = [new_tile(f"da_scales{e}", [P, 2, C], U8) for e in range(E)]
-        da_codes, dh_ps, parts, dx_ps, dx_sb = {}, {}, {}, {}, {}
+        da_codes, dx_sb = {}, {}
 
         def hidden(e, c):
-            dh = bank(f"dh{e}{c}", [P, PACK, CHUNK], HIDDEN_BANK[2 * e + c])
-            dh_ps[e, c] = dh
-            slots = slice(e * C + c * CHUNK, e * C + (c + 1) * CHUNK)
+            dh = bank(f"dh{e}{c}", [P, PACK, P], (2 * e + c) % DH_BANKS)
             for t in range(PACK):
                 nc.tensor.matmul_mx(
                     out=dh[:, t, :],
-                    lhsT=w2_perm[e // 2][:, e % 2, 2 * P * t : 2 * P * (t + 1)].bitcast(FP4X4),
+                    lhsT=w2_perm[:, e, 2 * P * t : 2 * P * (t + 1)].bitcast(FP4X4),
                     lhsT_scale=w2s_perm[:, e, P * t : P * (t + 1)],
-                    rhs=g_codes[e][:, chunk_cols(c)].bitcast(FP8X4),
-                    rhs_scale=g_scales[:, slots],
+                    rhs=g_codes[e][:, block_cols(c)].bitcast(FP8X4),
+                    rhs_scale=g_scales[:, e * C + c * P : e * C + (c + 1) * P],
                     start=True,
                     stop=True,
                 )
+            return dh
 
-        def partial(e, c):
-            parts[e, c] = new_tile(f"part{e}{c}", [P, PACK, CHUNK], F32)
+        def make_da3(e, c, dh):
             nc.vector.scalar_tensor_tensor(
-                parts[e, c][:], m_sb[e][:, :, chunk_cols(c)], 1.0, dh_ps[e, c][:], ALU.subtract, ALU.mult
-            )
-
-        def da3(e, c):
-            cols = chunk_cols(c)
-            nc.vector.scalar_tensor_tensor(
-                da_bf[e][:, 1, cols, :],
-                dh_ps[e, c][:].rearrange("p j n -> p n j"),
+                da_bf[e][:, 1, block_cols(c), :],
+                dh[:].rearrange("p j n -> p n j"),
                 2.0,
-                h_sb[e][:, cols, :],
+                silu_sb[e][:, block_cols(c), :],
                 ALU.mult,
                 ALU.mult,
             )
 
-        def da1(e, c, engine):
-            pieces = 1 if engine is nc.gpsimd else 1
-            for n in range(pieces):
-                inner = slice(n * CHUNK // pieces, (n + 1) * CHUNK // pieces)
-                cols = slice(c * CHUNK + inner.start, c * CHUNK + inner.stop)
-                engine.tensor_tensor(
-                    walk_packed(da_bf[e][:, 0, cols, :]),
-                    walk_planes(parts[e, c][:, :, inner]),
-                    walk_planes(y_sb[e][:, :, cols]),
+        def products_shared(e):
+            for c in range(2):
+                dh = hidden(e, c)
+                part = new_tile(f"part{e}{c}", [P, PACK, P], F32)
+                nc.vector.scalar_tensor_tensor(
+                    part[:], neg_sb[e][:, :, block_cols(c)], 1.0, dh[:], ALU.subtract, ALU.mult
+                )
+                make_da3(e, c, dh)
+                nc.gpsimd.tensor_tensor(
+                    walk_packed(da_bf[e][:, 0, block_cols(c), :]),
+                    walk_planar(part[:]),
+                    walk_planar(factor_sb[e][:, :, block_cols(c)]),
                     ALU.mult,
                 )
 
-        def quantize_da(e):
+        def make_whole_factor(e):
+            whole = new_tile(f"whole_{e}", [P, PACK, C], F32)
+            nc.vector.scalar_tensor_tensor(whole[:], neg_sb[e][:], 1.0, factor_sb[e][:], ALU.subtract, ALU.mult)
+            return whole
+
+        def products_on_vector(e, whole):
+            for c in range(2):
+                dh = hidden(e, c)
+                nc.vector.tensor_tensor(
+                    walk_packed(da_bf[e][:, 0, block_cols(c), :]),
+                    walk_planar(dh[:]),
+                    walk_planar(whole[:, :, block_cols(c)]),
+                    ALU.mult,
+                )
+                make_da3(e, c, dh)
+
+        def project(e):
             da_codes[e] = new_tile(f"da_codes{e}", [P, 2, C], U32)
             nc.vector.quantize_mx(
                 out=da_codes[e][:].rearrange("p i n -> p (i n)").bitcast(FP8X4),
                 scales=da_scales[e][:].rearrange("p i n -> p (i n)"),
                 in_=da_bf[e][:].rearrange("p i n j -> p (i n j)"),
             )
-
-        def project(e):
-            dx = bank(f"dx{e}", [P, 2, C], DX_BANK[e])
-            for b in range(2):
+            dx = bank(f"dx{e}", [P, K // P, C], DH_BANKS + e)
+            for b in range(K // P):
                 for c in range(2):
-                    cols = chunk_cols(c)
                     for i, (w, ws) in enumerate(((w1_sb, w1s), (w3_sb, w3s))):
                         nc.tensor.matmul_mx(
-                            out=dx[:, b, cols],
+                            out=dx[:, b, block_cols(c)],
                             lhsT=w[:, e, 2 * P * b : 2 * P * (b + 1)].bitcast(FP4X4),
                             lhsT_scale=ws[:, e, P * b : P * (b + 1)],
-                            rhs=da_codes[e][:, i, cols].bitcast(FP8X4),
-                            rhs_scale=da_scales[e][:, i, cols],
+                            rhs=da_codes[e][:, i, block_cols(c)].bitcast(FP8X4),
+                            rhs_scale=da_scales[e][:, i, block_cols(c)],
                             start=(i == 0),
                             stop=(i == 1),
                         )
-            dx_ps[e] = dx
-
-        def copy_out(e):
-            dx_sb[e] = new_tile(f"dx_sb{e}", [P, 2, C], F32)
-            nc.scalar.activation(dx_sb[e][:], dx_ps[e][:], ACT.Copy, scale=0.5)
-
-        def scatter(e, b):
-            nc.vector.tensor_copy(win[b][:].indirect(offsets[:, e * 16 : (e + 1) * 16]), dx_sb[e][:, b, :])
-
-        def store(b):
-            nc.sync.dma_start(out[b * P : (b + 1) * P, :], win[b][:])
+            dx_sb[e] = new_tile(f"dx_sb{e}", [P, K // P, C], F32)
+            nc.scalar.activation(dx_sb[e][:], dx[:], ACT.Copy, scale=0.5)
 
         permute_scales()
         turn_gate()
         gather(0, 0)
         gather(1, 0)
+        act_neg(0)
+        act_silu(0)
         act_tanh(0)
-        act_m(0)
-        act_h(0)
         act_tanh(1)
-        act_m(1)
-        act_h(1)
+        act_neg(1)
+        act_silu(1)
         gather(0, 1)
         gather(1, 1)
-        permute_words(0)
         gather(0, 2)
         gather(0, 3)
-        pack_blocks([0, 1], 6)
-        pack_blocks([2, 3], 7)
+        pack_g(0)
+        pack_g(1)
         gather(1, 3)
         gather(1, 2)
-        factor(0)
-        quantize_g(0, 2)
-        factor(1)
-        permute_words(1)
-        quantize_g(2, 2)
-        pack_blocks([4, 5], 4)
-        pack_blocks([6, 7], 5)
-        hidden(0, 0)
-        partial(0, 0)
-        da3(0, 0)
-        da1(0, 0, nc.gpsimd)
-        hidden(0, 1)
-        partial(0, 1)
-        da3(0, 1)
-        da1(0, 1, nc.gpsimd)
-        hidden(1, 0)
-        partial(1, 0)
-        da3(1, 0)
-        da1(1, 0, nc.gpsimd)
-        hidden(1, 1)
-        partial(1, 1)
-        da3(1, 1)
-        da1(1, 1, nc.gpsimd)
-        quantize_g(4, 2)
-        quantize_g(6, 2)
-        act_tanh(2)
+        permute_words()
+        for e in range(2):
+            make_factor(e)
+            quantize_g(e)
+        pack_g(2)
+        pack_g(3)
+
+        products_shared(0)
+        products_shared(1)
+        quantize_g(2)
+        quantize_g(3)
         act_tanh(3)
-        factor(2)
-        factor(3)
-        act_m(2)
-        act_h(2)
-        hidden(2, 0)
-        partial(2, 0)
-        da3(2, 0)
-        da1(2, 0, nc.gpsimd)
-        hidden(2, 1)
-        partial(2, 1)
-        da3(2, 1)
-        da1(2, 1, nc.gpsimd)
-        act_m(3)
-        act_h(3)
-        hidden(3, 0)
-        partial(3, 0)
-        da3(3, 0)
-        hidden(3, 1)
-        partial(3, 1)
-        da3(3, 1)
-        da1(3, 0, nc.vector)
-        da1(3, 1, nc.vector)
-        quantize_da(0)
-        project(0)
-        copy_out(0)
-        quantize_da(1)
-        project(1)
-        copy_out(1)
-        quantize_da(2)
-        project(2)
-        copy_out(2)
-        quantize_da(3)
-        project(3)
-        copy_out(3)
-        scatter(0, 0)
-        scatter(1, 0)
-        scatter(2, 0)
-        scatter(3, 0)
-        store(0)
-        scatter(0, 1)
-        scatter(1, 1)
-        scatter(2, 1)
-        scatter(3, 1)
-        store(1)
+        act_tanh(2)
+        act_neg(3)
+        make_factor(3)
+        make_factor(2)
+        whole = make_whole_factor(3)
+        act_neg(2)
+        act_silu(2)
+        products_shared(2)
+        act_silu(3)
+        products_on_vector(3, whole)
+
+        for e in range(E):
+            project(e)
+        for e in range(E):
+            for b in range(K // P):
+                nc.vector.tensor_copy(win[b][:].indirect(entries(e * C, C)), dx_sb[e][:, b, :])
+                if e == E - 1:
+                    nc.sync.dma_start(out[b * P : (b + 1) * P, :], win[b][:])

@@ -33,32 +33,37 @@ BYTES = 4 * (N * T + 2 * H * S + K * T + S) + E * P * (2 * H + 4 * K) + E * 16 *
 
 SUCCEEDS = {
     "gathered12": "gathered03",
-    "tanh_3": "gated3",
-    "tanh_2": "gated4",
-    "neg_3": "gated5",
-    "neg_2": "gated6",
-    "silu_2": "gated7",
-    "da_codes2": "da_bf0",
+    "late_factor4": "neg_1",
+    "late_factor6": "packed_late",
+    "dx_sb0": "late_neg7",
+    "late_tanh4": "plane0",
+    "late_tanh5": "plane1",
+    "late_tanh6": "plane2",
+    "late_tanh7": "plane3",
 }
 PLACES = {
     "tanh_1": 0,
     "part00": 3,
-    "factor_2": 8,
-    "silu_1": 10,
-    "factor_3": 12,
-    "neg_1": 16,
-    "g_codes2": 16,
-    "g_codes3": 17,
-    "silu_3": 20,
-    "da_codes0": 20,
-    "da_codes1": 22,
+    "late_neg4": 5,
+    "late_factor5": 6,
+    "late_neg5": 9,
+    "g_codes2": 8,
+    "da_codes0": 10,
+    "late_part6": 15,
+    "da_codes1": 14,
+    "da_codes2": 16,
     "factor_1": 24,
     "packed0": 27,
 }
 TURN_BANK = (0, 1, 2, 3, 2, 3, 6, 7)
-WORDS_BANK = (6, 7, 4, 5)
+WORDS_BANK = (6, 7, 0, 1)
 GATE_BANK = 6
 DH_BANKS = 4
+LATE_DH_BANK = (0, 1)
+A1_BANK = {4: 4, 5: 5, 6: 2, 7: 3}
+A3_BANK = {4: 6, 5: 7, 6: 6, 7: 7}
+DX_BANK = (6, 7, 0, 1)
+EARLY = 2
 
 
 def tile_moe_bdx_glu_silu_kernel(
@@ -94,7 +99,7 @@ def tile_moe_bdx_glu_silu_kernel(
         a3_sb = a3_sb + [a3_late[:, :, 0:C], a3_late[:, :, C:HALF]]
         w2_raw = new_tile("w2_raw", [P, E, 2 * H], U8)
         w2s_raw = new_tile("w2s_raw", [P, E, H], U8)
-        w2s_perm = new_tile("w2s_perm", [P, E, H], U8)
+        w2s_perm = new_tile("w2s_perm", [P, EARLY, H], U8)
         w1_sb = new_tile("w1_sb", [P, E, 2 * K], U8)
         w3_sb = new_tile("w3_sb", [P, E, 2 * K], U8)
         w1s = new_tile("w1s", [P, E, K], U8)
@@ -143,25 +148,25 @@ def tile_moe_bdx_glu_silu_kernel(
         load_words(w2_raw, w2_words)
         load_expert(a3_sb, a3_4, 0)
         load_expert(a3_sb, a3_4, 1)
-        nc.sync.dma_start(a1_late[:], a1_4[:, :, HALF:])
-        nc.sync.dma_start(a3_late[:], a3_4[:, :, HALF:])
+        nc.sync.dma_start(a1_late[:], a1.rearrange("(j p) s -> p j s", p=P)[:, :, HALF:])
+        nc.sync.dma_start(a3_late[:], a3.rearrange("(j p) s -> p j s", p=P)[:, :, HALF:])
         load_words(w1_sb, w1_words)
         load_words(w3_sb, w3_words)
         load_scales(w1s, w1_scales)
         load_scales(w3s, w3_scales)
 
-        w2_perm = new_tile("w2_perm", [P, E, 2 * H], U8)
+        w2_perm = new_tile("w2_perm", [P, EARLY, 2 * H], U8)
 
         def permute_words():
             nc.vector.tensor_copy(
                 w2_perm[:].bitcast(U16).rearrange("p e (t m) -> p e t m", t=PACK),
-                w2_raw[:].bitcast(U16).rearrange("p e (m t) -> p e t m", t=PACK),
+                w2_raw[:, 0:EARLY].bitcast(U16).rearrange("p e (m t) -> p e t m", t=PACK),
             )
 
         def permute_scales():
             nc.vector.tensor_copy(
                 w2s_perm[:].rearrange("p e (t m) -> p e t m", t=PACK),
-                w2s_raw[:].rearrange("p e (m t) -> p e t m", t=PACK),
+                w2s_raw[:, 0:EARLY].rearrange("p e (m t) -> p e t m", t=PACK),
             )
 
         def walk_planar(ap):
@@ -198,21 +203,33 @@ def tile_moe_bdx_glu_silu_kernel(
         g_bf, g_codes = {}, {}
         g_scales = new_tile("g_scales", [P, S], U8)
 
+        pairs = {}
+
+        def gate_g(e):
+            for block in (2 * e, 2 * e + 1):
+                pairs[block] = gate_block(block)
+
         def pack_g(e):
             words = bank(f"words{e}", [P, 2, 2, P], WORDS_BANK[e])
             for c in range(2):
-                pairs = gate_block(2 * e + c)
                 for u in range(2):
-                    nc.tensor.transpose(words[:, c, u, :], pairs[:, u * P : (u + 1) * P], ident[:])
-            packed = new_tile(f"packed{e}", [P, 2, P, 2], F32)
-            g_bf[e] = packed[:].rearrange("p c s u -> p (c s u)").bitcast(BF16)
-            nc.scalar.copy(packed[:], words[:].rearrange("p c u s -> p c s u"))
+                    nc.tensor.transpose(words[:, c, u, :], pairs[2 * e + c][:, u * P : (u + 1) * P], ident[:])
+            nc.scalar.copy(packed[e], words[:].rearrange("p c u s -> p c s u"))
 
-        def quantize_g(e):
-            g_codes[e] = new_tile(f"g_codes{e}", [P, C], U32)
+        packed_late = new_tile("packed_late", [P, 2, 2, P, 2], F32)
+        packed = [new_tile(f"packed{e}", [P, 2, P, 2], F32)[:] for e in range(2)]
+        packed = packed + [packed_late[:, 0], packed_late[:, 1]]
+        g_bf[0] = packed[0].rearrange("p c s u -> p (c s u)").bitcast(BF16)
+        g_bf[1] = packed[1].rearrange("p c s u -> p (c s u)").bitcast(BF16)
+        g_bf[2] = packed_late[:].rearrange("p e c s u -> p (e c s u)").bitcast(BF16)
+
+        def quantize_g(first, count):
+            codes = new_tile(f"g_codes{first}", [P, count * C], U32)
             nc.vector.quantize_mx(
-                out=g_codes[e][:].bitcast(FP8X4), scales=g_scales[:, e * C : (e + 1) * C], in_=g_bf[e]
+                out=codes[:].bitcast(FP8X4), scales=g_scales[:, first * C : (first + count) * C], in_=g_bf[first]
             )
+            for e in range(count):
+                g_codes[first + e] = codes[:, e * C : (e + 1) * C]
 
         neg_sb, silu_sb, tanh_sb, factor_sb = {}, {}, {}, {}
 
@@ -235,7 +252,10 @@ def tile_moe_bdx_glu_silu_kernel(
             factor_sb[e] = new_tile(f"factor_{e}", [P, PACK, C], F32)
             nc.vector.scalar_tensor_tensor(factor_sb[e][:], tanh_sb[e][:], 1.0, a3_sb[e], ALU.subtract, ALU.mult)
 
-        da_bf = [new_tile(f"da_bf{e}", [P, 2, C, PACK], BF16) for e in range(E)]
+        da_bf = [new_tile(f"da_bf{e}", [P, 2, C, PACK], BF16) for e in range(EARLY)]
+        da_late = {e: new_tile(f"da_late{e}", [P, 2, C, 2], F32) for e in range(EARLY, E)}
+        da_packed = [da_bf[e][:].rearrange("p i n j -> p (i n j)") for e in range(EARLY)]
+        da_packed = da_packed + [da_late[e][:].rearrange("p i n u -> p (i n u)").bitcast(BF16) for e in range(EARLY, E)]
         da_scales = [new_tile(f"da_scales{e}", [P, 2, C], U8) for e in range(E)]
         da_codes, dx_sb = {}, {}
 
@@ -278,30 +298,73 @@ def tile_moe_bdx_glu_silu_kernel(
                     ALU.mult,
                 )
 
-        def make_whole_factor(e):
-            whole = new_tile(f"whole_{e}", [P, PACK, C], F32)
-            nc.vector.scalar_tensor_tensor(whole[:], neg_sb[e][:], 1.0, factor_sb[e][:], ALU.subtract, ALU.mult)
-            return whole
+        def turn(name, source, block, number):
+            e, c = divmod(block, 2)
+            turned = bank(f"{name}{block}", [P, PACK, P], number)
+            for j in range(PACK):
+                nc.tensor.transpose(turned[:, j, :], source[e][:, j, block_cols(c)], ident[:])
+            return turned[:].rearrange("s j p -> s (j p)")
 
-        def products_on_vector(e, whole):
-            for c in range(2):
-                dh = hidden(e, c)
-                nc.vector.tensor_tensor(
-                    walk_packed(da_bf[e][:, 0, block_cols(c), :]),
-                    walk_planar(dh[:]),
-                    walk_planar(whole[:, :, block_cols(c)]),
-                    ALU.mult,
-                )
-                make_da3(e, c, dh)
+        a1_turned, late_neg, late_tanh, late_factor, late_part, da_turned = {}, {}, {}, {}, {}, {}
 
-        def project(e):
+        def late_activations(block):
+            a1_turned[block] = turn("a1_turned", a1_sb, block, A1_BANK[block])
+            late_neg[block] = new_tile(f"late_neg{block}", [P, H], F32)
+            late_tanh[block] = new_tile(f"late_tanh{block}", [P, H], F32)
+            nc.scalar.activation(late_neg[block][:], a1_turned[block], ACT.Silu, scale=-1.0)
+            nc.scalar.activation(late_tanh[block][:], a1_turned[block], ACT.Tanh, scale=-0.5)
+
+        def make_late_factor(block):
+            a3_turned = turn("a3_turned", a3_sb, block, A3_BANK[block])
+            late_factor[block] = new_tile(f"late_factor{block}", [P, H], F32)
+            nc.vector.scalar_tensor_tensor(
+                late_factor[block][:], late_neg[block][:], 1.0, a3_turned, ALU.subtract, ALU.mult
+            )
+
+        def make_late_part(block):
+            e, c = divmod(block, 2)
+            dh = bank(f"dh{block}", [P, H], LATE_DH_BANK[c])
+            nc.tensor.matmul_mx(
+                out=dh[:],
+                lhsT=g_codes[e][:, block_cols(c)].bitcast(FP8X4),
+                lhsT_scale=g_scales[:, block * P : (block + 1) * P],
+                rhs=w2_raw[:, e, :].bitcast(FP4X4),
+                rhs_scale=w2s_raw[:, e, :],
+                start=True,
+                stop=True,
+            )
+            late_part[block] = new_tile(f"late_part{block}", [P, H], F32)
+            nc.vector.scalar_tensor_tensor(
+                late_part[block][:], late_tanh[block][:], 1.0, dh[:], ALU.subtract, ALU.mult
+            )
+            da_turned[block, 0] = new_tile(f"da1_turned{block}", [P, H], BF16)
+            nc.gpsimd.tensor_tensor(da_turned[block, 0][:], late_part[block][:], late_factor[block][:], ALU.mult)
+
+        def make_late_da3(block):
+            da_turned[block, 1] = new_tile(f"da3_turned{block}", [P, H], BF16)
+            nc.vector.scalar_tensor_tensor(
+                da_turned[block, 1][:], late_part[block][:], -1.0, a1_turned[block], ALU.mult, ALU.mult
+            )
+
+        def pack_da(block):
+            e, c = divmod(block, 2)
+            words = bank(f"da_words{block}", [P, 2, 2, P], A1_BANK[block])
+            for i in range(2):
+                turned = da_turned[block, i][:].bitcast(F32)
+                for u in range(2):
+                    nc.tensor.transpose(words[:, i, u, :], turned[:, u : H // 2 : 2], ident[:])
+            nc.scalar.copy(da_late[e][:, :, block_cols(c), :], words[:].rearrange("p i u s -> p i s u"))
+
+        def quantize_da(e):
             da_codes[e] = new_tile(f"da_codes{e}", [P, 2, C], U32)
             nc.vector.quantize_mx(
                 out=da_codes[e][:].rearrange("p i n -> p (i n)").bitcast(FP8X4),
                 scales=da_scales[e][:].rearrange("p i n -> p (i n)"),
-                in_=da_bf[e][:].rearrange("p i n j -> p (i n j)"),
+                in_=da_packed[e],
             )
-            dx = bank(f"dx{e}", [P, K // P, C], DH_BANKS + e)
+
+        def project(e):
+            dx = bank(f"dx{e}", [P, K // P, C], DX_BANK[e])
             for b in range(K // P):
                 for c in range(2):
                     for i, (w, ws) in enumerate(((w1_sb, w1s), (w3_sb, w3s))):
@@ -331,34 +394,48 @@ def tile_moe_bdx_glu_silu_kernel(
         gather(1, 1)
         gather(0, 2)
         gather(0, 3)
+        gate_g(0)
         pack_g(0)
+        gate_g(1)
         pack_g(1)
         gather(1, 3)
         gather(1, 2)
         permute_words()
         for e in range(2):
             make_factor(e)
-            quantize_g(e)
-        pack_g(2)
-        pack_g(3)
+            quantize_g(e, 1)
+        gate_g(2)
+        gate_g(3)
 
         products_shared(0)
+        late_activations(4)
+        pack_g(2)
+        late_activations(5)
+        pack_g(3)
         products_shared(1)
-        quantize_g(2)
-        quantize_g(3)
-        act_tanh(3)
-        act_tanh(2)
-        act_neg(3)
-        make_factor(3)
-        make_factor(2)
-        whole = make_whole_factor(3)
-        act_neg(2)
-        act_silu(2)
-        products_shared(2)
-        act_silu(3)
-        products_on_vector(3, whole)
-
-        for e in range(E):
+        late_activations(6)
+        late_activations(7)
+        make_late_factor(4)
+        make_late_factor(5)
+        quantize_g(2, 2)
+        quantize_da(0)
+        make_late_factor(6)
+        make_late_part(4)
+        make_late_part(5)
+        make_late_da3(4)
+        make_late_da3(5)
+        make_late_part(6)
+        make_late_factor(7)
+        make_late_part(7)
+        make_late_da3(6)
+        make_late_da3(7)
+        pack_da(4)
+        pack_da(5)
+        project(0)
+        pack_da(6)
+        pack_da(7)
+        for e in range(1, E):
+            quantize_da(e)
             project(e)
         for e in range(E):
             for b in range(K // P):

@@ -33,7 +33,6 @@ BYTES = 4 * (N * T + 2 * H * S + K * T + S) + E * P * (2 * H + 4 * K) + E * 16 *
 
 SUCCEEDS = {
     "gathered12": "gathered03",
-    "late_factor4": "neg_1",
     "late_factor6": "packed_late",
     "dx_sb0": "late_neg7",
     "late_tanh4": "plane0",
@@ -44,9 +43,10 @@ SUCCEEDS = {
 PLACES = {
     "tanh_1": 0,
     "part00": 3,
-    "late_neg4": 5,
-    "late_factor5": 6,
-    "late_neg5": 9,
+    "neg_1": 18,
+    "late_factor4": 18,
+    "late_factor5": 20,
+    "late_neg4": 9,
     "g_codes2": 8,
     "da_codes0": 10,
     "late_part6": 15,
@@ -148,10 +148,10 @@ def tile_moe_bdx_glu_silu_kernel(
         load_words(w2_raw, w2_words)
         load_expert(a3_sb, a3_4, 0)
         load_expert(a3_sb, a3_4, 1)
-        nc.sync.dma_start(a1_late[:], a1.rearrange("(j p) s -> p j s", p=P)[:, :, HALF:])
-        nc.sync.dma_start(a3_late[:], a3.rearrange("(j p) s -> p j s", p=P)[:, :, HALF:])
         load_words(w1_sb, w1_words)
         load_words(w3_sb, w3_words)
+        nc.sync.dma_start(a1_late[:], a1.rearrange("(j p) s -> p j s", p=P)[:, :, HALF:])
+        nc.sync.dma_start(a3_late[:], a3.rearrange("(j p) s -> p j s", p=P)[:, :, HALF:])
         load_scales(w1s, w1_scales)
         load_scales(w3s, w3_scales)
 
@@ -363,6 +363,8 @@ def tile_moe_bdx_glu_silu_kernel(
                 in_=da_packed[e],
             )
 
+        dx_late = new_tile("dx_late", [P, K // P, HALF], F32)
+
         def project(e):
             dx = bank(f"dx{e}", [P, K // P, C], DX_BANK[e])
             for b in range(K // P):
@@ -377,8 +379,11 @@ def tile_moe_bdx_glu_silu_kernel(
                             start=(i == 0),
                             stop=(i == 1),
                         )
-            dx_sb[e] = new_tile(f"dx_sb{e}", [P, K // P, C], F32)
-            nc.scalar.activation(dx_sb[e][:], dx[:], ACT.Copy, scale=0.5)
+            if e < EARLY:
+                dx_sb[e] = new_tile(f"dx_sb{e}", [P, K // P, C], F32)[:]
+            else:
+                dx_sb[e] = dx_late[:, :, (e - EARLY) * C : (e - EARLY + 1) * C]
+            nc.scalar.activation(dx_sb[e], dx[:], ACT.Copy, scale=0.5)
 
         permute_scales()
         turn_gate()
@@ -437,8 +442,9 @@ def tile_moe_bdx_glu_silu_kernel(
         for e in range(1, E):
             quantize_da(e)
             project(e)
-        for e in range(E):
+        for e in range(EARLY):
             for b in range(K // P):
                 nc.vector.tensor_copy(win[b][:].indirect(entries(e * C, C)), dx_sb[e][:, b, :])
-                if e == E - 1:
-                    nc.sync.dma_start(out[b * P : (b + 1) * P, :], win[b][:])
+        for b in range(K // P):
+            nc.vector.tensor_copy(win[b][:].indirect(entries(HALF, HALF)), dx_late[:, b, :])
+            nc.sync.dma_start(out[b * P : (b + 1) * P, :], win[b][:])

@@ -35,6 +35,12 @@ SUCCEEDS = {
     "gathered12": "gathered03",
     "late_factor6": "packed_late",
     "dx_sb0": "late_neg7",
+    "da_codes1": "late_part6",
+    "da_codes2": "da_bf1",
+    "da_codes3": "da_late2",
+    "dx_sb1": "da1_turned7",
+    "win0": "a1_late",
+    "win1": "a3_late",
     "late_tanh4": "plane0",
     "late_tanh5": "plane1",
     "late_tanh6": "plane2",
@@ -49,9 +55,6 @@ PLACES = {
     "late_neg4": 9,
     "g_codes2": 8,
     "da_codes0": 10,
-    "late_part6": 15,
-    "da_codes1": 14,
-    "da_codes2": 16,
     "factor_1": 24,
     "packed0": 27,
 }
@@ -62,7 +65,8 @@ DH_BANKS = 4
 LATE_DH_BANK = (0, 1)
 A1_BANK = {4: 4, 5: 5, 6: 2, 7: 3}
 A3_BANK = {4: 6, 5: 7, 6: 6, 7: 7}
-DX_BANK = (6, 7, 0, 1)
+DX_BANK = (4, 7, 0, 1)
+DA_WORDS_BANK = {4: 6, 5: 5, 6: 2, 7: 3}
 EARLY = 2
 
 
@@ -104,17 +108,16 @@ def tile_moe_bdx_glu_silu_kernel(
         w3_sb = new_tile("w3_sb", [P, E, 2 * K], U8)
         w1s = new_tile("w1s", [P, E, K], U8)
         w3s = new_tile("w3s", [P, E, K], U8)
-        win = [new_tile(f"win{b}", [P, T], F32) for b in range(K // P)]
         gate_rows = new_tile("gate_rows", [P, P], F32)
         gate_col = new_tile("gate_col", [P, BLOCKS], F32)
 
-        nc.gpsimd.memset(w2s_raw[:].bitcast(I32), 0)
+        zero = new_tile("zero", [P, 1], F32)
+        nc.vector.memset(w2s_raw[:].bitcast(I32), 0)
         nc.gpsimd.memset(gate_rows[:], 0.0)
         make_identity(nc, ident[:])
-        nc.gpsimd.memset(w1s[:].bitcast(I32), 0)
-        nc.gpsimd.memset(w3s[:].bitcast(I32), 0)
-        for b in range(K // P):
-            nc.vector.memset(win[b][:], 0.0)
+        nc.gpsimd.memset(zero[:], 0.0)
+        nc.vector.memset(w1s[:].bitcast(I32), 0)
+        nc.vector.memset(w3s[:].bitcast(I32), 0)
 
         def load_words(tile, dram):
             nc.sync.dma_start(tile[:].bitcast(I32), dram.bitcast(I32)[:, 0].rearrange("e p b -> p e b"))
@@ -348,7 +351,7 @@ def tile_moe_bdx_glu_silu_kernel(
 
         def pack_da(block):
             e, c = divmod(block, 2)
-            words = bank(f"da_words{block}", [P, 2, 2, P], A1_BANK[block])
+            words = bank(f"da_words{block}", [P, 2, 2, P], DA_WORDS_BANK[block])
             for i in range(2):
                 turned = da_turned[block, i][:].bitcast(F32)
                 for u in range(2):
@@ -434,17 +437,27 @@ def tile_moe_bdx_glu_silu_kernel(
         make_late_part(7)
         make_late_da3(6)
         make_late_da3(7)
+        project(0)
         pack_da(4)
         pack_da(5)
-        project(0)
+        win = [new_tile(f"win{b}", [P, T], F32) for b in range(K // P)]
+        for b in range(K // P):
+            nc.scalar.activation(win[b][:], zero[:].to_broadcast([P, T]), ACT.Copy)
         pack_da(6)
         pack_da(7)
+
+        def scatter(e, b):
+            nc.vector.tensor_copy(win[b][:].indirect(entries(e * C, C)), dx_sb[e][:, b, :])
+
+        quantize_da(1)
+        scatter(0, 0)
+        quantize_da(2)
+        scatter(0, 1)
+        quantize_da(3)
         for e in range(1, E):
-            quantize_da(e)
             project(e)
-        for e in range(EARLY):
-            for b in range(K // P):
-                nc.vector.tensor_copy(win[b][:].indirect(entries(e * C, C)), dx_sb[e][:, b, :])
+        scatter(1, 0)
+        scatter(1, 1)
         for b in range(K // P):
             nc.vector.tensor_copy(win[b][:].indirect(entries(HALF, HALF)), dx_late[:, b, :])
             nc.sync.dma_start(out[b * P : (b + 1) * P, :], win[b][:])

@@ -31,43 +31,37 @@ KIB = 1024
 FLOPS = 2 * S * (N * H + 2 * H * K)
 BYTES = 4 * (N * T + 2 * H * S + K * T + S) + E * P * (2 * H + 4 * K) + E * 16 * (H + 2 * K) + 2 * 16 * S // 16
 
+
 SUCCEEDS = {
     "gathered12": "gathered03",
-    "late_factor6": "packed_late",
-    "dx_sb0": "late_neg7",
-    "da_codes1": "late_part6",
-    "da_codes2": "da_bf1",
-    "da_codes3": "da_late2",
-    "dx_sb1": "da1_turned7",
-    "win0": "a1_late",
-    "win1": "a3_late",
-    "late_tanh4": "plane0",
-    "late_tanh5": "plane1",
-    "late_tanh6": "plane2",
-    "late_tanh7": "plane3",
+    "w2_perm1": "packed0",
+    "da_bf00": "packed1",
+    "gated_a3_2": "da_bf11",
+    "gated_a3_3": "da_bf21",
+    "da_codes20": "neg3",
 }
 PLACES = {
-    "tanh_1": 0,
-    "part00": 3,
-    "neg_1": 18,
-    "late_factor4": 18,
-    "late_factor5": 20,
-    "late_neg4": 9,
-    "g_codes2": 8,
-    "da_codes0": 10,
-    "factor_1": 24,
-    "packed0": 27,
+    "part0": 0,
+    "g_codes2": 0,
+    "da_codes01": 2,
+    "packed_late": 4,
+    "da_bf10": 7,
+    "da_bf01": 8,
+    "part1": 10,
+    "da_codes11": 10,
+    "dx_sb0": 12,
+    "part2": 14,
+    "da_codes21": 14,
+    "dx_sb1": 16,
+    "part3": 18,
+    "da_codes31": 18,
+    "dx_sb21": 20,
 }
-TURN_BANK = (0, 1, 2, 3, 2, 3, 6, 7)
-WORDS_BANK = (6, 7, 0, 1)
-GATE_BANK = 6
-DH_BANKS = 4
-LATE_DH_BANK = (0, 1)
-A1_BANK = {4: 4, 5: 5, 6: 2, 7: 3}
-A3_BANK = {4: 6, 5: 7, 6: 6, 7: 7}
-DX_BANK = (4, 7, 0, 1)
-DA_WORDS_BANK = {4: 6, 5: 5, 6: 2, 7: 3}
-EARLY = 2
+TURN_BANK = (0, 1, 2, 3, 6, 7, 0, 1)
+WORDS_BANK = (4, 5, 6, 7)
+GATE_BANK = 7
+DH_BANK = (4, 2, 3, 5, 0, 1, 2, 3)
+DX_BANK = (4, 5, 6, 7)
 
 
 def tile_moe_bdx_glu_silu_kernel(
@@ -103,19 +97,17 @@ def tile_moe_bdx_glu_silu_kernel(
         a3_sb = a3_sb + [a3_late[:, :, 0:C], a3_late[:, :, C:HALF]]
         w2_raw = new_tile("w2_raw", [P, E, 2 * H], U8)
         w2s_raw = new_tile("w2s_raw", [P, E, H], U8)
-        w2s_perm = new_tile("w2s_perm", [P, EARLY, H], U8)
         w1_sb = new_tile("w1_sb", [P, E, 2 * K], U8)
         w3_sb = new_tile("w3_sb", [P, E, 2 * K], U8)
         w1s = new_tile("w1s", [P, E, K], U8)
         w3s = new_tile("w3s", [P, E, K], U8)
         gate_rows = new_tile("gate_rows", [P, P], F32)
         gate_col = new_tile("gate_col", [P, BLOCKS], F32)
+        win = [new_tile(f"win{b}", [P, T], F32) for b in range(K // P)]
 
-        zero = new_tile("zero", [P, 1], F32)
+        nc.vector.memset(gate_rows[:], 0.0)
         nc.vector.memset(w2s_raw[:].bitcast(I32), 0)
-        nc.gpsimd.memset(gate_rows[:], 0.0)
         make_identity(nc, ident[:])
-        nc.gpsimd.memset(zero[:], 0.0)
         nc.vector.memset(w1s[:].bitcast(I32), 0)
         nc.vector.memset(w3s[:].bitcast(I32), 0)
 
@@ -139,37 +131,42 @@ def tile_moe_bdx_glu_silu_kernel(
         def load_expert(tiles, dram, e):
             nc.sync.dma_start(tiles[e], dram[:, :, e * C : (e + 1) * C])
 
-        nc.sync.dma_start(offsets[:], offs)
-        load_scales(w2s_raw, w2_scales)
+        def load_late(tile, dram):
+            nc.sync.dma_start(tile[:], dram[:, :, HALF:])
+
         load_plane(0)
-        nc.sync.dma_start(gate_rows[0:BLOCKS, :], gate[0, :].rearrange("(b n) -> b n", n=P))
+        nc.sync.dma_start(offsets[:], offs)
         load_expert(a1_sb, a1_4, 0)
+        nc.sync.dma_start(gate_rows[0:BLOCKS, :], gate[0, :].rearrange("(b n) -> b n", n=P))
         load_plane(1)
-        load_expert(a1_sb, a1_4, 1)
+        load_scales(w2s_raw, w2_scales)
         load_plane(2)
+        load_expert(a1_sb, a1_4, 1)
         load_plane(3)
-        load_words(w2_raw, w2_words)
         load_expert(a3_sb, a3_4, 0)
+        load_words(w2_raw, w2_words)
         load_expert(a3_sb, a3_4, 1)
+        load_late(a1_late, a1_4)
         load_words(w1_sb, w1_words)
         load_words(w3_sb, w3_words)
-        nc.sync.dma_start(a1_late[:], a1.rearrange("(j p) s -> p j s", p=P)[:, :, HALF:])
-        nc.sync.dma_start(a3_late[:], a3.rearrange("(j p) s -> p j s", p=P)[:, :, HALF:])
         load_scales(w1s, w1_scales)
         load_scales(w3s, w3_scales)
+        load_late(a3_late, a3_4)
 
-        w2_perm = new_tile("w2_perm", [P, EARLY, 2 * H], U8)
+        w2_perm, w2s_perm = {}, {}
 
-        def permute_words():
+        def permute_words(h):
+            w2_perm[h] = new_tile(f"w2_perm{h}", [P, 2, 2 * H], U8)
             nc.vector.tensor_copy(
-                w2_perm[:].bitcast(U16).rearrange("p e (t m) -> p e t m", t=PACK),
-                w2_raw[:, 0:EARLY].bitcast(U16).rearrange("p e (m t) -> p e t m", t=PACK),
+                w2_perm[h][:].bitcast(U16).rearrange("p e (t m) -> p e t m", t=PACK),
+                w2_raw[:, 2 * h : 2 * h + 2].bitcast(U16).rearrange("p e (m t) -> p e t m", t=PACK),
             )
 
-        def permute_scales():
-            nc.vector.tensor_copy(
-                w2s_perm[:].rearrange("p e (t m) -> p e t m", t=PACK),
-                w2s_raw[:, 0:EARLY].rearrange("p e (m t) -> p e t m", t=PACK),
+        def permute_scales(h):
+            w2s_perm[h] = new_tile(f"w2s_perm{h}", [P, 2, H], U8)
+            nc.gpsimd.tensor_copy(
+                w2s_perm[h][:].rearrange("p e (t m) -> p e t m", t=PACK),
+                w2s_raw[:, 2 * h : 2 * h + 2].rearrange("p e (m t) -> p e t m", t=PACK),
             )
 
         def walk_planar(ap):
@@ -177,6 +174,9 @@ def tile_moe_bdx_glu_silu_kernel(
 
         def walk_packed(ap):
             return ap.rearrange("p (c i) j -> p c j i", i=4)
+
+        def block_cols(c):
+            return slice(c * P, (c + 1) * P)
 
         def turn_gate():
             turned = bank("turned", [P, P], GATE_BANK)
@@ -188,6 +188,8 @@ def tile_moe_bdx_glu_silu_kernel(
         def gather(h, t):
             gathered[h, t] = new_tile(f"gathered{h}{t}", [P, HALF], F32)
             nc.vector.tensor_copy(gathered[h, t][:], planes[t][:].indirect(entries(h * HALF, HALF)))
+
+        pairs = {}
 
         def gate_block(block):
             h, first = divmod(block * P, HALF)
@@ -201,16 +203,16 @@ def tile_moe_bdx_glu_silu_kernel(
                 ACT.Copy,
                 scale=gate_col[:, block : block + 1],
             )
-            return gated[:].rearrange("s u p v -> s (u p v)").bitcast(F32)
+            pairs[block] = gated[:].rearrange("s u p v -> s (u p v)").bitcast(F32)
 
         g_bf, g_codes = {}, {}
         g_scales = new_tile("g_scales", [P, S], U8)
-
-        pairs = {}
-
-        def gate_g(e):
-            for block in (2 * e, 2 * e + 1):
-                pairs[block] = gate_block(block)
+        packed_late = new_tile("packed_late", [P, 2, 2, P, 2], F32)
+        packed = [new_tile(f"packed{e}", [P, 2, P, 2], F32)[:] for e in range(2)]
+        packed = packed + [packed_late[:, 0], packed_late[:, 1]]
+        g_bf[0] = packed[0].rearrange("p c s u -> p (c s u)").bitcast(BF16)
+        g_bf[1] = packed[1].rearrange("p c s u -> p (c s u)").bitcast(BF16)
+        g_bf[2] = packed_late[:].rearrange("p e c s u -> p (e c s u)").bitcast(BF16)
 
         def pack_g(e):
             words = bank(f"words{e}", [P, 2, 2, P], WORDS_BANK[e])
@@ -218,13 +220,6 @@ def tile_moe_bdx_glu_silu_kernel(
                 for u in range(2):
                     nc.tensor.transpose(words[:, c, u, :], pairs[2 * e + c][:, u * P : (u + 1) * P], ident[:])
             nc.scalar.copy(packed[e], words[:].rearrange("p c u s -> p c s u"))
-
-        packed_late = new_tile("packed_late", [P, 2, 2, P, 2], F32)
-        packed = [new_tile(f"packed{e}", [P, 2, P, 2], F32)[:] for e in range(2)]
-        packed = packed + [packed_late[:, 0], packed_late[:, 1]]
-        g_bf[0] = packed[0].rearrange("p c s u -> p (c s u)").bitcast(BF16)
-        g_bf[1] = packed[1].rearrange("p c s u -> p (c s u)").bitcast(BF16)
-        g_bf[2] = packed_late[:].rearrange("p e c s u -> p (e c s u)").bitcast(BF16)
 
         def quantize_g(first, count):
             codes = new_tile(f"g_codes{first}", [P, count * C], U32)
@@ -234,230 +229,214 @@ def tile_moe_bdx_glu_silu_kernel(
             for e in range(count):
                 g_codes[first + e] = codes[:, e * C : (e + 1) * C]
 
-        neg_sb, silu_sb, tanh_sb, factor_sb = {}, {}, {}, {}
+        neg_sb, silu_sb, sig_sb, gated_a3, part, dh = {}, {}, {}, {}, {}, {}
 
         def act_neg(e):
-            neg_sb[e] = new_tile(f"neg_{e}", [P, PACK, C], F32)
-            nc.scalar.activation(neg_sb[e][:], a1_sb[e], ACT.Silu, scale=-1.0)
+            neg_sb[e] = new_tile(f"neg{e}", [P, C, PACK], F32)
+            nc.scalar.activation(walk_packed(neg_sb[e][:]), walk_planar(a1_sb[e]), ACT.Silu, scale=-1.0)
 
         def act_silu(e):
-            silu_sb[e] = new_tile(f"silu_{e}", [P, C, PACK], F32)
+            silu_sb[e] = new_tile(f"silu{e}", [P, C, PACK], F32)
             nc.scalar.activation(walk_packed(silu_sb[e][:]), walk_planar(a1_sb[e]), ACT.Silu)
 
         def act_tanh(e):
-            tanh_sb[e] = new_tile(f"tanh_{e}", [P, PACK, C], F32)
-            nc.scalar.activation(tanh_sb[e][:], a1_sb[e], ACT.Tanh, scale=-0.5)
+            sig_sb[e] = new_tile(f"sig{e}", [P, PACK, C], F32)
+            nc.scalar.activation(sig_sb[e][:], a1_sb[e], ACT.Tanh, scale=-0.5)
 
-        def block_cols(c):
-            return slice(c * P, (c + 1) * P)
+        def act_sig(e):
+            nc.scalar.activation(sig_sb[e][:], sig_sb[e][:], ACT.Identity, bias=-1.0)
+
+        def shift_tanh(e):
+            nc.gpsimd.tensor_scalar(sig_sb[e][:], sig_sb[e][:], 1.0, -1.0, ALU.mult, ALU.add)
+
+        def make_gated_a3(e):
+            gated_a3[e] = new_tile(f"gated_a3_{e}", [P, PACK, C], F32)
+            nc.gpsimd.tensor_tensor(gated_a3[e][:], sig_sb[e][:], a3_sb[e], ALU.mult)
 
         def make_factor(e):
-            factor_sb[e] = new_tile(f"factor_{e}", [P, PACK, C], F32)
-            nc.vector.scalar_tensor_tensor(factor_sb[e][:], tanh_sb[e][:], 1.0, a3_sb[e], ALU.subtract, ALU.mult)
+            gated_a3[e] = new_tile(f"gated_a3_{e}", [P, PACK, C], F32)
+            nc.vector.scalar_tensor_tensor(gated_a3[e][:], sig_sb[e][:], 1.0, a3_sb[e], ALU.subtract, ALU.mult)
 
-        da_bf = [new_tile(f"da_bf{e}", [P, 2, C, PACK], BF16) for e in range(EARLY)]
-        da_late = {e: new_tile(f"da_late{e}", [P, 2, C, 2], F32) for e in range(EARLY, E)}
-        da_packed = [da_bf[e][:].rearrange("p i n j -> p (i n j)") for e in range(EARLY)]
-        da_packed = da_packed + [da_late[e][:].rearrange("p i n u -> p (i n u)").bitcast(BF16) for e in range(EARLY, E)]
+        da_bf = {(e, i): new_tile(f"da_bf{e}{i}", [P, C, PACK], BF16) for e in range(E) for i in range(2)}
         da_scales = [new_tile(f"da_scales{e}", [P, 2, C], U8) for e in range(E)]
-        da_codes, dx_sb = {}, {}
+        da_codes = {}
 
-        def hidden(e, c):
-            dh = bank(f"dh{e}{c}", [P, PACK, P], (2 * e + c) % DH_BANKS)
+        def make_part(e, c):
+            h, k = divmod(e, 2)
+            dh[e, c] = bank(f"dh{e}{c}", [P, PACK, P], DH_BANK[2 * e + c])
             for t in range(PACK):
                 nc.tensor.matmul_mx(
-                    out=dh[:, t, :],
-                    lhsT=w2_perm[:, e, 2 * P * t : 2 * P * (t + 1)].bitcast(FP4X4),
-                    lhsT_scale=w2s_perm[:, e, P * t : P * (t + 1)],
+                    out=dh[e, c][:, t, :],
+                    lhsT=w2_perm[h][:, k, 2 * P * t : 2 * P * (t + 1)].bitcast(FP4X4),
+                    lhsT_scale=w2s_perm[h][:, k, P * t : P * (t + 1)],
                     rhs=g_codes[e][:, block_cols(c)].bitcast(FP8X4),
                     rhs_scale=g_scales[:, e * C + c * P : e * C + (c + 1) * P],
                     start=True,
                     stop=True,
                 )
-            return dh
-
-        def make_da3(e, c, dh):
+            if c == 0:
+                part[e] = new_tile(f"part{e}", [P, C, PACK], F32)
             nc.vector.scalar_tensor_tensor(
-                da_bf[e][:, 1, block_cols(c), :],
-                dh[:].rearrange("p j n -> p n j"),
+                part[e][:, block_cols(c), :],
+                neg_sb[e][:, block_cols(c), :],
+                1.0,
+                dh[e, c][:].rearrange("p j n -> p n j"),
+                ALU.subtract,
+                ALU.mult,
+            )
+
+        def make_da3(e, c):
+            nc.vector.scalar_tensor_tensor(
+                da_bf[e, 1][:, block_cols(c), :],
+                dh[e, c][:].rearrange("p j n -> p n j"),
                 2.0,
                 silu_sb[e][:, block_cols(c), :],
                 ALU.mult,
                 ALU.mult,
             )
 
-        def products_shared(e):
-            for c in range(2):
-                dh = hidden(e, c)
-                part = new_tile(f"part{e}{c}", [P, PACK, P], F32)
-                nc.vector.scalar_tensor_tensor(
-                    part[:], neg_sb[e][:, :, block_cols(c)], 1.0, dh[:], ALU.subtract, ALU.mult
-                )
-                make_da3(e, c, dh)
-                nc.gpsimd.tensor_tensor(
-                    walk_packed(da_bf[e][:, 0, block_cols(c), :]),
-                    walk_planar(part[:]),
-                    walk_planar(factor_sb[e][:, :, block_cols(c)]),
-                    ALU.mult,
-                )
-
-        def turn(name, source, block, number):
-            e, c = divmod(block, 2)
-            turned = bank(f"{name}{block}", [P, PACK, P], number)
-            for j in range(PACK):
-                nc.tensor.transpose(turned[:, j, :], source[e][:, j, block_cols(c)], ident[:])
-            return turned[:].rearrange("s j p -> s (j p)")
-
-        a1_turned, late_neg, late_tanh, late_factor, late_part, da_turned = {}, {}, {}, {}, {}, {}
-
-        def late_activations(block):
-            a1_turned[block] = turn("a1_turned", a1_sb, block, A1_BANK[block])
-            late_neg[block] = new_tile(f"late_neg{block}", [P, H], F32)
-            late_tanh[block] = new_tile(f"late_tanh{block}", [P, H], F32)
-            nc.scalar.activation(late_neg[block][:], a1_turned[block], ACT.Silu, scale=-1.0)
-            nc.scalar.activation(late_tanh[block][:], a1_turned[block], ACT.Tanh, scale=-0.5)
-
-        def make_late_factor(block):
-            a3_turned = turn("a3_turned", a3_sb, block, A3_BANK[block])
-            late_factor[block] = new_tile(f"late_factor{block}", [P, H], F32)
-            nc.vector.scalar_tensor_tensor(
-                late_factor[block][:], late_neg[block][:], 1.0, a3_turned, ALU.subtract, ALU.mult
+        def make_da1(e, cols):
+            nc.gpsimd.tensor_tensor(
+                da_bf[e, 0][:, cols, :],
+                part[e][:, cols, :],
+                gated_a3[e][:, :, cols].rearrange("p j n -> p n j"),
+                ALU.mult,
             )
-
-        def make_late_part(block):
-            e, c = divmod(block, 2)
-            dh = bank(f"dh{block}", [P, H], LATE_DH_BANK[c])
-            nc.tensor.matmul_mx(
-                out=dh[:],
-                lhsT=g_codes[e][:, block_cols(c)].bitcast(FP8X4),
-                lhsT_scale=g_scales[:, block * P : (block + 1) * P],
-                rhs=w2_raw[:, e, :].bitcast(FP4X4),
-                rhs_scale=w2s_raw[:, e, :],
-                start=True,
-                stop=True,
-            )
-            late_part[block] = new_tile(f"late_part{block}", [P, H], F32)
-            nc.vector.scalar_tensor_tensor(
-                late_part[block][:], late_tanh[block][:], 1.0, dh[:], ALU.subtract, ALU.mult
-            )
-            da_turned[block, 0] = new_tile(f"da1_turned{block}", [P, H], BF16)
-            nc.gpsimd.tensor_tensor(da_turned[block, 0][:], late_part[block][:], late_factor[block][:], ALU.mult)
-
-        def make_late_da3(block):
-            da_turned[block, 1] = new_tile(f"da3_turned{block}", [P, H], BF16)
-            nc.vector.scalar_tensor_tensor(
-                da_turned[block, 1][:], late_part[block][:], -1.0, a1_turned[block], ALU.mult, ALU.mult
-            )
-
-        def pack_da(block):
-            e, c = divmod(block, 2)
-            words = bank(f"da_words{block}", [P, 2, 2, P], DA_WORDS_BANK[block])
-            for i in range(2):
-                turned = da_turned[block, i][:].bitcast(F32)
-                for u in range(2):
-                    nc.tensor.transpose(words[:, i, u, :], turned[:, u : H // 2 : 2], ident[:])
-            nc.scalar.copy(da_late[e][:, :, block_cols(c), :], words[:].rearrange("p i u s -> p i s u"))
 
         def quantize_da(e):
-            da_codes[e] = new_tile(f"da_codes{e}", [P, 2, C], U32)
-            nc.vector.quantize_mx(
-                out=da_codes[e][:].rearrange("p i n -> p (i n)").bitcast(FP8X4),
-                scales=da_scales[e][:].rearrange("p i n -> p (i n)"),
-                in_=da_packed[e],
-            )
+            for i in range(2):
+                da_codes[e, i] = new_tile(f"da_codes{e}{i}", [P, C], U32)
+                nc.vector.quantize_mx(
+                    out=da_codes[e, i][:].bitcast(FP8X4),
+                    scales=da_scales[e][:, i, :],
+                    in_=da_bf[e, i][:].rearrange("p n j -> p (n j)"),
+                )
 
-        dx_late = new_tile("dx_late", [P, K // P, HALF], F32)
+        dx, dx_sb = {}, {}
 
         def project(e):
-            dx = bank(f"dx{e}", [P, K // P, C], DX_BANK[e])
+            dx[e] = bank(f"dx{e}", [P, K // P, C], DX_BANK[e])
             for b in range(K // P):
                 for c in range(2):
                     for i, (w, ws) in enumerate(((w1_sb, w1s), (w3_sb, w3s))):
                         nc.tensor.matmul_mx(
-                            out=dx[:, b, block_cols(c)],
+                            out=dx[e][:, b, block_cols(c)],
                             lhsT=w[:, e, 2 * P * b : 2 * P * (b + 1)].bitcast(FP4X4),
                             lhsT_scale=ws[:, e, P * b : P * (b + 1)],
-                            rhs=da_codes[e][:, i, block_cols(c)].bitcast(FP8X4),
+                            rhs=da_codes[e, i][:, block_cols(c)].bitcast(FP8X4),
                             rhs_scale=da_scales[e][:, i, block_cols(c)],
                             start=(i == 0),
                             stop=(i == 1),
                         )
-            if e < EARLY:
-                dx_sb[e] = new_tile(f"dx_sb{e}", [P, K // P, C], F32)[:]
-            else:
-                dx_sb[e] = dx_late[:, :, (e - EARLY) * C : (e - EARLY + 1) * C]
-            nc.scalar.activation(dx_sb[e], dx[:], ACT.Copy, scale=0.5)
 
-        permute_scales()
+        def copy_dx(e):
+            both = new_tile(f"dx_sb{e}", [P, K // P, C], F32)
+            nc.scalar.activation(both[:], dx[e][:], ACT.Copy, scale=0.5)
+            for b in range(K // P):
+                dx_sb[e, b] = both[:, b, :]
+
+        def copy_dx_rows(e, b):
+            dx_sb[e, b] = new_tile(f"dx_sb{e}{b}", [P, C], F32)[:]
+            nc.scalar.activation(dx_sb[e, b], dx[e][:, b, :], ACT.Copy, scale=0.5)
+
+        def scatter(e, b):
+            nc.vector.tensor_copy(win[b][:].indirect(entries(e * C, C)), dx_sb[e, b])
+
+        def store(b):
+            nc.sync.dma_start(out[b * P : (b + 1) * P, :], win[b][:])
+
+        whole = slice(0, C)
+
         turn_gate()
+        permute_scales(0)
+        permute_scales(1)
+        for b in range(K // P):
+            nc.gpsimd.memset(win[b][:], 0.0)
         gather(0, 0)
         gather(1, 0)
-        act_neg(0)
-        act_silu(0)
         act_tanh(0)
-        act_tanh(1)
-        act_neg(1)
-        act_silu(1)
+        act_neg(0)
+        shift_tanh(0)
+        act_silu(0)
         gather(0, 1)
         gather(1, 1)
         gather(0, 2)
+        act_tanh(1)
+        act_neg(1)
         gather(0, 3)
-        gate_g(0)
+        gate_block(0)
+        gate_block(1)
+        gate_block(2)
         pack_g(0)
-        gate_g(1)
+        gate_block(3)
         pack_g(1)
+        act_silu(1)
         gather(1, 3)
         gather(1, 2)
-        permute_words()
-        for e in range(2):
-            make_factor(e)
-            quantize_g(e, 1)
-        gate_g(2)
-        gate_g(3)
-
-        products_shared(0)
-        late_activations(4)
+        make_gated_a3(0)
+        permute_words(0)
+        make_factor(1)
+        quantize_g(0, 1)
+        permute_words(1)
+        make_part(0, 0)
+        quantize_g(1, 1)
+        make_part(0, 1)
+        make_da1(0, block_cols(0))
+        make_da1(0, block_cols(1))
+        make_da3(0, 0)
+        make_da3(0, 1)
+        gate_block(4)
+        gate_block(5)
+        gate_block(6)
         pack_g(2)
-        late_activations(5)
+        gate_block(7)
         pack_g(3)
-        products_shared(1)
-        late_activations(6)
-        late_activations(7)
-        make_late_factor(4)
-        make_late_factor(5)
+        make_part(1, 0)
+        make_part(1, 1)
+        make_da3(1, 0)
+        make_da3(1, 1)
         quantize_g(2, 2)
         quantize_da(0)
-        make_late_factor(6)
-        make_late_part(4)
-        make_late_part(5)
-        make_late_da3(4)
-        make_late_da3(5)
-        make_late_part(6)
-        make_late_factor(7)
-        make_late_part(7)
-        make_late_da3(6)
-        make_late_da3(7)
+        make_da1(1, whole)
+        act_neg(2)
+        act_silu(2)
+        act_tanh(2)
+        act_sig(2)
+        make_part(2, 0)
+        make_part(2, 1)
         project(0)
-        pack_da(4)
-        pack_da(5)
-        win = [new_tile(f"win{b}", [P, T], F32) for b in range(K // P)]
-        for b in range(K // P):
-            nc.scalar.activation(win[b][:], zero[:].to_broadcast([P, T]), ACT.Copy)
-        pack_da(6)
-        pack_da(7)
-
-        def scatter(e, b):
-            nc.vector.tensor_copy(win[b][:].indirect(entries(e * C, C)), dx_sb[e][:, b, :])
-
+        make_da3(2, 0)
+        make_da3(2, 1)
         quantize_da(1)
+        make_gated_a3(2)
+        make_da1(2, whole)
+        copy_dx(0)
         scatter(0, 0)
-        quantize_da(2)
         scatter(0, 1)
-        quantize_da(3)
-        for e in range(1, E):
-            project(e)
+        project(1)
+        act_neg(3)
+        act_silu(3)
+        act_tanh(3)
+        act_sig(3)
+        make_part(3, 0)
+        make_part(3, 1)
+        make_da3(3, 0)
+        make_da3(3, 1)
+        quantize_da(2)
+        project(2)
+        make_gated_a3(3)
+        make_da1(3, whole)
+        copy_dx(1)
         scatter(1, 0)
         scatter(1, 1)
+        copy_dx_rows(2, 0)
+        scatter(2, 0)
+        quantize_da(3)
+        project(3)
+        copy_dx_rows(2, 1)
+        scatter(2, 1)
         for b in range(K // P):
-            nc.vector.tensor_copy(win[b][:].indirect(entries(HALF, HALF)), dx_late[:, b, :])
-            nc.sync.dma_start(out[b * P : (b + 1) * P, :], win[b][:])
+            copy_dx_rows(3, b)
+        for b in range(K // P):
+            scatter(3, b)
+            store(b)

@@ -33,17 +33,21 @@ BYTES = 4 * (N * T + 2 * H * S + K * T + S) + E * P * (2 * H + 4 * K) + E * 16 *
 
 
 SUCCEEDS = {
-    "gathered12": "gathered03",
-    "w2_perm1": "packed0",
+    "silu1": "gated7",
     "da_bf00": "packed1",
-    "gated_a3_2": "da_bf11",
     "gated_a3_3": "da_bf21",
     "da_codes20": "neg3",
 }
 PLACES = {
-    "part0": 0,
-    "g_codes2": 0,
-    "da_codes01": 2,
+    "gathered12": 22,
+    "w2_raw": 23,
+    "gathered13": 24,
+    "gated_a3_0": 26,
+    "part0": 30,
+    "g_codes2": 30,
+    "da_codes01": 32,
+    "da_bf11": 33,
+    "gated_a3_2": 34,
     "packed_late": 4,
     "da_bf10": 7,
     "da_bf01": 8,
@@ -143,8 +147,8 @@ def tile_moe_bdx_glu_silu_kernel(
         load_plane(2)
         load_expert(a1_sb, a1_4, 1)
         load_plane(3)
-        load_expert(a3_sb, a3_4, 0)
         load_words(w2_raw, w2_words)
+        load_expert(a3_sb, a3_4, 0)
         load_expert(a3_sb, a3_4, 1)
         load_late(a1_late, a1_4)
         load_words(w1_sb, w1_words)
@@ -162,9 +166,9 @@ def tile_moe_bdx_glu_silu_kernel(
                 w2_raw[:, 2 * h : 2 * h + 2].bitcast(U16).rearrange("p e (m t) -> p e t m", t=PACK),
             )
 
-        def permute_scales(h):
+        def permute_scales(h, engine):
             w2s_perm[h] = new_tile(f"w2s_perm{h}", [P, 2, H], U8)
-            nc.gpsimd.tensor_copy(
+            engine.tensor_copy(
                 w2s_perm[h][:].rearrange("p e (t m) -> p e t m", t=PACK),
                 w2s_raw[:, 2 * h : 2 * h + 2].rearrange("p e (m t) -> p e t m", t=PACK),
             )
@@ -348,8 +352,8 @@ def tile_moe_bdx_glu_silu_kernel(
         whole = slice(0, C)
 
         turn_gate()
-        permute_scales(0)
-        permute_scales(1)
+        permute_scales(0, nc.gpsimd)
+        permute_scales(1, nc.gpsimd)
         for b in range(K // P):
             nc.gpsimd.memset(win[b][:], 0.0)
         gather(0, 0)
@@ -370,16 +374,15 @@ def tile_moe_bdx_glu_silu_kernel(
         pack_g(0)
         gate_block(3)
         pack_g(1)
-        act_silu(1)
+        permute_words(0)
+        permute_words(1)
         gather(1, 3)
         gather(1, 2)
         make_gated_a3(0)
-        permute_words(0)
-        make_factor(1)
         quantize_g(0, 1)
-        permute_words(1)
-        make_part(0, 0)
+        make_factor(1)
         quantize_g(1, 1)
+        make_part(0, 0)
         make_part(0, 1)
         make_da1(0, block_cols(0))
         make_da1(0, block_cols(1))
@@ -391,13 +394,14 @@ def tile_moe_bdx_glu_silu_kernel(
         pack_g(2)
         gate_block(7)
         pack_g(3)
+        act_silu(1)
         make_part(1, 0)
         make_part(1, 1)
-        make_da3(1, 0)
-        make_da3(1, 1)
         quantize_g(2, 2)
         quantize_da(0)
         make_da1(1, whole)
+        make_da3(1, 0)
+        make_da3(1, 1)
         act_neg(2)
         act_silu(2)
         act_tanh(2)

@@ -34,11 +34,13 @@ BYTES = 4 * (N * T + 2 * H * S + K * T + S) + E * P * (2 * H + 4 * K) + E * 16 *
 
 SUCCEEDS = {
     "silu1": "gated7",
+    "silu31": "da_bf20",
     "da_bf00": "packed1",
     "gated_a3_3": "da_bf21",
     "da_codes20": "neg3",
 }
 PLACES = {
+    "silu21": 7,
     "gathered12": 22,
     "w2_raw": 23,
     "gathered13": 24,
@@ -109,11 +111,11 @@ def tile_moe_bdx_glu_silu_kernel(
         gate_col = new_tile("gate_col", [P, BLOCKS], F32)
         win = [new_tile(f"win{b}", [P, T], F32) for b in range(K // P)]
 
-        nc.vector.memset(gate_rows[:], 0.0)
-        nc.vector.memset(w2s_raw[:].bitcast(I32), 0)
+        nc.gpsimd.memset(gate_rows[:], 0.0)
+        nc.gpsimd.memset(w2s_raw[:].bitcast(I32), 0)
         make_identity(nc, ident[:])
-        nc.vector.memset(w1s[:].bitcast(I32), 0)
-        nc.vector.memset(w3s[:].bitcast(I32), 0)
+        nc.gpsimd.memset(w1s[:].bitcast(I32), 0)
+        nc.gpsimd.memset(w3s[:].bitcast(I32), 0)
 
         def load_words(tile, dram):
             nc.sync.dma_start(tile[:].bitcast(I32), dram.bitcast(I32)[:, 0].rearrange("e p b -> p e b"))
@@ -236,12 +238,18 @@ def tile_moe_bdx_glu_silu_kernel(
         neg_sb, silu_sb, sig_sb, gated_a3, part, dh = {}, {}, {}, {}, {}, {}
 
         def act_neg(e):
-            neg_sb[e] = new_tile(f"neg{e}", [P, C, PACK], F32)
-            nc.scalar.activation(walk_packed(neg_sb[e][:]), walk_planar(a1_sb[e]), ACT.Silu, scale=-1.0)
+            neg_sb[e] = new_tile(f"neg{e}", [P, PACK, C], F32)
+            nc.scalar.activation(neg_sb[e][:], a1_sb[e], ACT.Silu, scale=-1.0)
 
         def act_silu(e):
-            silu_sb[e] = new_tile(f"silu{e}", [P, C, PACK], F32)
-            nc.scalar.activation(walk_packed(silu_sb[e][:]), walk_planar(a1_sb[e]), ACT.Silu)
+            both = new_tile(f"silu{e}", [P, C, PACK], F32)
+            nc.scalar.activation(walk_packed(both[:]), walk_planar(a1_sb[e]), ACT.Silu)
+            for c in range(2):
+                silu_sb[e, c] = both[:, block_cols(c), :]
+
+        def act_silu_block(e, c):
+            silu_sb[e, c] = new_tile(f"silu{e}{c}", [P, P, PACK], F32)[:]
+            nc.scalar.activation(walk_packed(silu_sb[e, c]), walk_planar(a1_sb[e][:, :, block_cols(c)]), ACT.Silu)
 
         def act_tanh(e):
             sig_sb[e] = new_tile(f"sig{e}", [P, PACK, C], F32)
@@ -279,12 +287,12 @@ def tile_moe_bdx_glu_silu_kernel(
                     stop=True,
                 )
             if c == 0:
-                part[e] = new_tile(f"part{e}", [P, C, PACK], F32)
+                part[e] = new_tile(f"part{e}", [P, PACK, C], F32)
             nc.vector.scalar_tensor_tensor(
-                part[e][:, block_cols(c), :],
-                neg_sb[e][:, block_cols(c), :],
+                part[e][:, :, block_cols(c)],
+                neg_sb[e][:, :, block_cols(c)],
                 1.0,
-                dh[e, c][:].rearrange("p j n -> p n j"),
+                dh[e, c][:],
                 ALU.subtract,
                 ALU.mult,
             )
@@ -294,16 +302,16 @@ def tile_moe_bdx_glu_silu_kernel(
                 da_bf[e, 1][:, block_cols(c), :],
                 dh[e, c][:].rearrange("p j n -> p n j"),
                 2.0,
-                silu_sb[e][:, block_cols(c), :],
+                silu_sb[e, c],
                 ALU.mult,
                 ALU.mult,
             )
 
         def make_da1(e, cols):
             nc.gpsimd.tensor_tensor(
-                da_bf[e, 0][:, cols, :],
-                part[e][:, cols, :],
-                gated_a3[e][:, :, cols].rearrange("p j n -> p n j"),
+                walk_packed(da_bf[e, 0][:, cols, :]),
+                walk_planar(part[e][:, :, cols]),
+                walk_planar(gated_a3[e][:, :, cols]),
                 ALU.mult,
             )
 
@@ -403,35 +411,37 @@ def tile_moe_bdx_glu_silu_kernel(
         make_da3(1, 0)
         make_da3(1, 1)
         act_neg(2)
-        act_silu(2)
+        act_silu_block(2, 0)
         act_tanh(2)
         act_sig(2)
         make_part(2, 0)
         make_part(2, 1)
         project(0)
         make_da3(2, 0)
-        make_da3(2, 1)
         quantize_da(1)
         make_gated_a3(2)
         make_da1(2, whole)
         copy_dx(0)
+        act_silu_block(2, 1)
         scatter(0, 0)
+        make_da3(2, 1)
         scatter(0, 1)
         project(1)
         act_neg(3)
-        act_silu(3)
+        act_silu_block(3, 0)
         act_tanh(3)
         act_sig(3)
         make_part(3, 0)
         make_part(3, 1)
         make_da3(3, 0)
-        make_da3(3, 1)
         quantize_da(2)
         project(2)
         make_gated_a3(3)
         make_da1(3, whole)
         copy_dx(1)
+        act_silu_block(3, 1)
         scatter(1, 0)
+        make_da3(3, 1)
         scatter(1, 1)
         copy_dx_rows(2, 0)
         scatter(2, 0)

@@ -34,25 +34,16 @@ BYTES = 4 * (N * T + 2 * H * S + K * T + S) + E * P * (2 * H + 4 * K) + E * 16 *
 
 SUCCEEDS = {
     "silu1": "gated7",
-    "silu31": "da_bf20",
     "da_bf00": "packed1",
-    "gated_a3_3": "da_bf21",
     "da_codes20": "neg3",
+    "factor3": "da_bf21",
+    "silu31": "da_bf20",
 }
 PLACES = {
-    "silu21": 7,
-    "gathered12": 22,
-    "w2_raw": 23,
-    "gathered13": 24,
-    "gated_a3_0": 26,
-    "part0": 30,
-    "g_codes2": 30,
-    "da_codes01": 32,
-    "da_bf11": 33,
-    "gated_a3_2": 34,
-    "packed_late": 4,
+    "packed_half1": 4,
     "da_bf10": 7,
     "da_bf01": 8,
+    "silu21": 7,
     "part1": 10,
     "da_codes11": 10,
     "dx_sb0": 12,
@@ -62,12 +53,22 @@ PLACES = {
     "part3": 18,
     "da_codes31": 18,
     "dx_sb21": 20,
+    "gathered12": 22,
+    "w2_raw": 23,
+    "gathered13": 24,
+    "factor0": 26,
+    "part0": 30,
+    "g_codes2": 30,
+    "da_codes01": 32,
+    "da_bf11": 33,
+    "factor2": 34,
 }
+GATE_BANK = 7
 TURN_BANK = (0, 1, 2, 3, 6, 7, 0, 1)
 WORDS_BANK = (4, 5, 6, 7)
-GATE_BANK = 7
 DH_BANK = (4, 2, 3, 5, 0, 1, 2, 3)
-DX_BANK = (4, 5, 6, 7)
+DX_BANK = (4, 5, 6)
+LAST_DX_BANK = (7, 0)
 
 
 def tile_moe_bdx_glu_silu_kernel(
@@ -95,12 +96,12 @@ def tile_moe_bdx_glu_silu_kernel(
 
         planes = [new_tile(f"plane{t}", [P, T], F32) for t in range(PACK)]
         ident = new_tile("ident", [P, P], F32)
-        a1_late = new_tile("a1_late", [P, PACK, HALF], F32)
-        a3_late = new_tile("a3_late", [P, PACK, HALF], F32)
+        a1_half1 = new_tile("a1_half1", [P, PACK, HALF], F32)
+        a3_half1 = new_tile("a3_half1", [P, PACK, HALF], F32)
         a1_sb = [new_tile(f"a1_{e}", [P, PACK, C], F32)[:] for e in range(2)]
         a3_sb = [new_tile(f"a3_{e}", [P, PACK, C], F32)[:] for e in range(2)]
-        a1_sb = a1_sb + [a1_late[:, :, 0:C], a1_late[:, :, C:HALF]]
-        a3_sb = a3_sb + [a3_late[:, :, 0:C], a3_late[:, :, C:HALF]]
+        a1_sb = a1_sb + [a1_half1[:, :, 0:C], a1_half1[:, :, C:HALF]]
+        a3_sb = a3_sb + [a3_half1[:, :, 0:C], a3_half1[:, :, C:HALF]]
         w2_raw = new_tile("w2_raw", [P, E, 2 * H], U8)
         w2s_raw = new_tile("w2s_raw", [P, E, H], U8)
         w1_sb = new_tile("w1_sb", [P, E, 2 * K], U8)
@@ -137,7 +138,7 @@ def tile_moe_bdx_glu_silu_kernel(
         def load_expert(tiles, dram, e):
             nc.sync.dma_start(tiles[e], dram[:, :, e * C : (e + 1) * C])
 
-        def load_late(tile, dram):
+        def load_half1(tile, dram):
             nc.sync.dma_start(tile[:], dram[:, :, HALF:])
 
         load_plane(0)
@@ -152,12 +153,12 @@ def tile_moe_bdx_glu_silu_kernel(
         load_words(w2_raw, w2_words)
         load_expert(a3_sb, a3_4, 0)
         load_expert(a3_sb, a3_4, 1)
-        load_late(a1_late, a1_4)
+        load_half1(a1_half1, a1_4)
         load_words(w1_sb, w1_words)
         load_words(w3_sb, w3_words)
         load_scales(w1s, w1_scales)
         load_scales(w3s, w3_scales)
-        load_late(a3_late, a3_4)
+        load_half1(a3_half1, a3_4)
 
         w2_perm, w2s_perm = {}, {}
 
@@ -168,9 +169,9 @@ def tile_moe_bdx_glu_silu_kernel(
                 w2_raw[:, 2 * h : 2 * h + 2].bitcast(U16).rearrange("p e (m t) -> p e t m", t=PACK),
             )
 
-        def permute_scales(h, engine):
+        def permute_scales(h):
             w2s_perm[h] = new_tile(f"w2s_perm{h}", [P, 2, H], U8)
-            engine.tensor_copy(
+            nc.gpsimd.tensor_copy(
                 w2s_perm[h][:].rearrange("p e (t m) -> p e t m", t=PACK),
                 w2s_raw[:, 2 * h : 2 * h + 2].rearrange("p e (m t) -> p e t m", t=PACK),
             )
@@ -213,12 +214,12 @@ def tile_moe_bdx_glu_silu_kernel(
 
         g_bf, g_codes = {}, {}
         g_scales = new_tile("g_scales", [P, S], U8)
-        packed_late = new_tile("packed_late", [P, 2, 2, P, 2], F32)
+        packed_half1 = new_tile("packed_half1", [P, 2, 2, P, 2], F32)
         packed = [new_tile(f"packed{e}", [P, 2, P, 2], F32)[:] for e in range(2)]
-        packed = packed + [packed_late[:, 0], packed_late[:, 1]]
+        packed = packed + [packed_half1[:, 0], packed_half1[:, 1]]
         g_bf[0] = packed[0].rearrange("p c s u -> p (c s u)").bitcast(BF16)
         g_bf[1] = packed[1].rearrange("p c s u -> p (c s u)").bitcast(BF16)
-        g_bf[2] = packed_late[:].rearrange("p e c s u -> p (e c s u)").bitcast(BF16)
+        g_bf[2] = packed_half1[:].rearrange("p e c s u -> p (e c s u)").bitcast(BF16)
 
         def pack_g(e):
             words = bank(f"words{e}", [P, 2, 2, P], WORDS_BANK[e])
@@ -235,7 +236,7 @@ def tile_moe_bdx_glu_silu_kernel(
             for e in range(count):
                 g_codes[first + e] = codes[:, e * C : (e + 1) * C]
 
-        neg_sb, silu_sb, sig_sb, gated_a3, part, dh = {}, {}, {}, {}, {}, {}
+        neg_sb, silu_sb, tanh_sb, factor, part, dh = {}, {}, {}, {}, {}, {}
 
         def act_neg(e):
             neg_sb[e] = new_tile(f"neg{e}", [P, PACK, C], F32)
@@ -252,35 +253,35 @@ def tile_moe_bdx_glu_silu_kernel(
             nc.scalar.activation(walk_packed(silu_sb[e, c]), walk_planar(a1_sb[e][:, :, block_cols(c)]), ACT.Silu)
 
         def act_tanh(e):
-            sig_sb[e] = new_tile(f"sig{e}", [P, PACK, C], F32)
-            nc.scalar.activation(sig_sb[e][:], a1_sb[e], ACT.Tanh, scale=-0.5)
+            tanh_sb[e] = new_tile(f"tanh{e}", [P, PACK, C], F32)
+            nc.scalar.activation(tanh_sb[e][:], a1_sb[e], ACT.Tanh, scale=-0.5)
 
-        def act_sig(e):
-            nc.scalar.activation(sig_sb[e][:], sig_sb[e][:], ACT.Identity, bias=-1.0)
+        def shift_tanh_scalar(e):
+            nc.scalar.activation(tanh_sb[e][:], tanh_sb[e][:], ACT.Identity, bias=-1.0)
 
-        def shift_tanh(e):
-            nc.gpsimd.tensor_scalar(sig_sb[e][:], sig_sb[e][:], 1.0, -1.0, ALU.mult, ALU.add)
+        def shift_tanh_gpsimd(e):
+            nc.gpsimd.tensor_scalar(tanh_sb[e][:], tanh_sb[e][:], 1.0, -1.0, ALU.mult, ALU.add)
 
-        def make_gated_a3(e):
-            gated_a3[e] = new_tile(f"gated_a3_{e}", [P, PACK, C], F32)
-            nc.gpsimd.tensor_tensor(gated_a3[e][:], sig_sb[e][:], a3_sb[e], ALU.mult)
+        def factor_gpsimd(e):
+            factor[e] = new_tile(f"factor{e}", [P, PACK, C], F32)
+            nc.gpsimd.tensor_tensor(factor[e][:], tanh_sb[e][:], a3_sb[e], ALU.mult)
 
-        def make_factor(e):
-            gated_a3[e] = new_tile(f"gated_a3_{e}", [P, PACK, C], F32)
-            nc.vector.scalar_tensor_tensor(gated_a3[e][:], sig_sb[e][:], 1.0, a3_sb[e], ALU.subtract, ALU.mult)
+        def factor_vector(e):
+            factor[e] = new_tile(f"factor{e}", [P, PACK, C], F32)
+            nc.vector.scalar_tensor_tensor(factor[e][:], tanh_sb[e][:], 1.0, a3_sb[e], ALU.subtract, ALU.mult)
 
         da_bf = {(e, i): new_tile(f"da_bf{e}{i}", [P, C, PACK], BF16) for e in range(E) for i in range(2)}
         da_scales = [new_tile(f"da_scales{e}", [P, 2, C], U8) for e in range(E)]
         da_codes = {}
 
         def make_part(e, c):
-            h, k = divmod(e, 2)
+            h, within = divmod(e, 2)
             dh[e, c] = bank(f"dh{e}{c}", [P, PACK, P], DH_BANK[2 * e + c])
             for t in range(PACK):
                 nc.tensor.matmul_mx(
                     out=dh[e, c][:, t, :],
-                    lhsT=w2_perm[h][:, k, 2 * P * t : 2 * P * (t + 1)].bitcast(FP4X4),
-                    lhsT_scale=w2s_perm[h][:, k, P * t : P * (t + 1)],
+                    lhsT=w2_perm[h][:, within, 2 * P * t : 2 * P * (t + 1)].bitcast(FP4X4),
+                    lhsT_scale=w2s_perm[h][:, within, P * t : P * (t + 1)],
                     rhs=g_codes[e][:, block_cols(c)].bitcast(FP8X4),
                     rhs_scale=g_scales[:, e * C + c * P : e * C + (c + 1) * P],
                     start=True,
@@ -311,7 +312,7 @@ def tile_moe_bdx_glu_silu_kernel(
             nc.gpsimd.tensor_tensor(
                 walk_packed(da_bf[e, 0][:, cols, :]),
                 walk_planar(part[e][:, :, cols]),
-                walk_planar(gated_a3[e][:, :, cols]),
+                walk_planar(factor[e][:, :, cols]),
                 ALU.mult,
             )
 
@@ -324,32 +325,41 @@ def tile_moe_bdx_glu_silu_kernel(
                     in_=da_bf[e, i][:].rearrange("p n j -> p (n j)"),
                 )
 
-        dx, dx_sb = {}, {}
+        dx_both, dx, dx_sb = {}, {}, {}
+
+        def project_rows(e, b):
+            for c in range(2):
+                for i, (w, ws) in enumerate(((w1_sb, w1s), (w3_sb, w3s))):
+                    nc.tensor.matmul_mx(
+                        out=dx[e, b][:, block_cols(c)],
+                        lhsT=w[:, e, 2 * P * b : 2 * P * (b + 1)].bitcast(FP4X4),
+                        lhsT_scale=ws[:, e, P * b : P * (b + 1)],
+                        rhs=da_codes[e, i][:, block_cols(c)].bitcast(FP8X4),
+                        rhs_scale=da_scales[e][:, i, block_cols(c)],
+                        start=(i == 0),
+                        stop=(i == 1),
+                    )
 
         def project(e):
-            dx[e] = bank(f"dx{e}", [P, K // P, C], DX_BANK[e])
+            dx_both[e] = bank(f"dx{e}", [P, K // P, C], DX_BANK[e])
             for b in range(K // P):
-                for c in range(2):
-                    for i, (w, ws) in enumerate(((w1_sb, w1s), (w3_sb, w3s))):
-                        nc.tensor.matmul_mx(
-                            out=dx[e][:, b, block_cols(c)],
-                            lhsT=w[:, e, 2 * P * b : 2 * P * (b + 1)].bitcast(FP4X4),
-                            lhsT_scale=ws[:, e, P * b : P * (b + 1)],
-                            rhs=da_codes[e, i][:, block_cols(c)].bitcast(FP8X4),
-                            rhs_scale=da_scales[e][:, i, block_cols(c)],
-                            start=(i == 0),
-                            stop=(i == 1),
-                        )
+                dx[e, b] = dx_both[e][:, b, :]
+                project_rows(e, b)
+
+        def project_last(e):
+            for b in range(K // P):
+                dx[e, b] = bank(f"dx{e}{b}", [P, C], LAST_DX_BANK[b])[:]
+                project_rows(e, b)
 
         def copy_dx(e):
             both = new_tile(f"dx_sb{e}", [P, K // P, C], F32)
-            nc.scalar.activation(both[:], dx[e][:], ACT.Copy, scale=0.5)
+            nc.scalar.activation(both[:], dx_both[e][:], ACT.Copy, scale=0.5)
             for b in range(K // P):
                 dx_sb[e, b] = both[:, b, :]
 
         def copy_dx_rows(e, b):
             dx_sb[e, b] = new_tile(f"dx_sb{e}{b}", [P, C], F32)[:]
-            nc.scalar.activation(dx_sb[e, b], dx[e][:, b, :], ACT.Copy, scale=0.5)
+            nc.scalar.activation(dx_sb[e, b], dx[e, b], ACT.Copy, scale=0.5)
 
         def scatter(e, b):
             nc.vector.tensor_copy(win[b][:].indirect(entries(e * C, C)), dx_sb[e, b])
@@ -357,18 +367,18 @@ def tile_moe_bdx_glu_silu_kernel(
         def store(b):
             nc.sync.dma_start(out[b * P : (b + 1) * P, :], win[b][:])
 
-        whole = slice(0, C)
+        all_cols = slice(0, C)
 
         turn_gate()
-        permute_scales(0, nc.gpsimd)
-        permute_scales(1, nc.gpsimd)
+        permute_scales(0)
+        permute_scales(1)
         for b in range(K // P):
             nc.gpsimd.memset(win[b][:], 0.0)
         gather(0, 0)
         gather(1, 0)
         act_tanh(0)
         act_neg(0)
-        shift_tanh(0)
+        shift_tanh_gpsimd(0)
         act_silu(0)
         gather(0, 1)
         gather(1, 1)
@@ -382,14 +392,16 @@ def tile_moe_bdx_glu_silu_kernel(
         pack_g(0)
         gate_block(3)
         pack_g(1)
+
         permute_words(0)
         permute_words(1)
         gather(1, 3)
         gather(1, 2)
-        make_gated_a3(0)
+        factor_gpsimd(0)
         quantize_g(0, 1)
-        make_factor(1)
+        factor_vector(1)
         quantize_g(1, 1)
+
         make_part(0, 0)
         make_part(0, 1)
         make_da1(0, block_cols(0))
@@ -407,20 +419,22 @@ def tile_moe_bdx_glu_silu_kernel(
         make_part(1, 1)
         quantize_g(2, 2)
         quantize_da(0)
-        make_da1(1, whole)
+
+        make_da1(1, all_cols)
         make_da3(1, 0)
         make_da3(1, 1)
         act_neg(2)
         act_silu_block(2, 0)
         act_tanh(2)
-        act_sig(2)
+        shift_tanh_scalar(2)
         make_part(2, 0)
         make_part(2, 1)
         project(0)
         make_da3(2, 0)
         quantize_da(1)
-        make_gated_a3(2)
-        make_da1(2, whole)
+
+        factor_gpsimd(2)
+        make_da1(2, all_cols)
         copy_dx(0)
         act_silu_block(2, 1)
         scatter(0, 0)
@@ -430,14 +444,15 @@ def tile_moe_bdx_glu_silu_kernel(
         act_neg(3)
         act_silu_block(3, 0)
         act_tanh(3)
-        act_sig(3)
+        shift_tanh_scalar(3)
         make_part(3, 0)
         make_part(3, 1)
         make_da3(3, 0)
         quantize_da(2)
         project(2)
-        make_gated_a3(3)
-        make_da1(3, whole)
+
+        factor_gpsimd(3)
+        make_da1(3, all_cols)
         copy_dx(1)
         act_silu_block(3, 1)
         scatter(1, 0)
@@ -446,7 +461,8 @@ def tile_moe_bdx_glu_silu_kernel(
         copy_dx_rows(2, 0)
         scatter(2, 0)
         quantize_da(3)
-        project(3)
+
+        project_last(3)
         copy_dx_rows(2, 1)
         scatter(2, 1)
         for b in range(K // P):

@@ -24,51 +24,17 @@ E = 4
 C = 256
 S = E * C
 HALF = S // 2
-BLOCKS = S // P
 LIST_ROWS = 16
 KIB = 1024
 
 FLOPS = 2 * S * (N * H + 2 * H * K)
 BYTES = 4 * (N * T + 2 * H * S + K * T + S) + E * P * (2 * H + 4 * K) + E * 16 * (H + 2 * K) + 2 * 16 * S // 16
 
-
-SUCCEEDS = {
-    "silu1": "gated7",
-    "da_bf00": "packed1",
-    "da_codes20": "neg3",
-    "factor3": "da_bf21",
-    "silu31": "da_bf20",
-}
-PLACES = {
-    "packed_half1": 4,
-    "da_bf10": 7,
-    "da_bf01": 8,
-    "silu21": 7,
-    "part1": 10,
-    "da_codes11": 10,
-    "dx_sb0": 12,
-    "part2": 14,
-    "da_codes21": 14,
-    "dx_sb1": 16,
-    "part3": 18,
-    "da_codes31": 18,
-    "dx_sb21": 20,
-    "gathered12": 22,
-    "w2_raw": 23,
-    "gathered13": 24,
-    "factor0": 26,
-    "part0": 30,
-    "g_codes2": 30,
-    "da_codes01": 32,
-    "da_bf11": 33,
-    "factor2": 34,
-}
-GATE_BANK = 7
-TURN_BANK = (0, 1, 2, 3, 6, 7, 0, 1)
-WORDS_BANK = (4, 5, 6, 7)
-DH_BANK = (4, 2, 3, 5, 0, 1, 2, 3)
-DX_BANK = (4, 5, 6)
-LAST_DX_BANK = (7, 0)
+SUCCEEDS = {}
+GATE_BANK = (6, 7)
+DH_BANK = (0, 1, 2, 3, 0, 1, 2, 3)
+DX_BANK = (4, 5, 4)
+LAST_DX_BANK = (6, 7)
 
 
 def tile_moe_bdx_glu_silu_kernel(
@@ -79,11 +45,8 @@ def tile_moe_bdx_glu_silu_kernel(
         listp = ctx.enter_context(tc.tile_pool(name="listp", bufs=1))
         keep = ctx.enter_context(tc.tile_pool(name="keep", bufs=1))
         psum = ctx.enter_context(tc.psum_pool(name="psum", bufs=1))
-        shared = ctx.enter_context(tc.tile_pool(name="shared", bufs=1))
 
         def new_tile(name, shape, dtype):
-            if name in PLACES:
-                return shared.tile(shape, dtype, name=name, offset=PLACES[name] * KIB, align_bytes=64)
             return keep.tile(shape, dtype, name=name, tag=SUCCEEDS.get(name, name), align_bytes=64)
 
         def bank(name, shape, number):
@@ -96,30 +59,29 @@ def tile_moe_bdx_glu_silu_kernel(
 
         planes = [new_tile(f"plane{t}", [P, T], F32) for t in range(PACK)]
         ident = new_tile("ident", [P, P], F32)
+        zero = new_tile("zero", [P, 1], F32)
         a1_half1 = new_tile("a1_half1", [P, PACK, HALF], F32)
         a3_half1 = new_tile("a3_half1", [P, PACK, HALF], F32)
         a1_sb = [new_tile(f"a1_{e}", [P, PACK, C], F32)[:] for e in range(2)]
         a3_sb = [new_tile(f"a3_{e}", [P, PACK, C], F32)[:] for e in range(2)]
         a1_sb = a1_sb + [a1_half1[:, :, 0:C], a1_half1[:, :, C:HALF]]
         a3_sb = a3_sb + [a3_half1[:, :, 0:C], a3_half1[:, :, C:HALF]]
-        w2_raw = new_tile("w2_raw", [P, E, 2 * H], U8)
+        w2_raw = [new_tile(f"w2_raw{h}", [P, 2, 2 * H], U8) for h in range(2)]
         w2s_raw = new_tile("w2s_raw", [P, E, H], U8)
         w1_sb = new_tile("w1_sb", [P, E, 2 * K], U8)
         w3_sb = new_tile("w3_sb", [P, E, 2 * K], U8)
         w1s = new_tile("w1s", [P, E, K], U8)
         w3s = new_tile("w3s", [P, E, K], U8)
-        gate_rows = new_tile("gate_rows", [P, P], F32)
-        gate_col = new_tile("gate_col", [P, BLOCKS], F32)
+        gate_col = new_tile("gate_col", [P, 2, 8], F32)
         win = [new_tile(f"win{b}", [P, T], F32) for b in range(K // P)]
-
-        nc.gpsimd.memset(gate_rows[:], 0.0)
-        nc.gpsimd.memset(w2s_raw[:].bitcast(I32), 0)
-        make_identity(nc, ident[:])
-        nc.gpsimd.memset(w1s[:].bitcast(I32), 0)
-        nc.gpsimd.memset(w3s[:].bitcast(I32), 0)
 
         def load_words(tile, dram):
             nc.sync.dma_start(tile[:].bitcast(I32), dram.bitcast(I32)[:, 0].rearrange("e p b -> p e b"))
+
+        def load_w2(h):
+            nc.sync.dma_start(
+                w2_raw[h][:].bitcast(I32), w2_words.bitcast(I32)[2 * h : 2 * h + 2, 0].rearrange("e p b -> p e b")
+            )
 
         def load_scales(tile, dram):
             for q in range(4):
@@ -141,24 +103,8 @@ def tile_moe_bdx_glu_silu_kernel(
         def load_half1(tile, dram):
             nc.sync.dma_start(tile[:], dram[:, :, HALF:])
 
-        load_plane(0)
-        nc.sync.dma_start(offsets[:], offs)
-        load_expert(a1_sb, a1_4, 0)
-        nc.sync.dma_start(gate_rows[0:BLOCKS, :], gate[0, :].rearrange("(b n) -> b n", n=P))
-        load_plane(1)
-        load_scales(w2s_raw, w2_scales)
-        load_plane(2)
-        load_expert(a1_sb, a1_4, 1)
-        load_plane(3)
-        load_words(w2_raw, w2_words)
-        load_expert(a3_sb, a3_4, 0)
-        load_expert(a3_sb, a3_4, 1)
-        load_half1(a1_half1, a1_4)
-        load_words(w1_sb, w1_words)
-        load_words(w3_sb, w3_words)
-        load_scales(w1s, w1_scales)
-        load_scales(w3s, w3_scales)
-        load_half1(a3_half1, a3_4)
+        def load_gate():
+            nc.sync.dma_start(gate_col[:, :, 0:4], gate[0, :].rearrange("(h n i) -> n h i", h=2, i=4))
 
         w2_perm, w2s_perm = {}, {}
 
@@ -166,7 +112,7 @@ def tile_moe_bdx_glu_silu_kernel(
             w2_perm[h] = new_tile(f"w2_perm{h}", [P, 2, 2 * H], U8)
             nc.vector.tensor_copy(
                 w2_perm[h][:].bitcast(U16).rearrange("p e (t m) -> p e t m", t=PACK),
-                w2_raw[:, 2 * h : 2 * h + 2].bitcast(U16).rearrange("p e (m t) -> p e t m", t=PACK),
+                w2_raw[h][:].bitcast(U16).rearrange("p e (m t) -> p e t m", t=PACK),
             )
 
         def permute_scales(h):
@@ -185,56 +131,48 @@ def tile_moe_bdx_glu_silu_kernel(
         def block_cols(c):
             return slice(c * P, (c + 1) * P)
 
-        def turn_gate():
-            turned = bank("turned", [P, P], GATE_BANK)
-            nc.tensor.transpose(turned[:], gate_rows[:], ident[:])
-            nc.scalar.copy(gate_col[:], turned[:, 0:BLOCKS])
+        all_cols = slice(0, C)
+        gate_wide = {}
 
-        gathered = {}
+        def spread_gate(h):
+            gate_wide[h] = bank(f"gate_wide{h}", [P, 4, P], GATE_BANK[h])
+            for i in range(4):
+                nc.tensor.transpose(gate_wide[h][:, i, :], gate_col[:, h, i : i + 1].to_broadcast([P, P]), ident[:])
 
-        def gather(h, t):
-            gathered[h, t] = new_tile(f"gathered{h}{t}", [P, HALF], F32)
-            nc.vector.tensor_copy(gathered[h, t][:], planes[t][:].indirect(entries(h * HALF, HALF)))
+        gathered = [new_tile(f"gathered{h}", [P, PACK, HALF], F32) for h in range(2)]
 
-        pairs = {}
+        def gather_operands(t, first, count):
+            h, col = divmod(first, HALF)
+            return gathered[h][:, t, col : col + count], planes[t][:].indirect(entries(first, count))
 
-        def gate_block(block):
-            h, first = divmod(block * P, HALF)
-            by_slot = bank(f"by_slot{block}", [P, PACK, P], TURN_BANK[block])
-            for t in range(PACK):
-                nc.tensor.transpose(by_slot[:, t, :], gathered[h, t][:, first : first + P], ident[:])
-            gated = new_tile(f"gated{block}", [P, 2, P, 2], BF16)
-            nc.scalar.activation(
-                gated[:],
-                by_slot[:].rearrange("s (u v) p -> s u p v", u=2),
-                ACT.Copy,
-                scale=gate_col[:, block : block + 1],
-            )
-            pairs[block] = gated[:].rearrange("s u p v -> s (u p v)").bitcast(F32)
+        def gather_vector(t, first, count):
+            nc.vector.tensor_copy(*gather_operands(t, first, count))
+
+        def gather_scalar(t, first, count):
+            nc.scalar.activation(*gather_operands(t, first, count), ACT.Copy)
 
         g_bf, g_codes = {}, {}
         g_scales = new_tile("g_scales", [P, S], U8)
-        packed_half1 = new_tile("packed_half1", [P, 2, 2, P, 2], F32)
-        packed = [new_tile(f"packed{e}", [P, 2, P, 2], F32)[:] for e in range(2)]
-        packed = packed + [packed_half1[:, 0], packed_half1[:, 1]]
-        g_bf[0] = packed[0].rearrange("p c s u -> p (c s u)").bitcast(BF16)
-        g_bf[1] = packed[1].rearrange("p c s u -> p (c s u)").bitcast(BF16)
-        g_bf[2] = packed_half1[:].rearrange("p e c s u -> p (e c s u)").bitcast(BF16)
 
-        def pack_g(e):
-            words = bank(f"words{e}", [P, 2, 2, P], WORDS_BANK[e])
-            for c in range(2):
-                for u in range(2):
-                    nc.tensor.transpose(words[:, c, u, :], pairs[2 * e + c][:, u * P : (u + 1) * P], ident[:])
-            nc.scalar.copy(packed[e], words[:].rearrange("p c u s -> p c s u"))
-
-        def quantize_g(first, count):
-            codes = new_tile(f"g_codes{first}", [P, count * C], U32)
-            nc.vector.quantize_mx(
-                out=codes[:].bitcast(FP8X4), scales=g_scales[:, first * C : (first + count) * C], in_=g_bf[first]
+        def gate_g(e):
+            h, within = divmod(e, 2)
+            g_bf[e] = new_tile(f"g_bf{e}", [P, C, PACK], BF16)
+            groups = C // 4
+            gates = gate_wide[h][:, :, within * groups : (within + 1) * groups].rearrange("p i c -> p c i")
+            nc.vector.tensor_tensor(
+                walk_packed(g_bf[e][:]),
+                walk_planar(gathered[h][:, :, within * C : (within + 1) * C]),
+                gates.unsqueeze(2).broadcast_to([P, groups, PACK, 4]),
+                ALU.mult,
             )
-            for e in range(count):
-                g_codes[first + e] = codes[:, e * C : (e + 1) * C]
+
+        def quantize_g(e):
+            g_codes[e] = new_tile(f"g_codes{e}", [P, C], U32)
+            nc.vector.quantize_mx(
+                out=g_codes[e][:].bitcast(FP8X4),
+                scales=g_scales[:, e * C : (e + 1) * C],
+                in_=g_bf[e][:].rearrange("p n j -> p (n j)"),
+            )
 
         neg_sb, silu_sb, tanh_sb, factor, part, dh = {}, {}, {}, {}, {}, {}
 
@@ -243,102 +181,88 @@ def tile_moe_bdx_glu_silu_kernel(
             nc.scalar.activation(neg_sb[e][:], a1_sb[e], ACT.Silu, scale=-1.0)
 
         def act_silu(e):
-            both = new_tile(f"silu{e}", [P, C, PACK], F32)
-            nc.scalar.activation(walk_packed(both[:]), walk_planar(a1_sb[e]), ACT.Silu)
-            for c in range(2):
-                silu_sb[e, c] = both[:, block_cols(c), :]
-
-        def act_silu_block(e, c):
-            silu_sb[e, c] = new_tile(f"silu{e}{c}", [P, P, PACK], F32)[:]
-            nc.scalar.activation(walk_packed(silu_sb[e, c]), walk_planar(a1_sb[e][:, :, block_cols(c)]), ACT.Silu)
+            silu_sb[e] = new_tile(f"silu{e}", [P, C, PACK], F32)
+            nc.scalar.activation(walk_packed(silu_sb[e][:]), walk_planar(a1_sb[e]), ACT.Silu)
 
         def act_tanh(e):
             tanh_sb[e] = new_tile(f"tanh{e}", [P, PACK, C], F32)
             nc.scalar.activation(tanh_sb[e][:], a1_sb[e], ACT.Tanh, scale=-0.5)
 
-        def shift_tanh_scalar(e):
-            nc.scalar.activation(tanh_sb[e][:], tanh_sb[e][:], ACT.Identity, bias=-1.0)
-
-        def shift_tanh_gpsimd(e):
-            nc.gpsimd.tensor_scalar(tanh_sb[e][:], tanh_sb[e][:], 1.0, -1.0, ALU.mult, ALU.add)
-
-        def factor_gpsimd(e):
-            factor[e] = new_tile(f"factor{e}", [P, PACK, C], F32)
-            nc.gpsimd.tensor_tensor(factor[e][:], tanh_sb[e][:], a3_sb[e], ALU.mult)
-
         def factor_vector(e):
             factor[e] = new_tile(f"factor{e}", [P, PACK, C], F32)
             nc.vector.scalar_tensor_tensor(factor[e][:], tanh_sb[e][:], 1.0, a3_sb[e], ALU.subtract, ALU.mult)
 
-        da_bf = {(e, i): new_tile(f"da_bf{e}{i}", [P, C, PACK], BF16) for e in range(E) for i in range(2)}
-        da_scales = [new_tile(f"da_scales{e}", [P, 2, C], U8) for e in range(E)]
-        da_codes = {}
+        da_bf = [new_tile(f"da_bf{e}", [P, 2, C, PACK], BF16) for e in range(E)]
+        da_scales, da_codes = {}, {}
 
-        def make_part(e, c):
+        def make_dh(e):
             h, within = divmod(e, 2)
-            dh[e, c] = bank(f"dh{e}{c}", [P, PACK, P], DH_BANK[2 * e + c])
-            for t in range(PACK):
-                nc.tensor.matmul_mx(
-                    out=dh[e, c][:, t, :],
-                    lhsT=w2_perm[h][:, within, 2 * P * t : 2 * P * (t + 1)].bitcast(FP4X4),
-                    lhsT_scale=w2s_perm[h][:, within, P * t : P * (t + 1)],
-                    rhs=g_codes[e][:, block_cols(c)].bitcast(FP8X4),
-                    rhs_scale=g_scales[:, e * C + c * P : e * C + (c + 1) * P],
-                    start=True,
-                    stop=True,
+            for c in range(2):
+                dh[e, c] = bank(f"dh{e}{c}", [P, PACK, P], DH_BANK[2 * e + c])
+                for t in range(PACK):
+                    nc.tensor.matmul_mx(
+                        out=dh[e, c][:, t, :],
+                        lhsT=w2_perm[h][:, within, 2 * P * t : 2 * P * (t + 1)].bitcast(FP4X4),
+                        lhsT_scale=w2s_perm[h][:, within, P * t : P * (t + 1)],
+                        rhs=g_codes[e][:, block_cols(c)].bitcast(FP8X4),
+                        rhs_scale=g_scales[:, e * C + c * P : e * C + (c + 1) * P],
+                        start=True,
+                        stop=True,
+                    )
+
+        def make_part(e):
+            part[e] = new_tile(f"part{e}", [P, PACK, C], F32)
+            for c in range(2):
+                nc.vector.scalar_tensor_tensor(
+                    part[e][:, :, block_cols(c)],
+                    neg_sb[e][:, :, block_cols(c)],
+                    1.0,
+                    dh[e, c][:],
+                    ALU.subtract,
+                    ALU.mult,
                 )
-            if c == 0:
-                part[e] = new_tile(f"part{e}", [P, PACK, C], F32)
-            nc.vector.scalar_tensor_tensor(
-                part[e][:, :, block_cols(c)],
-                neg_sb[e][:, :, block_cols(c)],
-                1.0,
-                dh[e, c][:],
-                ALU.subtract,
-                ALU.mult,
-            )
 
-        def make_da3(e, c):
-            nc.vector.scalar_tensor_tensor(
-                da_bf[e, 1][:, block_cols(c), :],
-                dh[e, c][:].rearrange("p j n -> p n j"),
-                2.0,
-                silu_sb[e, c],
-                ALU.mult,
-                ALU.mult,
-            )
+        def make_da3(e):
+            for c in range(2):
+                nc.vector.scalar_tensor_tensor(
+                    da_bf[e][:, 1, block_cols(c), :],
+                    dh[e, c][:].rearrange("p j n -> p n j"),
+                    2.0,
+                    silu_sb[e][:, block_cols(c), :],
+                    ALU.mult,
+                    ALU.mult,
+                )
 
-        def make_da1(e, cols):
-            nc.gpsimd.tensor_tensor(
-                walk_packed(da_bf[e, 0][:, cols, :]),
+        def make_da1(engine, e, cols):
+            engine.tensor_tensor(
+                walk_packed(da_bf[e][:, 0, cols, :]),
                 walk_planar(part[e][:, :, cols]),
                 walk_planar(factor[e][:, :, cols]),
                 ALU.mult,
             )
 
         def quantize_da(e):
-            for i in range(2):
-                da_codes[e, i] = new_tile(f"da_codes{e}{i}", [P, C], U32)
-                nc.vector.quantize_mx(
-                    out=da_codes[e, i][:].bitcast(FP8X4),
-                    scales=da_scales[e][:, i, :],
-                    in_=da_bf[e, i][:].rearrange("p n j -> p (n j)"),
-                )
+            da_codes[e] = new_tile(f"da_codes{e}", [P, 2, C], U32)
+            da_scales[e] = new_tile(f"da_scales{e}", [P, 2, C], U8)
+            nc.vector.quantize_mx(
+                out=da_codes[e][:].rearrange("p i n -> p (i n)").bitcast(FP8X4),
+                scales=da_scales[e][:].rearrange("p i n -> p (i n)"),
+                in_=da_bf[e][:].rearrange("p i n j -> p (i n j)"),
+            )
 
         dx_both, dx, dx_sb = {}, {}, {}
 
         def project_rows(e, b):
-            for c in range(2):
-                for i, (w, ws) in enumerate(((w1_sb, w1s), (w3_sb, w3s))):
-                    nc.tensor.matmul_mx(
-                        out=dx[e, b][:, block_cols(c)],
-                        lhsT=w[:, e, 2 * P * b : 2 * P * (b + 1)].bitcast(FP4X4),
-                        lhsT_scale=ws[:, e, P * b : P * (b + 1)],
-                        rhs=da_codes[e, i][:, block_cols(c)].bitcast(FP8X4),
-                        rhs_scale=da_scales[e][:, i, block_cols(c)],
-                        start=(i == 0),
-                        stop=(i == 1),
-                    )
+            for i, (w, ws) in enumerate(((w1_sb, w1s), (w3_sb, w3s))):
+                nc.tensor.matmul_mx(
+                    out=dx[e, b],
+                    lhsT=w[:, e, 2 * P * b : 2 * P * (b + 1)].bitcast(FP4X4),
+                    lhsT_scale=ws[:, e, P * b : P * (b + 1)],
+                    rhs=da_codes[e][:, i, :].bitcast(FP8X4),
+                    rhs_scale=da_scales[e][:, i, :],
+                    start=(i == 0),
+                    stop=(i == 1),
+                )
 
         def project(e):
             dx_both[e] = bank(f"dx{e}", [P, K // P, C], DX_BANK[e])
@@ -361,112 +285,122 @@ def tile_moe_bdx_glu_silu_kernel(
             dx_sb[e, b] = new_tile(f"dx_sb{e}{b}", [P, C], F32)[:]
             nc.scalar.activation(dx_sb[e, b], dx[e, b], ACT.Copy, scale=0.5)
 
-        def scatter(e, b):
+        def scatter_vector(e, b):
             nc.vector.tensor_copy(win[b][:].indirect(entries(e * C, C)), dx_sb[e, b])
+
+        def scatter_scalar(e, b):
+            nc.scalar.activation(win[b][:].indirect(entries(e * C, C)), dx_sb[e, b], ACT.Copy)
 
         def store(b):
             nc.sync.dma_start(out[b * P : (b + 1) * P, :], win[b][:])
 
-        all_cols = slice(0, C)
 
-        turn_gate()
+        nc.gpsimd.memset(zero[:], 0.0)
+        nc.gpsimd.memset(w2s_raw[:].bitcast(I32), 0)
+        make_identity(nc, ident[:])
+        nc.gpsimd.memset(w1s[:].bitcast(I32), 0)
+        nc.gpsimd.memset(w3s[:].bitcast(I32), 0)
+        nc.gpsimd.memset(win[0][:], 0.0)
+        nc.scalar.activation(win[1][:], zero[:].to_broadcast([P, T]), ACT.Silu)
+
+        load_plane(0)
+        nc.sync.dma_start(offsets[:], offs)
+        load_gate()
+        load_plane(1)
+        load_plane(2)
+        load_scales(w2s_raw, w2_scales)
+        load_plane(3)
+        load_w2(0)
+        load_expert(a1_sb, a1_4, 0)
+        load_expert(a3_sb, a3_4, 0)
+        load_expert(a1_sb, a1_4, 1)
+        load_expert(a3_sb, a3_4, 1)
+        load_w2(1)
+        load_half1(a1_half1, a1_4)
+        load_words(w1_sb, w1_words)
+        load_words(w3_sb, w3_words)
+        load_scales(w1s, w1_scales)
+        load_scales(w3s, w3_scales)
+        load_half1(a3_half1, a3_4)
+
+        spread_gate(0)
+        spread_gate(1)
         permute_scales(0)
         permute_scales(1)
-        for b in range(K // P):
-            nc.gpsimd.memset(win[b][:], 0.0)
-        gather(0, 0)
-        gather(1, 0)
+        for t in range(PACK - 1):
+            gather_vector(t, 0, HALF)
+            gather_scalar(t, HALF, HALF)
+        gather_vector(PACK - 1, 0, C)
+        gather_scalar(PACK - 1, C, C)
+        gather_scalar(PACK - 1, HALF, HALF)
+
+        gate_g(0)
+        permute_words(0)
+        quantize_g(0)
+        make_dh(0)
         act_tanh(0)
         act_neg(0)
-        shift_tanh_gpsimd(0)
         act_silu(0)
-        gather(0, 1)
-        gather(1, 1)
-        gather(0, 2)
-        act_tanh(1)
+        gate_g(1)
+        factor_vector(0)
+        quantize_g(1)
+        make_dh(1)
+        make_part(0)
+
+        make_da1(nc.gpsimd, 0, all_cols)
         act_neg(1)
-        gather(0, 3)
-        gate_block(0)
-        gate_block(1)
-        gate_block(2)
-        pack_g(0)
-        gate_block(3)
-        pack_g(1)
-
-        permute_words(0)
-        permute_words(1)
-        gather(1, 3)
-        gather(1, 2)
-        factor_gpsimd(0)
-        quantize_g(0, 1)
-        factor_vector(1)
-        quantize_g(1, 1)
-
-        make_part(0, 0)
-        make_part(0, 1)
-        make_da1(0, block_cols(0))
-        make_da1(0, block_cols(1))
-        make_da3(0, 0)
-        make_da3(0, 1)
-        gate_block(4)
-        gate_block(5)
-        gate_block(6)
-        pack_g(2)
-        gate_block(7)
-        pack_g(3)
+        act_tanh(1)
         act_silu(1)
-        make_part(1, 0)
-        make_part(1, 1)
-        quantize_g(2, 2)
+        make_da3(0)
+        gate_g(2)
+        make_part(1)
+        permute_words(1)
+        quantize_g(2)
+        make_dh(2)
         quantize_da(0)
-
-        make_da1(1, all_cols)
-        make_da3(1, 0)
-        make_da3(1, 1)
-        act_neg(2)
-        act_silu_block(2, 0)
-        act_tanh(2)
-        shift_tanh_scalar(2)
-        make_part(2, 0)
-        make_part(2, 1)
         project(0)
-        make_da3(2, 0)
-        quantize_da(1)
+        factor_vector(1)
 
-        factor_gpsimd(2)
-        make_da1(2, all_cols)
-        copy_dx(0)
-        act_silu_block(2, 1)
-        scatter(0, 0)
-        make_da3(2, 1)
-        scatter(0, 1)
-        project(1)
+        make_da1(nc.gpsimd, 1, all_cols)
+        act_neg(2)
+        act_tanh(2)
+        act_silu(2)
         act_neg(3)
-        act_silu_block(3, 0)
         act_tanh(3)
-        shift_tanh_scalar(3)
-        make_part(3, 0)
-        make_part(3, 1)
-        make_da3(3, 0)
+        act_silu(3)
+        copy_dx(0)
+        scatter_scalar(0, 0)
+        scatter_scalar(0, 1)
+        make_da3(1)
+        gate_g(3)
+        make_part(2)
+        quantize_g(3)
+        make_dh(3)
+        quantize_da(1)
+        project(1)
+        factor_vector(2)
+
+        make_da1(nc.gpsimd, 2, all_cols)
+        copy_dx(1)
+        scatter_scalar(1, 0)
+        scatter_scalar(1, 1)
+        make_da3(2)
+        make_part(3)
         quantize_da(2)
         project(2)
+        factor_vector(3)
 
-        factor_gpsimd(3)
-        make_da1(3, all_cols)
-        copy_dx(1)
-        act_silu_block(3, 1)
-        scatter(1, 0)
-        make_da3(3, 1)
-        scatter(1, 1)
-        copy_dx_rows(2, 0)
-        scatter(2, 0)
+        make_da1(nc.gpsimd, 3, block_cols(0))
+        copy_dx(2)
+        scatter_scalar(2, 1)
+        make_da3(3)
+        make_da1(nc.vector, 3, block_cols(1))
         quantize_da(3)
-
         project_last(3)
-        copy_dx_rows(2, 1)
-        scatter(2, 1)
-        for b in range(K // P):
-            copy_dx_rows(3, b)
-        for b in range(K // P):
-            scatter(3, b)
-            store(b)
+        scatter_vector(2, 0)
+        copy_dx_rows(3, 0)
+        copy_dx_rows(3, 1)
+        scatter_vector(3, 0)
+        scatter_scalar(3, 1)
+        store(1)
+        store(0)

@@ -30,11 +30,12 @@ KIB = 1024
 FLOPS = 2 * S * (N * H + 2 * H * K)
 BYTES = 4 * (N * T + 2 * H * S + K * T + S) + E * P * (2 * H + 4 * K) + E * 16 * (H + 2 * K) + 2 * 16 * S // 16
 
-SUCCEEDS = {}
+SUCCEEDS = {"da_bf1": "da_bf0", "part2": "part0", "dx_sb0": "a1_half1", "dx_sb20": "tanh3", "dx_sb1": "a1_half1", "dx_sb21": "a1_half1"}
+PLACES = {"factor0": 0, "g_bf3": 0, "factor1": 2, "factor2": 4, "factor3": 6, "da_bf2": 10, "tanh2": 12, "part3": 14}
 GATE_BANK = (6, 7)
 DH_BANK = (0, 1, 2, 3, 0, 1, 2, 3)
-DX_BANK = (4, 5, 4)
-LAST_DX_BANK = (6, 7)
+DX_BANK = (4, 5)
+ROWS_DX_BANK = {(2, 0): 0, (2, 1): 1, (3, 0): 2, (3, 1): 3}
 
 
 def tile_moe_bdx_glu_silu_kernel(
@@ -46,7 +47,11 @@ def tile_moe_bdx_glu_silu_kernel(
         keep = ctx.enter_context(tc.tile_pool(name="keep", bufs=1))
         psum = ctx.enter_context(tc.psum_pool(name="psum", bufs=1))
 
+        shared = ctx.enter_context(tc.tile_pool(name="shared", bufs=1))
+
         def new_tile(name, shape, dtype):
+            if name in PLACES:
+                return shared.tile(shape, dtype, name=name, offset=PLACES[name] * KIB, align_bytes=64)
             return keep.tile(shape, dtype, name=name, tag=SUCCEEDS.get(name, name), align_bytes=64)
 
         def bank(name, shape, number):
@@ -83,9 +88,9 @@ def tile_moe_bdx_glu_silu_kernel(
                 w2_raw[h][:].bitcast(I32), w2_words.bitcast(I32)[2 * h : 2 * h + 2, 0].rearrange("e p b -> p e b")
             )
 
-        def load_scales(tile, dram):
+        def load_scales(queue, tile, dram):
             for q in range(4):
-                nc.sync.dma_start(
+                queue.dma_start(
                     tile[32 * q : 32 * q + 4].bitcast(I32),
                     dram.bitcast(I32)[:, 0, 4 * q : 4 * q + 4, :].rearrange("e f i -> f e i"),
                 )
@@ -108,9 +113,9 @@ def tile_moe_bdx_glu_silu_kernel(
 
         w2_perm, w2s_perm = {}, {}
 
-        def permute_words(h):
+        def permute_words(copy, h):
             w2_perm[h] = new_tile(f"w2_perm{h}", [P, 2, 2 * H], U8)
-            nc.vector.tensor_copy(
+            copy(
                 w2_perm[h][:].bitcast(U16).rearrange("p e (t m) -> p e t m", t=PACK),
                 w2_raw[h][:].bitcast(U16).rearrange("p e (m t) -> p e t m", t=PACK),
             )
@@ -192,8 +197,10 @@ def tile_moe_bdx_glu_silu_kernel(
             factor[e] = new_tile(f"factor{e}", [P, PACK, C], F32)
             nc.vector.scalar_tensor_tensor(factor[e][:], tanh_sb[e][:], 1.0, a3_sb[e], ALU.subtract, ALU.mult)
 
-        da_bf = [new_tile(f"da_bf{e}", [P, 2, C, PACK], BF16) for e in range(E)]
-        da_scales, da_codes = {}, {}
+        da_bf, da_scales, da_codes = {}, {}, {}
+
+        def new_da(e):
+            da_bf[e] = new_tile(f"da_bf{e}", [P, 2, C, PACK], BF16)
 
         def make_dh(e):
             h, within = divmod(e, 2)
@@ -270,9 +277,9 @@ def tile_moe_bdx_glu_silu_kernel(
                 dx[e, b] = dx_both[e][:, b, :]
                 project_rows(e, b)
 
-        def project_last(e):
-            for b in range(K // P):
-                dx[e, b] = bank(f"dx{e}{b}", [P, C], LAST_DX_BANK[b])[:]
+        def project_by_rows(e):
+            for b in reversed(range(K // P)):
+                dx[e, b] = bank(f"dx{e}{b}", [P, C], ROWS_DX_BANK[e, b])[:]
                 project_rows(e, b)
 
         def copy_dx(e):
@@ -285,6 +292,10 @@ def tile_moe_bdx_glu_silu_kernel(
             dx_sb[e, b] = new_tile(f"dx_sb{e}{b}", [P, C], F32)[:]
             nc.scalar.activation(dx_sb[e, b], dx[e, b], ACT.Copy, scale=0.5)
 
+        def copy_dx_rows_vector(e, b):
+            dx_sb[e, b] = new_tile(f"dx_sb{e}{b}", [P, C], F32)[:]
+            nc.vector.tensor_scalar(dx_sb[e, b], dx[e, b], 0.5, None, ALU.mult)
+
         def scatter_vector(e, b):
             nc.vector.tensor_copy(win[b][:].indirect(entries(e * C, C)), dx_sb[e, b])
 
@@ -295,20 +306,20 @@ def tile_moe_bdx_glu_silu_kernel(
             nc.sync.dma_start(out[b * P : (b + 1) * P, :], win[b][:])
 
 
-        nc.gpsimd.memset(zero[:], 0.0)
         nc.gpsimd.memset(w2s_raw[:].bitcast(I32), 0)
+        nc.vector.memset(zero[:], 0.0)
         make_identity(nc, ident[:])
         nc.gpsimd.memset(w1s[:].bitcast(I32), 0)
         nc.gpsimd.memset(w3s[:].bitcast(I32), 0)
-        nc.gpsimd.memset(win[0][:], 0.0)
-        nc.scalar.activation(win[1][:], zero[:].to_broadcast([P, T]), ACT.Silu)
+        nc.vector.memset(win[0][:], 0.0)
 
+        nc.scalar.activation(win[1][:], zero[:].to_broadcast([P, T]), ACT.Silu)
         load_plane(0)
         nc.sync.dma_start(offsets[:], offs)
-        load_gate()
         load_plane(1)
+        load_scales(nc.sync, w2s_raw, w2_scales)
         load_plane(2)
-        load_scales(w2s_raw, w2_scales)
+        load_gate()
         load_plane(3)
         load_w2(0)
         load_expert(a1_sb, a1_4, 0)
@@ -319,14 +330,14 @@ def tile_moe_bdx_glu_silu_kernel(
         load_half1(a1_half1, a1_4)
         load_words(w1_sb, w1_words)
         load_words(w3_sb, w3_words)
-        load_scales(w1s, w1_scales)
-        load_scales(w3s, w3_scales)
+        load_scales(nc.sync, w1s, w1_scales)
+        load_scales(nc.sync, w3s, w3_scales)
         load_half1(a3_half1, a3_4)
 
-        spread_gate(0)
-        spread_gate(1)
         permute_scales(0)
         permute_scales(1)
+        spread_gate(0)
+        spread_gate(1)
         for t in range(PACK - 1):
             gather_vector(t, 0, HALF)
             gather_scalar(t, HALF, HALF)
@@ -335,7 +346,7 @@ def tile_moe_bdx_glu_silu_kernel(
         gather_scalar(PACK - 1, HALF, HALF)
 
         gate_g(0)
-        permute_words(0)
+        permute_words(nc.vector.tensor_copy, 0)
         quantize_g(0)
         make_dh(0)
         act_tanh(0)
@@ -347,6 +358,7 @@ def tile_moe_bdx_glu_silu_kernel(
         make_dh(1)
         make_part(0)
 
+        new_da(0)
         make_da1(nc.gpsimd, 0, all_cols)
         act_neg(1)
         act_tanh(1)
@@ -354,13 +366,14 @@ def tile_moe_bdx_glu_silu_kernel(
         make_da3(0)
         gate_g(2)
         make_part(1)
-        permute_words(1)
+        permute_words(nc.vector.tensor_copy, 1)
         quantize_g(2)
         make_dh(2)
         quantize_da(0)
         project(0)
         factor_vector(1)
 
+        new_da(1)
         make_da1(nc.gpsimd, 1, all_cols)
         act_neg(2)
         act_tanh(2)
@@ -371,36 +384,38 @@ def tile_moe_bdx_glu_silu_kernel(
         copy_dx(0)
         scatter_scalar(0, 0)
         scatter_scalar(0, 1)
-        make_da3(1)
         gate_g(3)
+        make_da3(1)
         make_part(2)
-        quantize_g(3)
-        make_dh(3)
         quantize_da(1)
         project(1)
+        quantize_g(3)
+        make_dh(3)
         factor_vector(2)
 
+        new_da(2)
         make_da1(nc.gpsimd, 2, all_cols)
         copy_dx(1)
         scatter_scalar(1, 0)
         scatter_scalar(1, 1)
         make_da3(2)
         make_part(3)
+        new_da(3)
+        make_da3(3)
         quantize_da(2)
-        project(2)
+        project_by_rows(2)
         factor_vector(3)
 
-        make_da1(nc.gpsimd, 3, block_cols(0))
-        copy_dx(2)
+        copy_dx_rows(2, 1)
         scatter_scalar(2, 1)
-        make_da3(3)
-        make_da1(nc.vector, 3, block_cols(1))
+        make_da1(nc.vector, 3, all_cols)
+        copy_dx_rows_vector(2, 0)
         quantize_da(3)
-        project_last(3)
+        project_by_rows(3)
         scatter_vector(2, 0)
-        copy_dx_rows(3, 0)
         copy_dx_rows(3, 1)
-        scatter_vector(3, 0)
         scatter_scalar(3, 1)
+        copy_dx_rows_vector(3, 0)
+        scatter_vector(3, 0)
         store(1)
         store(0)

@@ -30,8 +30,9 @@ KIB = 1024
 FLOPS = 2 * S * (N * H + 2 * H * K)
 BYTES = 4 * (N * T + 2 * H * S + K * T + S) + E * P * (2 * H + 4 * K) + E * 16 * (H + 2 * K) + 2 * 16 * S // 16
 
-SUCCEEDS = {"da_bf1": "da_bf0", "part2": "part0", "dx_sb0": "a1_half1", "dx_sb20": "tanh3", "dx_sb1": "a1_half1", "dx_sb21": "a1_half1"}
-PLACES = {"factor0": 0, "g_bf3": 0, "factor1": 2, "factor2": 4, "factor3": 6, "da_bf2": 10, "tanh2": 12, "part3": 14}
+RUN = 2
+SUCCEEDS = {"part2": "a3_1", "da_codes0": "neg1", "g_codes3": "neg1", "da_codes1": "neg2", "da_bf3": "silu2", "dx_sb0": "a1_half1", "dx_sb1": "a1_half1", "dx_sb21": "a1_half1", "dx_sb20": "tanh3"}
+PLACES = {"factor0": 0, "factor1": 2, "factor2": 4, "factor3": 6, "da_bf2": 10, "tanh2": 12, "part3": 14, "da_bf1": 18, "tanh1": 20, "g_bf3": 22}
 GATE_BANK = (6, 7)
 DH_BANK = (0, 1, 2, 3, 0, 1, 2, 3)
 DX_BANK = (4, 5)
@@ -51,7 +52,7 @@ def tile_moe_bdx_glu_silu_kernel(
 
         def new_tile(name, shape, dtype):
             if name in PLACES:
-                return shared.tile(shape, dtype, name=name, offset=PLACES[name] * KIB, align_bytes=64)
+                return shared.tile(shape, dtype, name=name, offset=int(PLACES[name] * KIB), align_bytes=64)
             return keep.tile(shape, dtype, name=name, tag=SUCCEEDS.get(name, name), align_bytes=64)
 
         def bank(name, shape, number):
@@ -77,7 +78,7 @@ def tile_moe_bdx_glu_silu_kernel(
         w3_sb = new_tile("w3_sb", [P, E, 2 * K], U8)
         w1s = new_tile("w1s", [P, E, K], U8)
         w3s = new_tile("w3s", [P, E, K], U8)
-        gate_col = new_tile("gate_col", [P, 2, 8], F32)
+        gate_col = new_tile("gate_col", [P, E, 8], F32)
         win = [new_tile(f"win{b}", [P, T], F32) for b in range(K // P)]
 
         def load_words(tile, dram):
@@ -109,7 +110,7 @@ def tile_moe_bdx_glu_silu_kernel(
             nc.sync.dma_start(tile[:], dram[:, :, HALF:])
 
         def load_gate():
-            nc.sync.dma_start(gate_col[:, :, 0:4], gate[0, :].rearrange("(h n i) -> n h i", h=2, i=4))
+            nc.sync.dma_start(gate_col[:, :, 0:RUN], gate[0, :].rearrange("(e n i) -> n e i", e=E, i=RUN))
 
         w2_perm, w2s_perm = {}, {}
 
@@ -128,10 +129,10 @@ def tile_moe_bdx_glu_silu_kernel(
             )
 
         def walk_planar(ap):
-            return ap.rearrange("p j (c i) -> p c j i", i=4)
+            return ap.rearrange("p j (c i) -> p c j i", i=RUN)
 
         def walk_packed(ap):
-            return ap.rearrange("p (c i) j -> p c j i", i=4)
+            return ap.rearrange("p (c i) j -> p c j i", i=RUN)
 
         def block_cols(c):
             return slice(c * P, (c + 1) * P)
@@ -139,10 +140,12 @@ def tile_moe_bdx_glu_silu_kernel(
         all_cols = slice(0, C)
         gate_wide = {}
 
-        def spread_gate(h):
-            gate_wide[h] = bank(f"gate_wide{h}", [P, 4, P], GATE_BANK[h])
-            for i in range(4):
-                nc.tensor.transpose(gate_wide[h][:, i, :], gate_col[:, h, i : i + 1].to_broadcast([P, P]), ident[:])
+        def spread_gate(experts, number):
+            wide = bank(f"gate_wide{number}", [P, len(experts), RUN, P], number)
+            for slot, e in enumerate(experts):
+                gate_wide[e] = wide[:, slot].rearrange("p i c -> p c i")
+                for i in range(RUN):
+                    nc.tensor.transpose(wide[:, slot, i, :], gate_col[:, e, i : i + 1].to_broadcast([P, P]), ident[:])
 
         gathered = [new_tile(f"gathered{h}", [P, PACK, HALF], F32) for h in range(2)]
 
@@ -162,12 +165,10 @@ def tile_moe_bdx_glu_silu_kernel(
         def gate_g(e):
             h, within = divmod(e, 2)
             g_bf[e] = new_tile(f"g_bf{e}", [P, C, PACK], BF16)
-            groups = C // 4
-            gates = gate_wide[h][:, :, within * groups : (within + 1) * groups].rearrange("p i c -> p c i")
             nc.vector.tensor_tensor(
                 walk_packed(g_bf[e][:]),
                 walk_planar(gathered[h][:, :, within * C : (within + 1) * C]),
-                gates.unsqueeze(2).broadcast_to([P, groups, PACK, 4]),
+                gate_wide[e].unsqueeze(2).broadcast_to([P, C // RUN, PACK, RUN]),
                 ALU.mult,
             )
 
@@ -217,9 +218,10 @@ def tile_moe_bdx_glu_silu_kernel(
                         stop=True,
                     )
 
-        def make_part(e):
-            part[e] = new_tile(f"part{e}", [P, PACK, C], F32)
-            for c in range(2):
+        def make_part(e, blocks=(0, 1)):
+            if 0 in blocks:
+                part[e] = new_tile(f"part{e}", [P, PACK, C], F32)
+            for c in blocks:
                 nc.vector.scalar_tensor_tensor(
                     part[e][:, :, block_cols(c)],
                     neg_sb[e][:, :, block_cols(c)],
@@ -229,8 +231,8 @@ def tile_moe_bdx_glu_silu_kernel(
                     ALU.mult,
                 )
 
-        def make_da3(e):
-            for c in range(2):
+        def make_da3(e, blocks=(0, 1)):
+            for c in blocks:
                 nc.vector.scalar_tensor_tensor(
                     da_bf[e][:, 1, block_cols(c), :],
                     dh[e, c][:].rearrange("p j n -> p n j"),
@@ -321,8 +323,8 @@ def tile_moe_bdx_glu_silu_kernel(
         load_plane(2)
         load_gate()
         load_plane(3)
-        load_w2(0)
         load_expert(a1_sb, a1_4, 0)
+        load_w2(0)
         load_expert(a3_sb, a3_4, 0)
         load_expert(a1_sb, a1_4, 1)
         load_expert(a3_sb, a3_4, 1)
@@ -336,8 +338,8 @@ def tile_moe_bdx_glu_silu_kernel(
 
         permute_scales(0)
         permute_scales(1)
-        spread_gate(0)
-        spread_gate(1)
+        spread_gate((0, 1), GATE_BANK[0])
+        spread_gate((2, 3), GATE_BANK[1])
         for t in range(PACK - 1):
             gather_vector(t, 0, HALF)
             gather_scalar(t, HALF, HALF)
@@ -346,13 +348,13 @@ def tile_moe_bdx_glu_silu_kernel(
         gather_scalar(PACK - 1, HALF, HALF)
 
         gate_g(0)
+        gate_g(1)
         permute_words(nc.vector.tensor_copy, 0)
         quantize_g(0)
         make_dh(0)
         act_tanh(0)
         act_neg(0)
         act_silu(0)
-        gate_g(1)
         factor_vector(0)
         quantize_g(1)
         make_dh(1)
@@ -363,10 +365,10 @@ def tile_moe_bdx_glu_silu_kernel(
         act_neg(1)
         act_tanh(1)
         act_silu(1)
+        permute_words(nc.scalar.copy, 1)
         make_da3(0)
         gate_g(2)
         make_part(1)
-        permute_words(nc.vector.tensor_copy, 1)
         quantize_g(2)
         make_dh(2)
         quantize_da(0)
@@ -399,9 +401,10 @@ def tile_moe_bdx_glu_silu_kernel(
         scatter_scalar(1, 0)
         scatter_scalar(1, 1)
         make_da3(2)
-        make_part(3)
         new_da(3)
-        make_da3(3)
+        for c in range(2):
+            make_part(3, (c,))
+            make_da3(3, (c,))
         quantize_da(2)
         project_by_rows(2)
         factor_vector(3)

@@ -30,8 +30,7 @@ KIB = 1024
 FLOPS = 2 * S * (N * H + 2 * H * K)
 BYTES = 4 * (N * T + 2 * H * S + K * T + S) + E * P * (2 * H + 4 * K) + E * 16 * (H + 2 * K) + 2 * 16 * S // 16
 
-RUN = 2
-SUCCEEDS = {"part2": "a3_1", "da_codes0": "neg1", "g_codes3": "neg1", "da_codes1": "neg2", "da_bf3": "silu2", "dx_sb0": "a1_half1", "dx_sb1": "a1_half1", "dx_sb21": "a1_half1", "dx_sb20": "tanh3"}
+SUCCEEDS = {"g_bf2": "tanh0", "da_bf0": "a3_0", "part2": "a3_1", "da_codes0": "neg1", "g_codes3": "neg1", "da_codes1": "neg2", "da_bf3": "silu2", "dx_sb0": "a1_half1", "dx_sb1": "a1_half1", "dx_sb21": "a1_half1", "dx_sb20": "tanh3"}
 PLACES = {"factor0": 0, "factor1": 2, "factor2": 4, "factor3": 6, "da_bf2": 10, "tanh2": 12, "part3": 14, "da_bf1": 18, "tanh1": 20, "g_bf3": 22}
 GATE_BANK = (6, 7)
 DH_BANK = (0, 1, 2, 3, 0, 1, 2, 3)
@@ -52,7 +51,7 @@ def tile_moe_bdx_glu_silu_kernel(
 
         def new_tile(name, shape, dtype):
             if name in PLACES:
-                return shared.tile(shape, dtype, name=name, offset=int(PLACES[name] * KIB), align_bytes=64)
+                return shared.tile(shape, dtype, name=name, offset=PLACES[name] * KIB, align_bytes=64)
             return keep.tile(shape, dtype, name=name, tag=SUCCEEDS.get(name, name), align_bytes=64)
 
         def bank(name, shape, number):
@@ -78,7 +77,7 @@ def tile_moe_bdx_glu_silu_kernel(
         w3_sb = new_tile("w3_sb", [P, E, 2 * K], U8)
         w1s = new_tile("w1s", [P, E, K], U8)
         w3s = new_tile("w3s", [P, E, K], U8)
-        gate_col = new_tile("gate_col", [P, E, 8], F32)
+        gate_col = new_tile("gate_col", [P, 2, 8], F32)
         win = [new_tile(f"win{b}", [P, T], F32) for b in range(K // P)]
 
         def load_words(tile, dram):
@@ -110,7 +109,7 @@ def tile_moe_bdx_glu_silu_kernel(
             nc.sync.dma_start(tile[:], dram[:, :, HALF:])
 
         def load_gate():
-            nc.sync.dma_start(gate_col[:, :, 0:RUN], gate[0, :].rearrange("(e n i) -> n e i", e=E, i=RUN))
+            nc.scalar.dma_start(gate_col[:, :, 0:4], gate[0, :].rearrange("(h n i) -> n h i", h=2, i=4))
 
         w2_perm, w2s_perm = {}, {}
 
@@ -129,10 +128,10 @@ def tile_moe_bdx_glu_silu_kernel(
             )
 
         def walk_planar(ap):
-            return ap.rearrange("p j (c i) -> p c j i", i=RUN)
+            return ap.rearrange("p j (c i) -> p c j i", i=4)
 
         def walk_packed(ap):
-            return ap.rearrange("p (c i) j -> p c j i", i=RUN)
+            return ap.rearrange("p (c i) j -> p c j i", i=4)
 
         def block_cols(c):
             return slice(c * P, (c + 1) * P)
@@ -140,12 +139,10 @@ def tile_moe_bdx_glu_silu_kernel(
         all_cols = slice(0, C)
         gate_wide = {}
 
-        def spread_gate(experts, number):
-            wide = bank(f"gate_wide{number}", [P, len(experts), RUN, P], number)
-            for slot, e in enumerate(experts):
-                gate_wide[e] = wide[:, slot].rearrange("p i c -> p c i")
-                for i in range(RUN):
-                    nc.tensor.transpose(wide[:, slot, i, :], gate_col[:, e, i : i + 1].to_broadcast([P, P]), ident[:])
+        def spread_gate(h):
+            gate_wide[h] = bank(f"gate_wide{h}", [P, 4, P], GATE_BANK[h])
+            for i in range(4):
+                nc.tensor.transpose(gate_wide[h][:, i, :], gate_col[:, h, i : i + 1].to_broadcast([P, P]), ident[:])
 
         gathered = [new_tile(f"gathered{h}", [P, PACK, HALF], F32) for h in range(2)]
 
@@ -165,10 +162,12 @@ def tile_moe_bdx_glu_silu_kernel(
         def gate_g(e):
             h, within = divmod(e, 2)
             g_bf[e] = new_tile(f"g_bf{e}", [P, C, PACK], BF16)
+            groups = C // 4
+            gates = gate_wide[h][:, :, within * groups : (within + 1) * groups].rearrange("p i c -> p c i")
             nc.vector.tensor_tensor(
                 walk_packed(g_bf[e][:]),
                 walk_planar(gathered[h][:, :, within * C : (within + 1) * C]),
-                gate_wide[e].unsqueeze(2).broadcast_to([P, C // RUN, PACK, RUN]),
+                gates.unsqueeze(2).broadcast_to([P, groups, PACK, 4]),
                 ALU.mult,
             )
 
@@ -315,14 +314,14 @@ def tile_moe_bdx_glu_silu_kernel(
         nc.gpsimd.memset(w3s[:].bitcast(I32), 0)
         nc.vector.memset(win[0][:], 0.0)
 
+        load_gate()
         nc.scalar.activation(win[1][:], zero[:].to_broadcast([P, T]), ACT.Silu)
         load_plane(0)
         nc.sync.dma_start(offsets[:], offs)
         load_plane(1)
-        load_scales(nc.sync, w2s_raw, w2_scales)
         load_plane(2)
-        load_gate()
         load_plane(3)
+        load_scales(nc.sync, w2s_raw, w2_scales)
         load_expert(a1_sb, a1_4, 0)
         load_w2(0)
         load_expert(a3_sb, a3_4, 0)
@@ -338,8 +337,8 @@ def tile_moe_bdx_glu_silu_kernel(
 
         permute_scales(0)
         permute_scales(1)
-        spread_gate((0, 1), GATE_BANK[0])
-        spread_gate((2, 3), GATE_BANK[1])
+        spread_gate(0)
+        spread_gate(1)
         for t in range(PACK - 1):
             gather_vector(t, 0, HALF)
             gather_scalar(t, HALF, HALF)
@@ -365,10 +364,10 @@ def tile_moe_bdx_glu_silu_kernel(
         act_neg(1)
         act_tanh(1)
         act_silu(1)
-        permute_words(nc.scalar.copy, 1)
         make_da3(0)
         gate_g(2)
         make_part(1)
+        permute_words(nc.vector.tensor_copy, 1)
         quantize_g(2)
         make_dh(2)
         quantize_da(0)

@@ -30,12 +30,14 @@ KIB = 1024
 FLOPS = 2 * S * (N * H + 2 * H * K)
 BYTES = 4 * (N * T + 2 * H * S + K * T + S) + E * P * (2 * H + 4 * K) + E * 16 * (H + 2 * K) + 2 * 16 * S // 16
 
-SUCCEEDS = {"g_bf2": "tanh0", "da_bf0": "a3_0", "part2": "a3_1", "da_codes0": "neg1", "g_codes3": "neg1", "da_codes1": "neg2", "da_bf3": "silu2", "dx_sb0": "a1_half1", "dx_sb1": "a1_half1", "dx_sb21": "a1_half1", "dx_sb20": "tanh3"}
-PLACES = {"factor0": 0, "factor1": 2, "factor2": 4, "factor3": 6, "da_bf2": 10, "tanh2": 12, "part3": 14, "da_bf1": 18, "tanh1": 20, "g_bf3": 22}
+SUCCEEDS = {"g_bf2": "tanh0", "da_bf0": "a3_0", "part2": "silu1", "da_codes0": "neg1", "g_codes3": "neg1", "da_codes1": "neg2", "da_bf3": "silu2", "late0": "tanh3"}
+PLACES = {"factor0": 0, "factor1": 2, "factor2": 4, "factor3": 6, "tanh1": 6, "g_bf3": 6, "da_bf1": 8, "da_bf2": 12, "tanh2": 14, "part3": 16, "late1": 24, "a1_half1": 25, "dx_sb00": 25, "dx_sb01": 26, "dx_sb10": 25, "dx_sb11": 26}
 GATE_BANK = (6, 7)
 DH_BANK = (0, 1, 2, 3, 0, 1, 2, 3)
-DX_BANK = (4, 5)
-ROWS_DX_BANK = {(2, 0): 0, (2, 1): 1, (3, 0): 2, (3, 1): 3}
+DX_BANK = (4, 4)
+ROWS_DX_BANK = {(2, 0): 0, (2, 1): 1, ((3, 0), 0): 2, ((3, 0), 1): 3, ((3, 1), 0): 6, ((3, 1), 1): 7}
+FIRST_CUT = 192
+SECOND_CUT = 352
 
 
 def tile_moe_bdx_glu_silu_kernel(
@@ -66,26 +68,23 @@ def tile_moe_bdx_glu_silu_kernel(
         ident = new_tile("ident", [P, P], F32)
         zero = new_tile("zero", [P, 1], F32)
         a1_half1 = new_tile("a1_half1", [P, PACK, HALF], F32)
-        a3_half1 = new_tile("a3_half1", [P, PACK, HALF], F32)
+        a3_middle = new_tile("a3_middle", [P, PACK, 2 * C], F32)
         a1_sb = [new_tile(f"a1_{e}", [P, PACK, C], F32)[:] for e in range(2)]
-        a3_sb = [new_tile(f"a3_{e}", [P, PACK, C], F32)[:] for e in range(2)]
+        a3_sb = [new_tile(f"a3_{e}", [P, PACK, C], F32)[:] for e in (0, E - 1)]
         a1_sb = a1_sb + [a1_half1[:, :, 0:C], a1_half1[:, :, C:HALF]]
-        a3_sb = a3_sb + [a3_half1[:, :, 0:C], a3_half1[:, :, C:HALF]]
+        a3_sb = [a3_sb[0], a3_middle[:, :, 0:C], a3_middle[:, :, C:], a3_sb[1]]
         w2_raw = [new_tile(f"w2_raw{h}", [P, 2, 2 * H], U8) for h in range(2)]
         w2s_raw = new_tile("w2s_raw", [P, E, H], U8)
-        w1_sb = new_tile("w1_sb", [P, E, 2 * K], U8)
-        w3_sb = new_tile("w3_sb", [P, E, 2 * K], U8)
+        w1_sb = [new_tile(f"w1_sb{h}", [P, 2, 2 * K], U8) for h in range(2)]
+        w3_sb = [new_tile(f"w3_sb{h}", [P, 2, 2 * K], U8) for h in range(2)]
         w1s = new_tile("w1s", [P, E, K], U8)
         w3s = new_tile("w3s", [P, E, K], U8)
         gate_col = new_tile("gate_col", [P, 2, 8], F32)
         win = [new_tile(f"win{b}", [P, T], F32) for b in range(K // P)]
 
-        def load_words(tile, dram):
-            nc.sync.dma_start(tile[:].bitcast(I32), dram.bitcast(I32)[:, 0].rearrange("e p b -> p e b"))
-
-        def load_w2(h):
+        def load_words(tiles, dram, h):
             nc.sync.dma_start(
-                w2_raw[h][:].bitcast(I32), w2_words.bitcast(I32)[2 * h : 2 * h + 2, 0].rearrange("e p b -> p e b")
+                tiles[h][:].bitcast(I32), dram.bitcast(I32)[2 * h : 2 * h + 2, 0].rearrange("e p b -> p e b")
             )
 
         def load_scales(queue, tile, dram):
@@ -105,8 +104,8 @@ def tile_moe_bdx_glu_silu_kernel(
         def load_expert(tiles, dram, e):
             nc.sync.dma_start(tiles[e], dram[:, :, e * C : (e + 1) * C])
 
-        def load_half1(tile, dram):
-            nc.sync.dma_start(tile[:], dram[:, :, HALF:])
+        def load_two_experts(tile, dram, first):
+            nc.sync.dma_start(tile[:], dram[:, :, first * C : (first + 2) * C])
 
         def load_gate():
             nc.scalar.dma_start(gate_col[:, :, 0:4], gate[0, :].rearrange("(h n i) -> n h i", h=2, i=4))
@@ -193,14 +192,28 @@ def tile_moe_bdx_glu_silu_kernel(
             tanh_sb[e] = new_tile(f"tanh{e}", [P, PACK, C], F32)
             nc.scalar.activation(tanh_sb[e][:], a1_sb[e], ACT.Tanh, scale=-0.5)
 
-        def factor_vector(e):
-            factor[e] = new_tile(f"factor{e}", [P, PACK, C], F32)
-            nc.vector.scalar_tensor_tensor(factor[e][:], tanh_sb[e][:], 1.0, a3_sb[e], ALU.subtract, ALU.mult)
+        def factor_vector(e, cols=all_cols):
+            if e not in factor:
+                factor[e] = new_tile(f"factor{e}", [P, PACK, C], F32)
+            nc.vector.scalar_tensor_tensor(
+                factor[e][:, :, cols], tanh_sb[e][:, :, cols], 1.0, a3_sb[e][:, :, cols], ALU.subtract, ALU.mult
+            )
 
-        da_bf, da_scales, da_codes = {}, {}, {}
+        da_bf, da1_out, da3_out, da_scales, da_codes = {}, {}, {}, {}, {}
 
         def new_da(e):
-            da_bf[e] = new_tile(f"da_bf{e}", [P, 2, C, PACK], BF16)
+            tile = new_tile(f"da_bf{e}", [P, 2, C, PACK], BF16)
+            da_bf[e] = tile[:].rearrange("p i n j -> p (i n j)")
+            da1_out[e] = tile[:, 0]
+            for c in range(2):
+                da3_out[e, c] = tile[:, 1, block_cols(c), :]
+
+        def new_da_by_block(e):
+            tile = new_tile(f"da_bf{e}", [P, 2, 2, P, PACK], BF16)
+            for c in range(2):
+                da_bf[e, c] = tile[:, c].rearrange("p i n j -> p (i n j)")
+                da1_out[e, c] = tile[:, c, 0]
+                da3_out[e, c] = tile[:, c, 1]
 
         def make_dh(e):
             h, within = divmod(e, 2)
@@ -233,7 +246,7 @@ def tile_moe_bdx_glu_silu_kernel(
         def make_da3(e, blocks=(0, 1)):
             for c in blocks:
                 nc.vector.scalar_tensor_tensor(
-                    da_bf[e][:, 1, block_cols(c), :],
+                    da3_out[e, c],
                     dh[e, c][:].rearrange("p j n -> p n j"),
                     2.0,
                     silu_sb[e][:, block_cols(c), :],
@@ -241,67 +254,76 @@ def tile_moe_bdx_glu_silu_kernel(
                     ALU.mult,
                 )
 
-        def make_da1(engine, e, cols):
+        def make_da1(engine, target, e, cols):
             engine.tensor_tensor(
-                walk_packed(da_bf[e][:, 0, cols, :]),
-                walk_planar(part[e][:, :, cols]),
-                walk_planar(factor[e][:, :, cols]),
-                ALU.mult,
+                walk_packed(target), walk_planar(part[e][:, :, cols]), walk_planar(factor[e][:, :, cols]), ALU.mult
             )
 
-        def quantize_da(e):
-            da_codes[e] = new_tile(f"da_codes{e}", [P, 2, C], U32)
-            da_scales[e] = new_tile(f"da_scales{e}", [P, 2, C], U8)
+        def da1_gpsimd(e):
+            make_da1(nc.gpsimd, da1_out[e], e, all_cols)
+
+        def da1_vector(e, c):
+            make_da1(nc.vector, da1_out[e, c], e, block_cols(c))
+
+        def quantize_da(key, name, width):
+            da_codes[key] = new_tile(f"da_codes{name}", [P, 2, width], U32)
+            da_scales[key] = new_tile(f"da_scales{name}", [P, 2, width], U8)
             nc.vector.quantize_mx(
-                out=da_codes[e][:].rearrange("p i n -> p (i n)").bitcast(FP8X4),
-                scales=da_scales[e][:].rearrange("p i n -> p (i n)"),
-                in_=da_bf[e][:].rearrange("p i n j -> p (i n j)"),
+                out=da_codes[key][:].rearrange("p i n -> p (i n)").bitcast(FP8X4),
+                scales=da_scales[key][:].rearrange("p i n -> p (i n)"),
+                in_=da_bf[key],
             )
 
-        dx_both, dx, dx_sb = {}, {}, {}
+        def quantize_expert(e):
+            quantize_da(e, f"{e}", C)
 
-        def project_rows(e, b):
+        def quantize_block(e, c):
+            quantize_da((e, c), f"{e}{c}", P)
+
+        dx = {}
+
+        def project_rows(key, e, b):
             for i, (w, ws) in enumerate(((w1_sb, w1s), (w3_sb, w3s))):
                 nc.tensor.matmul_mx(
-                    out=dx[e, b],
-                    lhsT=w[:, e, 2 * P * b : 2 * P * (b + 1)].bitcast(FP4X4),
+                    out=dx[key, b],
+                    lhsT=w[e // 2][:, e % 2, 2 * P * b : 2 * P * (b + 1)].bitcast(FP4X4),
                     lhsT_scale=ws[:, e, P * b : P * (b + 1)],
-                    rhs=da_codes[e][:, i, :].bitcast(FP8X4),
-                    rhs_scale=da_scales[e][:, i, :],
+                    rhs=da_codes[key][:, i, :].bitcast(FP8X4),
+                    rhs_scale=da_scales[key][:, i, :],
                     start=(i == 0),
                     stop=(i == 1),
                 )
 
         def project(e):
-            dx_both[e] = bank(f"dx{e}", [P, K // P, C], DX_BANK[e])
+            both = bank(f"dx{e}", [P, K // P, C], DX_BANK[e])
             for b in range(K // P):
-                dx[e, b] = dx_both[e][:, b, :]
-                project_rows(e, b)
+                dx[e, b] = both[:, b, :]
+                project_rows(e, e, b)
 
-        def project_by_rows(e):
+        def project_by_rows(key, e, width):
             for b in reversed(range(K // P)):
-                dx[e, b] = bank(f"dx{e}{b}", [P, C], ROWS_DX_BANK[e, b])[:]
-                project_rows(e, b)
+                number = ROWS_DX_BANK[key, b]
+                dx[key, b] = bank(f"dx_late{number}", [P, width], number)[:]
+                project_rows(key, e, b)
 
-        def copy_dx(e):
-            both = new_tile(f"dx_sb{e}", [P, K // P, C], F32)
-            nc.scalar.activation(both[:], dx_both[e][:], ACT.Copy, scale=0.5)
+        def copy_scalar(target, key, b):
+            nc.scalar.activation(target, dx[key, b], ACT.Copy, scale=0.5)
+
+        def copy_vector(target, key, b):
+            nc.vector.tensor_scalar(target, dx[key, b], 0.5, None, ALU.mult)
+
+        def scatter_vector(b, first, values):
+            nc.vector.tensor_copy(win[b][:].indirect(entries(first, values.shape[1])), values)
+
+        def scatter_scalar(b, first, values):
+            nc.scalar.activation(win[b][:].indirect(entries(first, values.shape[1])), values, ACT.Copy)
+
+        def return_expert(e):
+            tiles = [new_tile(f"dx_sb{e}{b}", [P, C], F32) for b in range(K // P)]
             for b in range(K // P):
-                dx_sb[e, b] = both[:, b, :]
-
-        def copy_dx_rows(e, b):
-            dx_sb[e, b] = new_tile(f"dx_sb{e}{b}", [P, C], F32)[:]
-            nc.scalar.activation(dx_sb[e, b], dx[e, b], ACT.Copy, scale=0.5)
-
-        def copy_dx_rows_vector(e, b):
-            dx_sb[e, b] = new_tile(f"dx_sb{e}{b}", [P, C], F32)[:]
-            nc.vector.tensor_scalar(dx_sb[e, b], dx[e, b], 0.5, None, ALU.mult)
-
-        def scatter_vector(e, b):
-            nc.vector.tensor_copy(win[b][:].indirect(entries(e * C, C)), dx_sb[e, b])
-
-        def scatter_scalar(e, b):
-            nc.scalar.activation(win[b][:].indirect(entries(e * C, C)), dx_sb[e, b], ACT.Copy)
+                copy_scalar(tiles[b][:], e, b)
+            for b in range(K // P):
+                scatter_scalar(b, e * C, tiles[b][:])
 
         def store(b):
             nc.sync.dma_start(out[b * P : (b + 1) * P, :], win[b][:])
@@ -319,21 +341,23 @@ def tile_moe_bdx_glu_silu_kernel(
         load_plane(0)
         nc.sync.dma_start(offsets[:], offs)
         load_plane(1)
+        load_scales(nc.sync, w2s_raw, w2_scales)
         load_plane(2)
         load_plane(3)
-        load_scales(nc.sync, w2s_raw, w2_scales)
+        load_words(w2_raw, w2_words, 0)
         load_expert(a1_sb, a1_4, 0)
-        load_w2(0)
         load_expert(a3_sb, a3_4, 0)
         load_expert(a1_sb, a1_4, 1)
-        load_expert(a3_sb, a3_4, 1)
-        load_w2(1)
-        load_half1(a1_half1, a1_4)
-        load_words(w1_sb, w1_words)
-        load_words(w3_sb, w3_words)
-        load_scales(nc.sync, w1s, w1_scales)
+        load_two_experts(a1_half1, a1_4, 2)
+        load_words(w2_raw, w2_words, 1)
+        load_two_experts(a3_middle, a3_4, 1)
+        load_words(w3_sb, w3_words, 0)
+        load_words(w1_sb, w1_words, 0)
         load_scales(nc.sync, w3s, w3_scales)
-        load_half1(a3_half1, a3_4)
+        load_scales(nc.sync, w1s, w1_scales)
+        load_expert(a3_sb, a3_4, 3)
+        load_words(w3_sb, w3_words, 1)
+        load_words(w1_sb, w1_words, 1)
 
         permute_scales(0)
         permute_scales(1)
@@ -347,20 +371,21 @@ def tile_moe_bdx_glu_silu_kernel(
         gather_scalar(PACK - 1, HALF, HALF)
 
         gate_g(0)
-        gate_g(1)
         permute_words(nc.vector.tensor_copy, 0)
         quantize_g(0)
         make_dh(0)
-        act_tanh(0)
         act_neg(0)
+        act_tanh(0)
         act_silu(0)
-        factor_vector(0)
+        gate_g(1)
+        make_part(0, (0,))
         quantize_g(1)
         make_dh(1)
-        make_part(0)
+        make_part(0, (1,))
+        factor_vector(0)
 
         new_da(0)
-        make_da1(nc.gpsimd, 0, all_cols)
+        da1_gpsimd(0)
         act_neg(1)
         act_tanh(1)
         act_silu(1)
@@ -370,54 +395,58 @@ def tile_moe_bdx_glu_silu_kernel(
         permute_words(nc.vector.tensor_copy, 1)
         quantize_g(2)
         make_dh(2)
-        quantize_da(0)
+        quantize_expert(0)
         project(0)
         factor_vector(1)
 
         new_da(1)
-        make_da1(nc.gpsimd, 1, all_cols)
-        act_neg(2)
-        act_tanh(2)
-        act_silu(2)
-        act_neg(3)
-        act_tanh(3)
-        act_silu(3)
-        copy_dx(0)
-        scatter_scalar(0, 0)
-        scatter_scalar(0, 1)
-        gate_g(3)
+        da1_gpsimd(1)
+        for e in (2, 3):
+            act_neg(e)
+            act_tanh(e)
+            act_silu(e)
+        return_expert(0)
         make_da3(1)
+        gate_g(3)
         make_part(2)
-        quantize_da(1)
+        quantize_expert(1)
         project(1)
         quantize_g(3)
         make_dh(3)
         factor_vector(2)
 
         new_da(2)
-        make_da1(nc.gpsimd, 2, all_cols)
-        copy_dx(1)
-        scatter_scalar(1, 0)
-        scatter_scalar(1, 1)
+        da1_gpsimd(2)
+        return_expert(1)
         make_da3(2)
-        new_da(3)
+        new_da_by_block(3)
         for c in range(2):
             make_part(3, (c,))
             make_da3(3, (c,))
-        quantize_da(2)
-        project_by_rows(2)
-        factor_vector(3)
 
-        copy_dx_rows(2, 1)
-        scatter_scalar(2, 1)
-        make_da1(nc.vector, 3, all_cols)
-        copy_dx_rows_vector(2, 0)
-        quantize_da(3)
-        project_by_rows(3)
-        scatter_vector(2, 0)
-        copy_dx_rows(3, 1)
-        scatter_scalar(3, 1)
-        copy_dx_rows_vector(3, 0)
-        scatter_vector(3, 0)
+        late = [new_tile(f"late{b}", [P, HALF], F32) for b in range(K // P)]
+        factor_vector(3, block_cols(0))
+        quantize_expert(2)
+        project_by_rows(2, 2, C)
+        da1_vector(3, 0)
+        factor_vector(3, block_cols(1))
+        quantize_block(3, 0)
+        project_by_rows((3, 0), 3, P)
+        da1_vector(3, 1)
+        copy_vector(late[0][:, 0:C], 2, 0)
+        quantize_block(3, 1)
+        project_by_rows((3, 1), 3, P)
+
+        copy_scalar(late[1][:, 0:C], 2, 1)
+        scatter_scalar(1, HALF, late[1][:, 0:FIRST_CUT])
+        copy_scalar(late[1][:, C : C + P], (3, 0), 1)
+        scatter_scalar(1, HALF + FIRST_CUT, late[1][:, FIRST_CUT:SECOND_CUT])
+        copy_scalar(late[1][:, C + P :], (3, 1), 1)
+        scatter_scalar(1, HALF + SECOND_CUT, late[1][:, SECOND_CUT:])
         store(1)
+
+        copy_vector(late[0][:, C : C + P], (3, 0), 0)
+        scatter_vector(0, HALF, late[0][:, 0:FIRST_CUT])
+        copy_vector(late[0][:, C + P :], (3, 1), 0)
+        scatter_vector(0, HALF + FIRST_CUT, late[0][:, FIRST_CUT:])
         store(0)

@@ -30,14 +30,12 @@ KIB = 1024
 FLOPS = 2 * S * (N * H + 2 * H * K)
 BYTES = 4 * (N * T + 2 * H * S + K * T + S) + E * P * (2 * H + 4 * K) + E * 16 * (H + 2 * K) + 2 * 16 * S // 16
 
-SUCCEEDS = {"g_bf2": "tanh0", "da_bf0": "a3_0", "part2": "silu1", "da_codes0": "neg1", "g_codes3": "neg1", "da_codes1": "neg2", "da_bf3": "silu2", "late0": "tanh3"}
-PLACES = {"factor0": 0, "factor1": 2, "factor2": 4, "factor3": 6, "tanh1": 6, "g_bf3": 6, "da_bf1": 8, "da_bf2": 12, "tanh2": 14, "part3": 16, "late1": 24, "a1_half1": 25, "dx_sb00": 25, "dx_sb01": 26, "dx_sb10": 25, "dx_sb11": 26}
+SUCCEEDS = {"da_bf1": "da_bf0", "part2": "part0", "da_bf3": "silu2", "g_codes3": "da_codes0"}
+PLACES = {"factor0": 0, "g_bf3": 0, "factor1": 2, "factor2": 4, "factor3": 6, "da_bf2": 10, "tanh2": 12, "part3": 14, "dx_sb20": 14, "dx_sb21": 25, "a1_half1": 25, "dx_sb00": 25, "dx_sb01": 26, "dx_sb10": 25, "dx_sb11": 26}
 GATE_BANK = (6, 7)
 DH_BANK = (0, 1, 2, 3, 0, 1, 2, 3)
 DX_BANK = (4, 4)
-ROWS_DX_BANK = {(2, 0): 0, (2, 1): 1, ((3, 0), 0): 2, ((3, 0), 1): 3, ((3, 1), 0): 6, ((3, 1), 1): 7}
-FIRST_CUT = 192
-SECOND_CUT = 352
+ROWS_DX_BANK = {(2, 0): 0, (2, 1): 1, (3, 0): 2, (3, 1): 3}
 
 
 def tile_moe_bdx_glu_silu_kernel(
@@ -68,23 +66,23 @@ def tile_moe_bdx_glu_silu_kernel(
         ident = new_tile("ident", [P, P], F32)
         zero = new_tile("zero", [P, 1], F32)
         a1_half1 = new_tile("a1_half1", [P, PACK, HALF], F32)
-        a3_middle = new_tile("a3_middle", [P, PACK, 2 * C], F32)
+        a3_half1 = new_tile("a3_half1", [P, PACK, HALF], F32)
         a1_sb = [new_tile(f"a1_{e}", [P, PACK, C], F32)[:] for e in range(2)]
-        a3_sb = [new_tile(f"a3_{e}", [P, PACK, C], F32)[:] for e in (0, E - 1)]
+        a3_sb = [new_tile(f"a3_{e}", [P, PACK, C], F32)[:] for e in range(2)]
         a1_sb = a1_sb + [a1_half1[:, :, 0:C], a1_half1[:, :, C:HALF]]
-        a3_sb = [a3_sb[0], a3_middle[:, :, 0:C], a3_middle[:, :, C:], a3_sb[1]]
+        a3_sb = a3_sb + [a3_half1[:, :, 0:C], a3_half1[:, :, C:HALF]]
         w2_raw = [new_tile(f"w2_raw{h}", [P, 2, 2 * H], U8) for h in range(2)]
         w2s_raw = new_tile("w2s_raw", [P, E, H], U8)
-        w1_sb = [new_tile(f"w1_sb{h}", [P, 2, 2 * K], U8) for h in range(2)]
-        w3_sb = [new_tile(f"w3_sb{h}", [P, 2, 2 * K], U8) for h in range(2)]
+        w1_sb = new_tile("w1_sb", [P, E, 2 * K], U8)
+        w3_sb = new_tile("w3_sb", [P, E, 2 * K], U8)
         w1s = new_tile("w1s", [P, E, K], U8)
         w3s = new_tile("w3s", [P, E, K], U8)
         gate_col = new_tile("gate_col", [P, 2, 8], F32)
         win = [new_tile(f"win{b}", [P, T], F32) for b in range(K // P)]
 
-        def load_words(tiles, dram, h):
+        def load_words(tile, dram, first, count):
             nc.sync.dma_start(
-                tiles[h][:].bitcast(I32), dram.bitcast(I32)[2 * h : 2 * h + 2, 0].rearrange("e p b -> p e b")
+                tile[:].bitcast(I32), dram.bitcast(I32)[first : first + count, 0].rearrange("e p b -> p e b")
             )
 
         def load_scales(queue, tile, dram):
@@ -280,13 +278,13 @@ def tile_moe_bdx_glu_silu_kernel(
         def quantize_block(e, c):
             quantize_da((e, c), f"{e}{c}", P)
 
-        dx = {}
+        dx, dx_sb = {}, {}
 
-        def project_rows(key, e, b):
+        def project_rows(target, key, e, b):
             for i, (w, ws) in enumerate(((w1_sb, w1s), (w3_sb, w3s))):
                 nc.tensor.matmul_mx(
-                    out=dx[key, b],
-                    lhsT=w[e // 2][:, e % 2, 2 * P * b : 2 * P * (b + 1)].bitcast(FP4X4),
+                    out=target,
+                    lhsT=w[:, e, 2 * P * b : 2 * P * (b + 1)].bitcast(FP4X4),
                     lhsT_scale=ws[:, e, P * b : P * (b + 1)],
                     rhs=da_codes[key][:, i, :].bitcast(FP8X4),
                     rhs_scale=da_scales[key][:, i, :],
@@ -298,13 +296,22 @@ def tile_moe_bdx_glu_silu_kernel(
             both = bank(f"dx{e}", [P, K // P, C], DX_BANK[e])
             for b in range(K // P):
                 dx[e, b] = both[:, b, :]
-                project_rows(e, e, b)
+                project_rows(dx[e, b], e, e, b)
 
-        def project_by_rows(key, e, width):
+        def new_rows(e):
+            for b in range(K // P):
+                dx[e, b] = bank(f"dx{e}{b}", [P, C], ROWS_DX_BANK[e, b])[:]
+
+        def project_by_rows(e):
+            new_rows(e)
             for b in reversed(range(K // P)):
-                number = ROWS_DX_BANK[key, b]
-                dx[key, b] = bank(f"dx_late{number}", [P, width], number)[:]
-                project_rows(key, e, b)
+                project_rows(dx[e, b], e, e, b)
+
+        def project_by_blocks(e):
+            new_rows(e)
+            for b in reversed(range(K // P)):
+                for c in range(2):
+                    project_rows(dx[e, b][:, block_cols(c)], (e, c), e, b)
 
         def copy_scalar(target, key, b):
             nc.scalar.activation(target, dx[key, b], ACT.Copy, scale=0.5)
@@ -325,6 +332,10 @@ def tile_moe_bdx_glu_silu_kernel(
             for b in range(K // P):
                 scatter_scalar(b, e * C, tiles[b][:])
 
+        def copy_rows(copy, e, b):
+            dx_sb[e, b] = new_tile(f"dx_sb{e}{b}", [P, C], F32)[:]
+            copy(dx_sb[e, b], e, b)
+
         def store(b):
             nc.sync.dma_start(out[b * P : (b + 1) * P, :], win[b][:])
 
@@ -344,20 +355,18 @@ def tile_moe_bdx_glu_silu_kernel(
         load_scales(nc.sync, w2s_raw, w2_scales)
         load_plane(2)
         load_plane(3)
-        load_words(w2_raw, w2_words, 0)
+        load_words(w2_raw[0], w2_words, 0, 2)
         load_expert(a1_sb, a1_4, 0)
         load_expert(a3_sb, a3_4, 0)
         load_expert(a1_sb, a1_4, 1)
+        load_expert(a3_sb, a3_4, 1)
+        load_words(w2_raw[1], w2_words, 2, 2)
         load_two_experts(a1_half1, a1_4, 2)
-        load_words(w2_raw, w2_words, 1)
-        load_two_experts(a3_middle, a3_4, 1)
-        load_words(w3_sb, w3_words, 0)
-        load_words(w1_sb, w1_words, 0)
+        load_words(w3_sb, w3_words, 0, E)
+        load_words(w1_sb, w1_words, 0, E)
         load_scales(nc.sync, w3s, w3_scales)
         load_scales(nc.sync, w1s, w1_scales)
-        load_expert(a3_sb, a3_4, 3)
-        load_words(w3_sb, w3_words, 1)
-        load_words(w1_sb, w1_words, 1)
+        load_two_experts(a3_half1, a3_4, 2)
 
         permute_scales(0)
         permute_scales(1)
@@ -374,15 +383,14 @@ def tile_moe_bdx_glu_silu_kernel(
         permute_words(nc.vector.tensor_copy, 0)
         quantize_g(0)
         make_dh(0)
-        act_neg(0)
         act_tanh(0)
+        act_neg(0)
         act_silu(0)
         gate_g(1)
-        make_part(0, (0,))
+        factor_vector(0)
         quantize_g(1)
         make_dh(1)
-        make_part(0, (1,))
-        factor_vector(0)
+        make_part(0)
 
         new_da(0)
         da1_gpsimd(0)
@@ -406,8 +414,8 @@ def tile_moe_bdx_glu_silu_kernel(
             act_tanh(e)
             act_silu(e)
         return_expert(0)
-        make_da3(1)
         gate_g(3)
+        make_da3(1)
         make_part(2)
         quantize_expert(1)
         project(1)
@@ -424,29 +432,21 @@ def tile_moe_bdx_glu_silu_kernel(
             make_part(3, (c,))
             make_da3(3, (c,))
 
-        late = [new_tile(f"late{b}", [P, HALF], F32) for b in range(K // P)]
-        factor_vector(3, block_cols(0))
         quantize_expert(2)
-        project_by_rows(2, 2, C)
-        da1_vector(3, 0)
-        factor_vector(3, block_cols(1))
-        quantize_block(3, 0)
-        project_by_rows((3, 0), 3, P)
-        da1_vector(3, 1)
-        copy_vector(late[0][:, 0:C], 2, 0)
-        quantize_block(3, 1)
-        project_by_rows((3, 1), 3, P)
+        project_by_rows(2)
+        for c in range(2):
+            factor_vector(3, block_cols(c))
+        for c in range(2):
+            da1_vector(3, c)
+        for c in range(2):
+            quantize_block(3, c)
+        project_by_blocks(3)
 
-        copy_scalar(late[1][:, 0:C], 2, 1)
-        scatter_scalar(1, HALF, late[1][:, 0:FIRST_CUT])
-        copy_scalar(late[1][:, C : C + P], (3, 0), 1)
-        scatter_scalar(1, HALF + FIRST_CUT, late[1][:, FIRST_CUT:SECOND_CUT])
-        copy_scalar(late[1][:, C + P :], (3, 1), 1)
-        scatter_scalar(1, HALF + SECOND_CUT, late[1][:, SECOND_CUT:])
+        for e in (2, 3):
+            copy_rows(copy_scalar, e, 1)
+            scatter_scalar(1, e * C, dx_sb[e, 1])
         store(1)
-
-        copy_vector(late[0][:, C : C + P], (3, 0), 0)
-        scatter_vector(0, HALF, late[0][:, 0:FIRST_CUT])
-        copy_vector(late[0][:, C + P :], (3, 1), 0)
-        scatter_vector(0, HALF + FIRST_CUT, late[0][:, FIRST_CUT:])
+        for e in (2, 3):
+            copy_rows(copy_vector, e, 0)
+            scatter_vector(0, e * C, dx_sb[e, 0])
         store(0)

@@ -30,12 +30,13 @@ KIB = 1024
 FLOPS = 2 * S * (N * H + 2 * H * K)
 BYTES = 4 * (N * T + 2 * H * S + K * T + S) + E * P * (2 * H + 4 * K) + E * 16 * (H + 2 * K) + 2 * 16 * S // 16
 
-SUCCEEDS = {"da_bf1": "da_bf0", "part2": "part0", "da_bf3": "silu2", "g_codes3": "da_codes0"}
-PLACES = {"factor0": 0, "g_bf3": 0, "factor1": 2, "factor2": 4, "factor3": 6, "da_bf2": 10, "tanh2": 12, "part3": 14, "dx_sb20": 14, "dx_sb21": 25, "a1_half1": 25, "dx_sb00": 25, "dx_sb01": 26, "dx_sb10": 25, "dx_sb11": 26}
+SUCCEEDS = {"g_bf2": "tanh0", "da_bf0": "a3_0", "da_bf1": "a3_0", "part2": "part0", "da_bf3": "silu2", "g_bf31": "g_bf0"}
+PLACES = {"g_codes1": 0, "gate_last": 0.75, "factor0": 1, "g_bf30": 1, "factor1": 3, "factor2": 5, "factor3": 7, "da_bf2": 11, "tanh2": 13, "part3": 15, "da_codes0": 20, "g_codes30": 20, "g_codes31": 21, "a1_half1": 25, "dx_sb00": 25, "dx_sb01": 27, "middle0": 25, "dx_sb11": 27, "dx_sb21": 27}
 GATE_BANK = (6, 7)
 DH_BANK = (0, 1, 2, 3, 0, 1, 2, 3)
 DX_BANK = (4, 4)
 ROWS_DX_BANK = {(2, 0): 0, (2, 1): 1, (3, 0): 2, (3, 1): 3}
+CUT = 160
 
 
 def tile_moe_bdx_glu_silu_kernel(
@@ -51,7 +52,7 @@ def tile_moe_bdx_glu_silu_kernel(
 
         def new_tile(name, shape, dtype):
             if name in PLACES:
-                return shared.tile(shape, dtype, name=name, offset=PLACES[name] * KIB, align_bytes=64)
+                return shared.tile(shape, dtype, name=name, offset=int(PLACES[name] * KIB), align_bytes=64)
             return keep.tile(shape, dtype, name=name, tag=SUCCEEDS.get(name, name), align_bytes=64)
 
         def bank(name, shape, number):
@@ -156,25 +157,38 @@ def tile_moe_bdx_glu_silu_kernel(
         g_bf, g_codes = {}, {}
         g_scales = new_tile("g_scales", [P, S], U8)
 
-        def gate_g(e):
+        def gate_slots(engine, name, e, cols, gates):
             h, within = divmod(e, 2)
-            g_bf[e] = new_tile(f"g_bf{e}", [P, C, PACK], BF16)
-            groups = C // 4
-            gates = gate_wide[h][:, :, within * groups : (within + 1) * groups].rearrange("p i c -> p c i")
-            nc.vector.tensor_tensor(
-                walk_packed(g_bf[e][:]),
-                walk_planar(gathered[h][:, :, within * C : (within + 1) * C]),
-                gates.unsqueeze(2).broadcast_to([P, groups, PACK, 4]),
+            width = cols.stop - cols.start
+            first = within * C + cols.start
+            g_bf[name] = new_tile(f"g_bf{name}", [P, width, PACK], BF16)
+            engine.tensor_tensor(
+                walk_packed(g_bf[name][:]),
+                walk_planar(gathered[h][:, :, first : first + width]),
+                gates.unsqueeze(2).broadcast_to([P, width // 4, PACK, 4]),
                 ALU.mult,
             )
 
-        def quantize_g(e):
-            g_codes[e] = new_tile(f"g_codes{e}", [P, C], U32)
+        def wide_gates(e, cols):
+            h, within = divmod(e, 2)
+            first = (within * C + cols.start) // 4
+            return gate_wide[h][:, :, first : first + (cols.stop - cols.start) // 4].rearrange("p i c -> p c i")
+
+        def gate_g(e):
+            gate_slots(nc.vector, f"{e}", e, all_cols, wide_gates(e, all_cols))
+
+        def quantize_slots(name, e, cols):
+            codes = new_tile(f"g_codes{name}", [P, cols.stop - cols.start], U32)
             nc.vector.quantize_mx(
-                out=g_codes[e][:].bitcast(FP8X4),
-                scales=g_scales[:, e * C : (e + 1) * C],
-                in_=g_bf[e][:].rearrange("p n j -> p (n j)"),
+                out=codes[:].bitcast(FP8X4),
+                scales=g_scales[:, e * C + cols.start : e * C + cols.stop],
+                in_=g_bf[name][:].rearrange("p n j -> p (n j)"),
             )
+            for first in range(cols.start, cols.stop, P):
+                g_codes[e, first // P] = codes[:, first - cols.start : first - cols.start + P]
+
+        def quantize_g(e):
+            quantize_slots(f"{e}", e, all_cols)
 
         neg_sb, silu_sb, tanh_sb, factor, part, dh = {}, {}, {}, {}, {}, {}
 
@@ -222,7 +236,7 @@ def tile_moe_bdx_glu_silu_kernel(
                         out=dh[e, c][:, t, :],
                         lhsT=w2_perm[h][:, within, 2 * P * t : 2 * P * (t + 1)].bitcast(FP4X4),
                         lhsT_scale=w2s_perm[h][:, within, P * t : P * (t + 1)],
-                        rhs=g_codes[e][:, block_cols(c)].bitcast(FP8X4),
+                        rhs=g_codes[e, c].bitcast(FP8X4),
                         rhs_scale=g_scales[:, e * C + c * P : e * C + (c + 1) * P],
                         start=True,
                         stop=True,
@@ -375,6 +389,8 @@ def tile_moe_bdx_glu_silu_kernel(
         for t in range(PACK - 1):
             gather_vector(t, 0, HALF)
             gather_scalar(t, HALF, HALF)
+        gate_last = new_tile("gate_last", [P, P // 4, 4], F32)
+        nc.vector.tensor_copy(gate_last[:], wide_gates(3, block_cols(1)))
         gather_vector(PACK - 1, 0, C)
         gather_scalar(PACK - 1, C, C)
         gather_scalar(PACK - 1, HALF, HALF)
@@ -383,14 +399,15 @@ def tile_moe_bdx_glu_silu_kernel(
         permute_words(nc.vector.tensor_copy, 0)
         quantize_g(0)
         make_dh(0)
-        act_tanh(0)
+        gate_slots(nc.gpsimd, "31", 3, block_cols(1), gate_last[:])
         act_neg(0)
+        act_tanh(0)
         act_silu(0)
         gate_g(1)
+        make_part(0)
         factor_vector(0)
         quantize_g(1)
         make_dh(1)
-        make_part(0)
 
         new_da(0)
         da1_gpsimd(0)
@@ -414,18 +431,23 @@ def tile_moe_bdx_glu_silu_kernel(
             act_tanh(e)
             act_silu(e)
         return_expert(0)
-        gate_g(3)
+        gate_slots(nc.vector, "30", 3, block_cols(0), wide_gates(3, block_cols(0)))
         make_da3(1)
         make_part(2)
         quantize_expert(1)
         project(1)
-        quantize_g(3)
+        for c in range(2):
+            quantize_slots(f"3{c}", 3, block_cols(c))
         make_dh(3)
         factor_vector(2)
 
         new_da(2)
         da1_gpsimd(2)
-        return_expert(1)
+        middle = new_tile("middle0", [P, 2 * C], F32)
+        copy_scalar(middle[:, 0:C], 1, 0)
+        copy_rows(copy_scalar, 1, 1)
+        scatter_scalar(0, C, middle[:, 0:CUT])
+        scatter_scalar(1, C, dx_sb[1, 1])
         make_da3(2)
         new_da_by_block(3)
         for c in range(2):
@@ -442,11 +464,13 @@ def tile_moe_bdx_glu_silu_kernel(
             quantize_block(3, c)
         project_by_blocks(3)
 
-        for e in (2, 3):
-            copy_rows(copy_scalar, e, 1)
-            scatter_scalar(1, e * C, dx_sb[e, 1])
+        copy_rows(copy_scalar, 2, 1)
+        copy_scalar(middle[:, C:], 2, 0)
+        scatter_scalar(1, 2 * C, dx_sb[2, 1])
+        copy_rows(copy_scalar, 3, 1)
+        scatter_scalar(1, 3 * C, dx_sb[3, 1])
         store(1)
-        for e in (2, 3):
-            copy_rows(copy_vector, e, 0)
-            scatter_vector(0, e * C, dx_sb[e, 0])
+        scatter_vector(0, C + CUT, middle[:, CUT:])
+        copy_rows(copy_vector, 3, 0)
+        scatter_vector(0, 3 * C, dx_sb[3, 0])
         store(0)

@@ -391,7 +391,8 @@ def tile_moe_bdx_glu_silu_kernel(
             gather_scalar(t, HALF, HALF)
         gate_last = new_tile("gate_last", [P, P // 4, 4], F32)
         nc.vector.tensor_copy(gate_last[:], wide_gates(3, block_cols(1)))
-        gather_vector(PACK - 1, 0, C)
+        gather_vector(PACK - 1, 0, P)
+        gather_scalar(PACK - 1, P, P)
         gather_scalar(PACK - 1, C, C)
         gather_scalar(PACK - 1, HALF, HALF)
 
@@ -418,11 +419,11 @@ def tile_moe_bdx_glu_silu_kernel(
         gate_g(2)
         make_part(1)
         permute_words(nc.vector.tensor_copy, 1)
-        quantize_g(2)
-        make_dh(2)
         quantize_expert(0)
         project(0)
         factor_vector(1)
+        quantize_g(2)
+        make_dh(2)
 
         new_da(1)
         da1_gpsimd(1)
@@ -436,10 +437,10 @@ def tile_moe_bdx_glu_silu_kernel(
         make_part(2)
         quantize_expert(1)
         project(1)
+        factor_vector(2)
         for c in range(2):
             quantize_slots(f"3{c}", 3, block_cols(c))
         make_dh(3)
-        factor_vector(2)
 
         new_da(2)
         da1_gpsimd(2)

@@ -25,18 +25,47 @@ C = 256
 S = E * C
 HALF = S // 2
 LIST_ROWS = 16
+RUN = 4
+LAST = E - 1
 KIB = 1024
 
 FLOPS = 2 * S * (N * H + 2 * H * K)
 BYTES = 4 * (N * T + 2 * H * S + K * T + S) + E * P * (2 * H + 4 * K) + E * 16 * (H + 2 * K) + 2 * 16 * S // 16
 
-SUCCEEDS = {"g_bf2": "tanh0", "da_bf0": "a3_0", "da_bf1": "a3_0", "part2": "part0", "da_bf3": "silu2", "g_bf31": "g_bf0"}
-PLACES = {"g_codes1": 0, "gate_last": 0.75, "factor0": 1, "g_bf30": 1, "factor1": 3, "factor2": 5, "factor3": 7, "da_bf2": 11, "tanh2": 13, "part3": 15, "da_codes0": 20, "g_codes30": 20, "g_codes31": 21, "a1_half1": 25, "dx_sb00": 25, "dx_sb01": 27, "middle0": 25, "dx_sb11": 27, "dx_sb21": 27}
+SUCCEEDS = {
+    "g_bf31": "g_bf0",
+    "g_bf2": "tanh0",
+    "da_bf0": "a3_0",
+    "da_bf1": "a3_0",
+    "part2": "part0",
+    "da_bf3": "silu2",
+}
+PLACES = {
+    "g_codes1": 0,
+    "gate_last": 0.75,
+    "factor0": 1,
+    "g_bf30": 1,
+    "factor1": 3,
+    "factor2": 5,
+    "factor3": 7,
+    "da_bf2": 11,
+    "tanh2": 13,
+    "part3": 15,
+    "da_codes0": 20,
+    "g_codes30": 20,
+    "g_codes31": 21,
+    "a1_half1": 25,
+    "dx_sb00": 25,
+    "dx_middle": 25,
+    "dx_sb01": 27,
+    "dx_sb11": 27,
+    "dx_sb21": 27,
+}
 GATE_BANK = (6, 7)
 DH_BANK = (0, 1, 2, 3, 0, 1, 2, 3)
-DX_BANK = (4, 4)
-ROWS_DX_BANK = {(2, 0): 0, (2, 1): 1, (3, 0): 2, (3, 1): 3}
-CUT = 160
+EARLY_DX_BANK = 4
+LATE_DX_BANK = {(2, 0): 0, (2, 1): 1, (3, 0): 2, (3, 1): 3}
+SCALAR_SHARE = 160
 
 
 def tile_moe_bdx_glu_silu_kernel(
@@ -47,7 +76,6 @@ def tile_moe_bdx_glu_silu_kernel(
         listp = ctx.enter_context(tc.tile_pool(name="listp", bufs=1))
         keep = ctx.enter_context(tc.tile_pool(name="keep", bufs=1))
         psum = ctx.enter_context(tc.psum_pool(name="psum", bufs=1))
-
         shared = ctx.enter_context(tc.tile_pool(name="shared", bufs=1))
 
         def new_tile(name, shape, dtype):
@@ -78,7 +106,7 @@ def tile_moe_bdx_glu_silu_kernel(
         w3_sb = new_tile("w3_sb", [P, E, 2 * K], U8)
         w1s = new_tile("w1s", [P, E, K], U8)
         w3s = new_tile("w3s", [P, E, K], U8)
-        gate_col = new_tile("gate_col", [P, 2, 8], F32)
+        gate_col = new_tile("gate_col", [P, 2, 2 * RUN], F32)
         win = [new_tile(f"win{b}", [P, T], F32) for b in range(K // P)]
 
         def load_words(tile, dram, first, count):
@@ -86,9 +114,9 @@ def tile_moe_bdx_glu_silu_kernel(
                 tile[:].bitcast(I32), dram.bitcast(I32)[first : first + count, 0].rearrange("e p b -> p e b")
             )
 
-        def load_scales(queue, tile, dram):
+        def load_scales(tile, dram):
             for q in range(4):
-                queue.dma_start(
+                nc.sync.dma_start(
                     tile[32 * q : 32 * q + 4].bitcast(I32),
                     dram.bitcast(I32)[:, 0, 4 * q : 4 * q + 4, :].rearrange("e f i -> f e i"),
                 )
@@ -103,17 +131,17 @@ def tile_moe_bdx_glu_silu_kernel(
         def load_expert(tiles, dram, e):
             nc.sync.dma_start(tiles[e], dram[:, :, e * C : (e + 1) * C])
 
-        def load_two_experts(tile, dram, first):
-            nc.sync.dma_start(tile[:], dram[:, :, first * C : (first + 2) * C])
+        def load_half1(tile, dram):
+            nc.sync.dma_start(tile[:], dram[:, :, HALF:])
 
         def load_gate():
-            nc.scalar.dma_start(gate_col[:, :, 0:4], gate[0, :].rearrange("(h n i) -> n h i", h=2, i=4))
+            nc.scalar.dma_start(gate_col[:, :, 0:RUN], gate[0, :].rearrange("(h c i) -> c h i", h=2, i=RUN))
 
         w2_perm, w2s_perm = {}, {}
 
-        def permute_words(copy, h):
+        def permute_words(h):
             w2_perm[h] = new_tile(f"w2_perm{h}", [P, 2, 2 * H], U8)
-            copy(
+            nc.vector.tensor_copy(
                 w2_perm[h][:].bitcast(U16).rearrange("p e (t m) -> p e t m", t=PACK),
                 w2_raw[h][:].bitcast(U16).rearrange("p e (m t) -> p e t m", t=PACK),
             )
@@ -126,20 +154,21 @@ def tile_moe_bdx_glu_silu_kernel(
             )
 
         def walk_planar(ap):
-            return ap.rearrange("p j (c i) -> p c j i", i=4)
+            return ap.rearrange("p j (c i) -> p c j i", i=RUN)
 
         def walk_packed(ap):
-            return ap.rearrange("p (c i) j -> p c j i", i=4)
+            return ap.rearrange("p (c i) j -> p c j i", i=RUN)
 
         def block_cols(c):
             return slice(c * P, (c + 1) * P)
 
         all_cols = slice(0, C)
+
         gate_wide = {}
 
         def spread_gate(h):
-            gate_wide[h] = bank(f"gate_wide{h}", [P, 4, P], GATE_BANK[h])
-            for i in range(4):
+            gate_wide[h] = bank(f"gate_wide{h}", [P, RUN, P], GATE_BANK[h])
+            for i in range(RUN):
                 nc.tensor.transpose(gate_wide[h][:, i, :], gate_col[:, h, i : i + 1].to_broadcast([P, P]), ident[:])
 
         gathered = [new_tile(f"gathered{h}", [P, PACK, HALF], F32) for h in range(2)]
@@ -165,14 +194,14 @@ def tile_moe_bdx_glu_silu_kernel(
             engine.tensor_tensor(
                 walk_packed(g_bf[name][:]),
                 walk_planar(gathered[h][:, :, first : first + width]),
-                gates.unsqueeze(2).broadcast_to([P, width // 4, PACK, 4]),
+                gates.unsqueeze(2).broadcast_to([P, width // RUN, PACK, RUN]),
                 ALU.mult,
             )
 
         def wide_gates(e, cols):
             h, within = divmod(e, 2)
-            first = (within * C + cols.start) // 4
-            return gate_wide[h][:, :, first : first + (cols.stop - cols.start) // 4].rearrange("p i c -> p c i")
+            first = (within * C + cols.start) // RUN
+            return gate_wide[h][:, :, first : first + (cols.stop - cols.start) // RUN].rearrange("p i c -> p c i")
 
         def gate_g(e):
             gate_slots(nc.vector, f"{e}", e, all_cols, wide_gates(e, all_cols))
@@ -204,7 +233,7 @@ def tile_moe_bdx_glu_silu_kernel(
             tanh_sb[e] = new_tile(f"tanh{e}", [P, PACK, C], F32)
             nc.scalar.activation(tanh_sb[e][:], a1_sb[e], ACT.Tanh, scale=-0.5)
 
-        def factor_vector(e, cols=all_cols):
+        def make_factor(e, cols=all_cols):
             if e not in factor:
                 factor[e] = new_tile(f"factor{e}", [P, PACK, C], F32)
             nc.vector.scalar_tensor_tensor(
@@ -307,14 +336,14 @@ def tile_moe_bdx_glu_silu_kernel(
                 )
 
         def project(e):
-            both = bank(f"dx{e}", [P, K // P, C], DX_BANK[e])
+            both = bank(f"dx{e}", [P, K // P, C], EARLY_DX_BANK)
             for b in range(K // P):
                 dx[e, b] = both[:, b, :]
                 project_rows(dx[e, b], e, e, b)
 
         def new_rows(e):
             for b in range(K // P):
-                dx[e, b] = bank(f"dx{e}{b}", [P, C], ROWS_DX_BANK[e, b])[:]
+                dx[e, b] = bank(f"dx{e}{b}", [P, C], LATE_DX_BANK[e, b])[:]
 
         def project_by_rows(e):
             new_rows(e)
@@ -327,11 +356,11 @@ def tile_moe_bdx_glu_silu_kernel(
                 for c in range(2):
                     project_rows(dx[e, b][:, block_cols(c)], (e, c), e, b)
 
-        def copy_scalar(target, key, b):
-            nc.scalar.activation(target, dx[key, b], ACT.Copy, scale=0.5)
+        def copy_scalar(target, e, b):
+            nc.scalar.activation(target, dx[e, b], ACT.Copy, scale=0.5)
 
-        def copy_vector(target, key, b):
-            nc.vector.tensor_scalar(target, dx[key, b], 0.5, None, ALU.mult)
+        def copy_vector(target, e, b):
+            nc.vector.tensor_scalar(target, dx[e, b], 0.5, None, ALU.mult)
 
         def scatter_vector(b, first, values):
             nc.vector.tensor_copy(win[b][:].indirect(entries(first, values.shape[1])), values)
@@ -339,20 +368,12 @@ def tile_moe_bdx_glu_silu_kernel(
         def scatter_scalar(b, first, values):
             nc.scalar.activation(win[b][:].indirect(entries(first, values.shape[1])), values, ACT.Copy)
 
-        def return_expert(e):
-            tiles = [new_tile(f"dx_sb{e}{b}", [P, C], F32) for b in range(K // P)]
-            for b in range(K // P):
-                copy_scalar(tiles[b][:], e, b)
-            for b in range(K // P):
-                scatter_scalar(b, e * C, tiles[b][:])
-
         def copy_rows(copy, e, b):
             dx_sb[e, b] = new_tile(f"dx_sb{e}{b}", [P, C], F32)[:]
             copy(dx_sb[e, b], e, b)
 
         def store(b):
             nc.sync.dma_start(out[b * P : (b + 1) * P, :], win[b][:])
-
 
         nc.gpsimd.memset(w2s_raw[:].bitcast(I32), 0)
         nc.vector.memset(zero[:], 0.0)
@@ -363,10 +384,11 @@ def tile_moe_bdx_glu_silu_kernel(
 
         load_gate()
         nc.scalar.activation(win[1][:], zero[:].to_broadcast([P, T]), ACT.Silu)
+
         load_plane(0)
         nc.sync.dma_start(offsets[:], offs)
         load_plane(1)
-        load_scales(nc.sync, w2s_raw, w2_scales)
+        load_scales(w2s_raw, w2_scales)
         load_plane(2)
         load_plane(3)
         load_words(w2_raw[0], w2_words, 0, 2)
@@ -375,12 +397,12 @@ def tile_moe_bdx_glu_silu_kernel(
         load_expert(a1_sb, a1_4, 1)
         load_expert(a3_sb, a3_4, 1)
         load_words(w2_raw[1], w2_words, 2, 2)
-        load_two_experts(a1_half1, a1_4, 2)
+        load_half1(a1_half1, a1_4)
         load_words(w3_sb, w3_words, 0, E)
         load_words(w1_sb, w1_words, 0, E)
-        load_scales(nc.sync, w3s, w3_scales)
-        load_scales(nc.sync, w1s, w1_scales)
-        load_two_experts(a3_half1, a3_4, 2)
+        load_scales(w3s, w3_scales)
+        load_scales(w1s, w1_scales)
+        load_half1(a3_half1, a3_4)
 
         permute_scales(0)
         permute_scales(1)
@@ -389,24 +411,23 @@ def tile_moe_bdx_glu_silu_kernel(
         for t in range(PACK - 1):
             gather_vector(t, 0, HALF)
             gather_scalar(t, HALF, HALF)
-        gate_last = new_tile("gate_last", [P, P // 4, 4], F32)
-        nc.vector.tensor_copy(gate_last[:], wide_gates(3, block_cols(1)))
-        gather_vector(PACK - 1, 0, P)
-        gather_scalar(PACK - 1, P, P)
+        gate_last = new_tile("gate_last", [P, P // RUN, RUN], F32)
+        nc.vector.tensor_copy(gate_last[:], wide_gates(LAST, block_cols(1)))
+        gather_vector(PACK - 1, 0, C)
         gather_scalar(PACK - 1, C, C)
         gather_scalar(PACK - 1, HALF, HALF)
 
         gate_g(0)
-        permute_words(nc.vector.tensor_copy, 0)
+        permute_words(0)
         quantize_g(0)
         make_dh(0)
-        gate_slots(nc.gpsimd, "31", 3, block_cols(1), gate_last[:])
+        gate_slots(nc.gpsimd, f"{LAST}1", LAST, block_cols(1), gate_last[:])
         act_neg(0)
         act_tanh(0)
         act_silu(0)
         gate_g(1)
         make_part(0)
-        factor_vector(0)
+        make_factor(0)
         quantize_g(1)
         make_dh(1)
 
@@ -418,60 +439,63 @@ def tile_moe_bdx_glu_silu_kernel(
         make_da3(0)
         gate_g(2)
         make_part(1)
-        permute_words(nc.vector.tensor_copy, 1)
+        permute_words(1)
         quantize_expert(0)
         project(0)
-        factor_vector(1)
+        make_factor(1)
         quantize_g(2)
         make_dh(2)
 
         new_da(1)
         da1_gpsimd(1)
-        for e in (2, 3):
+        for e in range(2, E):
             act_neg(e)
             act_tanh(e)
             act_silu(e)
-        return_expert(0)
-        gate_slots(nc.vector, "30", 3, block_cols(0), wide_gates(3, block_cols(0)))
+        for b in range(K // P):
+            copy_rows(copy_scalar, 0, b)
+        for b in range(K // P):
+            scatter_scalar(b, 0, dx_sb[0, b])
+        gate_slots(nc.vector, f"{LAST}0", LAST, block_cols(0), wide_gates(LAST, block_cols(0)))
         make_da3(1)
         make_part(2)
         quantize_expert(1)
         project(1)
-        factor_vector(2)
+        make_factor(2)
         for c in range(2):
-            quantize_slots(f"3{c}", 3, block_cols(c))
-        make_dh(3)
+            quantize_slots(f"{LAST}{c}", LAST, block_cols(c))
+        make_dh(LAST)
 
         new_da(2)
         da1_gpsimd(2)
-        middle = new_tile("middle0", [P, 2 * C], F32)
-        copy_scalar(middle[:, 0:C], 1, 0)
+        dx_middle = new_tile("dx_middle", [P, 2 * C], F32)
+        copy_scalar(dx_middle[:, 0:C], 1, 0)
         copy_rows(copy_scalar, 1, 1)
-        scatter_scalar(0, C, middle[:, 0:CUT])
+        scatter_scalar(0, C, dx_middle[:, 0:SCALAR_SHARE])
         scatter_scalar(1, C, dx_sb[1, 1])
         make_da3(2)
-        new_da_by_block(3)
+        new_da_by_block(LAST)
         for c in range(2):
-            make_part(3, (c,))
-            make_da3(3, (c,))
+            make_part(LAST, (c,))
+            make_da3(LAST, (c,))
 
         quantize_expert(2)
         project_by_rows(2)
         for c in range(2):
-            factor_vector(3, block_cols(c))
+            make_factor(LAST, block_cols(c))
         for c in range(2):
-            da1_vector(3, c)
+            da1_vector(LAST, c)
         for c in range(2):
-            quantize_block(3, c)
-        project_by_blocks(3)
+            quantize_block(LAST, c)
+        project_by_blocks(LAST)
 
         copy_rows(copy_scalar, 2, 1)
-        copy_scalar(middle[:, C:], 2, 0)
+        copy_scalar(dx_middle[:, C:], 2, 0)
         scatter_scalar(1, 2 * C, dx_sb[2, 1])
-        copy_rows(copy_scalar, 3, 1)
-        scatter_scalar(1, 3 * C, dx_sb[3, 1])
+        copy_rows(copy_scalar, LAST, 1)
+        scatter_scalar(1, LAST * C, dx_sb[LAST, 1])
         store(1)
-        scatter_vector(0, C + CUT, middle[:, CUT:])
-        copy_rows(copy_vector, 3, 0)
-        scatter_vector(0, 3 * C, dx_sb[3, 0])
+        scatter_vector(0, C + SCALAR_SHARE, dx_middle[:, SCALAR_SHARE:])
+        copy_rows(copy_vector, LAST, 0)
+        scatter_vector(0, LAST * C, dx_sb[LAST, 0])
         store(0)

from contextlib import ExitStack

import concourse.mybir as mybir
from concourse.masks import make_identity

F32 = mybir.dt.float32
BF16 = mybir.dt.bfloat16
U32 = mybir.dt.uint32
I32 = mybir.dt.int32
U16 = mybir.dt.uint16
U8 = mybir.dt.uint8
FP8X4 = mybir.dt.float8_e4m3fn_x4
FP4X4 = mybir.dt.float4_e2m1fn_x4
ACT = mybir.ActivationFunctionType
ALU = mybir.AluOpType

P = 128
PACK = 4
N = 512
H = 512
K = 256
T = 1280
E = 4
C = 256
S = E * C
HALF = S // 2
LIST_ROWS = 16
RUN = 4
LAST = E - 1
KIB = 1024

FLOPS = 2 * S * (N * H + 2 * H * K)
BYTES = 4 * (N * T + 2 * H * S + K * T + S) + E * P * (2 * H + 4 * K) + E * 16 * (H + 2 * K) + 2 * 16 * S // 16

SUCCEEDS = {
    "g_bf31": "g_bf0",
    "g_bf2": "tanh0",
    "da_bf0": "a3_0",
    "da_bf1": "a3_0",
    "part2": "part0",
    "da_bf3": "silu2",
}
PLACES = {
    "g_codes1": 0,
    "gate_last": 0.75,
    "factor0": 1,
    "g_bf30": 1,
    "factor1": 3,
    "factor2": 5,
    "factor3": 7,
    "da_bf2": 11,
    "tanh2": 13,
    "part3": 15,
    "da_codes0": 20,
    "g_codes30": 20,
    "g_codes31": 21,
    "a1_half1": 25,
    "dx_sb00": 25,
    "dx_middle": 25,
    "dx_sb01": 27,
    "dx_sb11": 27,
    "dx_sb21": 27,
}
GATE_BANK = (6, 7)
DH_BANK = (0, 1, 2, 3, 0, 1, 2, 3)
EARLY_DX_BANK = 4
LATE_DX_BANK = {(2, 0): 0, (2, 1): 1, (3, 0): 2, (3, 1): 3}
SCALAR_SHARE = 160


def tile_moe_bdx_glu_silu_kernel(
    tc, dyT, a1, a3, w2_words, w2_scales, w1_words, w1_scales, w3_words, w3_scales, gate, offs, out
):
    nc = tc.nc
    with ExitStack() as ctx:
        listp = ctx.enter_context(tc.tile_pool(name="listp", bufs=1))
        keep = ctx.enter_context(tc.tile_pool(name="keep", bufs=1))
        psum = ctx.enter_context(tc.psum_pool(name="psum", bufs=1))
        shared = ctx.enter_context(tc.tile_pool(name="shared", bufs=1))

        def new_tile(name, shape, dtype):
            if name in PLACES:
                return shared.tile(shape, dtype, name=name, offset=int(PLACES[name] * KIB), align_bytes=64)
            return keep.tile(shape, dtype, name=name, tag=SUCCEEDS.get(name, name), align_bytes=64)

        def bank(name, shape, number):
            return psum.tile(shape, F32, name=name, tag=f"bank{number}")

        offsets = listp.tile([P, S // LIST_ROWS], U16, name="offsets")

        def entries(first, count):
            return offsets[:, first // LIST_ROWS : (first + count) // LIST_ROWS]

        planes = [new_tile(f"plane{t}", [P, T], F32) for t in range(PACK)]
        ident = new_tile("ident", [P, P], F32)
        zero = new_tile("zero", [P, 1], F32)
        a1_half1 = new_tile("a1_half1", [P, PACK, HALF], F32)
        a3_half1 = new_tile("a3_half1", [P, PACK, HALF], F32)
        a1_sb = [new_tile(f"a1_{e}", [P, PACK, C], F32)[:] for e in range(2)]
        a3_sb = [new_tile(f"a3_{e}", [P, PACK, C], F32)[:] for e in range(2)]
        a1_sb = a1_sb + [a1_half1[:, :, 0:C], a1_half1[:, :, C:HALF]]
        a3_sb = a3_sb + [a3_half1[:, :, 0:C], a3_half1[:, :, C:HALF]]
        w2_raw = [new_tile(f"w2_raw{h}", [P, 2, 2 * H], U8) for h in range(2)]
        w2s_raw = new_tile("w2s_raw", [P, E, H], U8)
        w1_sb = new_tile("w1_sb", [P, E, 2 * K], U8)
        w3_sb = new_tile("w3_sb", [P, E, 2 * K], U8)
        w1s = new_tile("w1s", [P, E, K], U8)
        w3s = new_tile("w3s", [P, E, K], U8)
        gate_col = new_tile("gate_col", [P, 2, 2 * RUN], F32)
        win = [new_tile(f"win{b}", [P, T], F32) for b in range(K // P)]

        def load_words(tile, dram, first, count):
            nc.sync.dma_start(
                tile[:].bitcast(I32), dram.bitcast(I32)[first : first + count, 0].rearrange("e p b -> p e b")
            )

        def load_scales(tile, dram):
            for q in range(4):
                nc.sync.dma_start(
                    tile[32 * q : 32 * q + 4].bitcast(I32),
                    dram.bitcast(I32)[:, 0, 4 * q : 4 * q + 4, :].rearrange("e f i -> f e i"),
                )

        dy4 = dyT.rearrange("(p j) t -> p j t", j=PACK)
        a1_4 = a1.rearrange("(p j) s -> p j s", j=PACK)
        a3_4 = a3.rearrange("(p j) s -> p j s", j=PACK)

        def load_plane(t):
            nc.sync.dma_start(planes[t][:], dy4[:, t, :])

        def load_expert(tiles, dram, e):
            nc.sync.dma_start(tiles[e], dram[:, :, e * C : (e + 1) * C])

        def load_half1(tile, dram):
            nc.sync.dma_start(tile[:], dram[:, :, HALF:])

        def load_gate():
            nc.scalar.dma_start(gate_col[:, :, 0:RUN], gate[0, :].rearrange("(h c i) -> c h i", h=2, i=RUN))

        w2_perm, w2s_perm = {}, {}

        def permute_words(h):
            w2_perm[h] = new_tile(f"w2_perm{h}", [P, 2, 2 * H], U8)
            nc.vector.tensor_copy(
                w2_perm[h][:].bitcast(U16).rearrange("p e (t m) -> p e t m", t=PACK),
                w2_raw[h][:].bitcast(U16).rearrange("p e (m t) -> p e t m", t=PACK),
            )

        def permute_scales(h):
            w2s_perm[h] = new_tile(f"w2s_perm{h}", [P, 2, H], U8)
            nc.gpsimd.tensor_copy(
                w2s_perm[h][:].rearrange("p e (t m) -> p e t m", t=PACK),
                w2s_raw[:, 2 * h : 2 * h + 2].rearrange("p e (m t) -> p e t m", t=PACK),
            )

        def walk_planar(ap):
            return ap.rearrange("p j (c i) -> p c j i", i=RUN)

        def walk_packed(ap):
            return ap.rearrange("p (c i) j -> p c j i", i=RUN)

        def block_cols(c):
            return slice(c * P, (c + 1) * P)

        all_cols = slice(0, C)

        gate_wide = {}

        def spread_gate(h):
            gate_wide[h] = bank(f"gate_wide{h}", [P, RUN, P], GATE_BANK[h])
            for i in range(RUN):
                nc.tensor.transpose(gate_wide[h][:, i, :], gate_col[:, h, i : i + 1].to_broadcast([P, P]), ident[:])

        gathered = [new_tile(f"gathered{h}", [P, PACK, HALF], F32) for h in range(2)]

        def gather_operands(t, first, count):
            h, col = divmod(first, HALF)
            return gathered[h][:, t, col : col + count], planes[t][:].indirect(entries(first, count))

        def gather_vector(t, first, count):
            nc.vector.tensor_copy(*gather_operands(t, first, count))

        def gather_scalar(t, first, count):
            nc.scalar.activation(*gather_operands(t, first, count), ACT.Copy)

        g_bf, g_codes = {}, {}
        g_scales = new_tile("g_scales", [P, S], U8)

        def gate_slots(engine, name, e, cols, gates):
            h, within = divmod(e, 2)
            width = cols.stop - cols.start
            first = within * C + cols.start
            g_bf[name] = new_tile(f"g_bf{name}", [P, width, PACK], BF16)
            engine.tensor_tensor(
                walk_packed(g_bf[name][:]),
                walk_planar(gathered[h][:, :, first : first + width]),
                gates.unsqueeze(2).broadcast_to([P, width // RUN, PACK, RUN]),
                ALU.mult,
            )

        def wide_gates(e, cols):
            h, within = divmod(e, 2)
            first = (within * C + cols.start) // RUN
            return gate_wide[h][:, :, first : first + (cols.stop - cols.start) // RUN].rearrange("p i c -> p c i")

        def gate_g(e):
            gate_slots(nc.vector, f"{e}", e, all_cols, wide_gates(e, all_cols))

        def quantize_slots(name, e, cols):
            codes = new_tile(f"g_codes{name}", [P, cols.stop - cols.start], U32)
            nc.vector.quantize_mx(
                out=codes[:].bitcast(FP8X4),
                scales=g_scales[:, e * C + cols.start : e * C + cols.stop],
                in_=g_bf[name][:].rearrange("p n j -> p (n j)"),
            )
            for first in range(cols.start, cols.stop, P):
                g_codes[e, first // P] = codes[:, first - cols.start : first - cols.start + P]

        def quantize_g(e):
            quantize_slots(f"{e}", e, all_cols)

        neg_sb, silu_sb, tanh_sb, factor, part, dh = {}, {}, {}, {}, {}, {}

        def act_neg(e):
            neg_sb[e] = new_tile(f"neg{e}", [P, PACK, C], F32)
            nc.scalar.activation(neg_sb[e][:], a1_sb[e], ACT.Silu, scale=-1.0)

        def act_silu(e):
            silu_sb[e] = new_tile(f"silu{e}", [P, C, PACK], F32)
            nc.scalar.activation(walk_packed(silu_sb[e][:]), walk_planar(a1_sb[e]), ACT.Silu)

        def act_tanh(e):
            tanh_sb[e] = new_tile(f"tanh{e}", [P, PACK, C], F32)
            nc.scalar.activation(tanh_sb[e][:], a1_sb[e], ACT.Tanh, scale=-0.5)

        def make_factor(e, cols=all_cols):
            if e not in factor:
                factor[e] = new_tile(f"factor{e}", [P, PACK, C], F32)
            nc.vector.scalar_tensor_tensor(
                factor[e][:, :, cols], tanh_sb[e][:, :, cols], 1.0, a3_sb[e][:, :, cols], ALU.subtract, ALU.mult
            )

        da_bf, da1_out, da3_out, da_scales, da_codes = {}, {}, {}, {}, {}

        def new_da(e):
            tile = new_tile(f"da_bf{e}", [P, 2, C, PACK], BF16)
            da_bf[e] = tile[:].rearrange("p i n j -> p (i n j)")
            da1_out[e] = tile[:, 0]
            for c in range(2):
                da3_out[e, c] = tile[:, 1, block_cols(c), :]

        def new_da_by_block(e):
            tile = new_tile(f"da_bf{e}", [P, 2, 2, P, PACK], BF16)
            for c in range(2):
                da_bf[e, c] = tile[:, c].rearrange("p i n j -> p (i n j)")
                da1_out[e, c] = tile[:, c, 0]
                da3_out[e, c] = tile[:, c, 1]

        def make_dh(e):
            h, within = divmod(e, 2)
            for c in range(2):
                dh[e, c] = bank(f"dh{e}{c}", [P, PACK, P], DH_BANK[2 * e + c])
                for t in range(PACK):
                    nc.tensor.matmul_mx(
                        out=dh[e, c][:, t, :],
                        lhsT=w2_perm[h][:, within, 2 * P * t : 2 * P * (t + 1)].bitcast(FP4X4),
                        lhsT_scale=w2s_perm[h][:, within, P * t : P * (t + 1)],
                        rhs=g_codes[e, c].bitcast(FP8X4),
                        rhs_scale=g_scales[:, e * C + c * P : e * C + (c + 1) * P],
                        start=True,
                        stop=True,
                    )

        def make_part(e, blocks=(0, 1)):
            if 0 in blocks:
                part[e] = new_tile(f"part{e}", [P, PACK, C], F32)
            for c in blocks:
                nc.vector.scalar_tensor_tensor(
                    part[e][:, :, block_cols(c)],
                    neg_sb[e][:, :, block_cols(c)],
                    1.0,
                    dh[e, c][:],
                    ALU.subtract,
                    ALU.mult,
                )

        def make_da3(e, blocks=(0, 1)):
            for c in blocks:
                nc.vector.scalar_tensor_tensor(
                    da3_out[e, c],
                    dh[e, c][:].rearrange("p j n -> p n j"),
                    2.0,
                    silu_sb[e][:, block_cols(c), :],
                    ALU.mult,
                    ALU.mult,
                )

        def make_da1(engine, target, e, cols):
            engine.tensor_tensor(
                walk_packed(target), walk_planar(part[e][:, :, cols]), walk_planar(factor[e][:, :, cols]), ALU.mult
            )

        def da1_gpsimd(e):
            make_da1(nc.gpsimd, da1_out[e], e, all_cols)

        def da1_vector(e, c):
            make_da1(nc.vector, da1_out[e, c], e, block_cols(c))

        def quantize_da(key, name, width):
            da_codes[key] = new_tile(f"da_codes{name}", [P, 2, width], U32)
            da_scales[key] = new_tile(f"da_scales{name}", [P, 2, width], U8)
            nc.vector.quantize_mx(
                out=da_codes[key][:].rearrange("p i n -> p (i n)").bitcast(FP8X4),
                scales=da_scales[key][:].rearrange("p i n -> p (i n)"),
                in_=da_bf[key],
            )

        def quantize_expert(e):
            quantize_da(e, f"{e}", C)

        def quantize_block(e, c):
            quantize_da((e, c), f"{e}{c}", P)

        dx, dx_sb = {}, {}

        def project_rows(target, key, e, b):
            for i, (w, ws) in enumerate(((w1_sb, w1s), (w3_sb, w3s))):
                nc.tensor.matmul_mx(
                    out=target,
                    lhsT=w[:, e, 2 * P * b : 2 * P * (b + 1)].bitcast(FP4X4),
                    lhsT_scale=ws[:, e, P * b : P * (b + 1)],
                    rhs=da_codes[key][:, i, :].bitcast(FP8X4),
                    rhs_scale=da_scales[key][:, i, :],
                    start=(i == 0),
                    stop=(i == 1),
                )

        def project(e):
            both = bank(f"dx{e}", [P, K // P, C], EARLY_DX_BANK)
            for b in range(K // P):
                dx[e, b] = both[:, b, :]
                project_rows(dx[e, b], e, e, b)

        def new_rows(e):
            for b in range(K // P):
                dx[e, b] = bank(f"dx{e}{b}", [P, C], LATE_DX_BANK[e, b])[:]

        def project_by_rows(e):
            new_rows(e)
            for b in reversed(range(K // P)):
                project_rows(dx[e, b], e, e, b)

        def project_by_blocks(e):
            new_rows(e)
            for b in reversed(range(K // P)):
                for c in range(2):
                    project_rows(dx[e, b][:, block_cols(c)], (e, c), e, b)

        def copy_scalar(target, e, b):
            nc.scalar.activation(target, dx[e, b], ACT.Copy, scale=0.5)

        def copy_vector(target, e, b):
            nc.vector.tensor_scalar(target, dx[e, b], 0.5, None, ALU.mult)

        def scatter_vector(b, first, values):
            nc.vector.tensor_copy(win[b][:].indirect(entries(first, values.shape[1])), values)

        def scatter_scalar(b, first, values):
            nc.scalar.activation(win[b][:].indirect(entries(first, values.shape[1])), values, ACT.Copy)

        def copy_rows(copy, e, b):
            dx_sb[e, b] = new_tile(f"dx_sb{e}{b}", [P, C], F32)[:]
            copy(dx_sb[e, b], e, b)

        def store(b):
            nc.sync.dma_start(out[b * P : (b + 1) * P, :], win[b][:])

        nc.gpsimd.memset(w2s_raw[:].bitcast(I32), 0)
        nc.vector.memset(zero[:], 0.0)
        make_identity(nc, ident[:])
        nc.gpsimd.memset(w1s[:].bitcast(I32), 0)
        nc.gpsimd.memset(w3s[:].bitcast(I32), 0)
        nc.vector.memset(win[0][:], 0.0)

        load_gate()
        nc.scalar.activation(win[1][:], zero[:].to_broadcast([P, T]), ACT.Silu)

        load_plane(0)
        nc.sync.dma_start(offsets[:], offs)
        load_plane(1)
        load_scales(w2s_raw, w2_scales)
        load_plane(2)
        load_plane(3)
        load_words(w2_raw[0], w2_words, 0, 2)
        load_expert(a1_sb, a1_4, 0)
        load_expert(a3_sb, a3_4, 0)
        load_expert(a1_sb, a1_4, 1)
        load_expert(a3_sb, a3_4, 1)
        load_words(w2_raw[1], w2_words, 2, 2)
        load_half1(a1_half1, a1_4)
        load_words(w3_sb, w3_words, 0, E)
        load_words(w1_sb, w1_words, 0, E)
        load_scales(w3s, w3_scales)
        load_scales(w1s, w1_scales)
        load_half1(a3_half1, a3_4)

        permute_scales(0)
        permute_scales(1)
        spread_gate(0)
        spread_gate(1)
        for t in range(PACK - 1):
            gather_vector(t, 0, HALF)
            gather_scalar(t, HALF, HALF)
        gate_last = new_tile("gate_last", [P, P // RUN, RUN], F32)
        nc.vector.tensor_copy(gate_last[:], wide_gates(LAST, block_cols(1)))
        gather_vector(PACK - 1, 0, C)
        gather_scalar(PACK - 1, C, C)
        gather_scalar(PACK - 1, HALF, HALF)

        gate_g(0)
        permute_words(0)
        quantize_g(0)
        make_dh(0)
        gate_slots(nc.gpsimd, f"{LAST}1", LAST, block_cols(1), gate_last[:])
        act_neg(0)
        act_tanh(0)
        act_silu(0)
        gate_g(1)
        make_part(0)
        make_factor(0)
        quantize_g(1)
        make_dh(1)

        new_da(0)
        da1_gpsimd(0)
        act_neg(1)
        act_tanh(1)
        act_silu(1)
        make_da3(0)
        gate_g(2)
        make_part(1)
        permute_words(1)
        quantize_expert(0)
        project(0)
        make_factor(1)
        quantize_g(2)
        make_dh(2)

        new_da(1)
        da1_gpsimd(1)
        for e in range(2, E):
            act_neg(e)
            act_tanh(e)
            act_silu(e)
        for b in range(K // P):
            copy_rows(copy_scalar, 0, b)
        for b in range(K // P):
            scatter_scalar(b, 0, dx_sb[0, b])
        gate_slots(nc.vector, f"{LAST}0", LAST, block_cols(0), wide_gates(LAST, block_cols(0)))
        make_da3(1)
        make_part(2)
        quantize_expert(1)
        project(1)
        make_factor(2)
        for c in range(2):
            quantize_slots(f"{LAST}{c}", LAST, block_cols(c))
        make_dh(LAST)

        new_da(2)
        da1_gpsimd(2)
        dx_middle = new_tile("dx_middle", [P, 2 * C], F32)
        copy_scalar(dx_middle[:, 0:C], 1, 0)
        copy_rows(copy_scalar, 1, 1)
        scatter_scalar(0, C, dx_middle[:, 0:SCALAR_SHARE])
        scatter_scalar(1, C, dx_sb[1, 1])
        make_da3(2)
        new_da_by_block(LAST)
        for c in range(2):
            make_part(LAST, (c,))
            make_da3(LAST, (c,))

        quantize_expert(2)
        project_by_rows(2)
        for c in range(2):
            make_factor(LAST, block_cols(c))
        for c in range(2):
            da1_vector(LAST, c)
        for c in range(2):
            quantize_block(LAST, c)
        project_by_blocks(LAST)

        copy_rows(copy_scalar, 2, 1)
        copy_scalar(dx_middle[:, C:], 2, 0)
        scatter_scalar(1, 2 * C, dx_sb[2, 1])
        copy_rows(copy_scalar, LAST, 1)
        scatter_scalar(1, LAST * C, dx_sb[LAST, 1])
        store(1)
        scatter_vector(0, C + SCALAR_SHARE, dx_middle[:, SCALAR_SHARE:])
        copy_rows(copy_vector, LAST, 0)
        scatter_vector(0, LAST * C, dx_sb[LAST, 0])
        store(0)
